import numpy as np, ml_dtypes
CORES = [16,17,18,19,32,33,34,35]
N = 8
import mx_ref
BF = ml_dtypes.bfloat16
def gcols(t, e):
    v = np.concatenate([t.reshape(8, 16, -1, 4), np.zeros((8, 16, 1, 4), BF)], axis=2)
    return np.ascontiguousarray(np.stack([v[g][:, e[g]] for g in range(8)])).reshape(128, -1)
def tile(rs):
    return np.stack(rs, axis=2).reshape(128, -1).astype(BF)
def pick(q, e):
    c = np.concatenate([q[0].reshape(128, -1, 4), np.zeros((128, 1, 4), np.uint8)], axis=1); s = np.concatenate([q[1], np.ones((16, 1), np.uint8)], axis=1)
    return (np.ascontiguousarray(c[:, e].reshape(128, -1)), np.ascontiguousarray(s[:, e]))
def join(*qs):
    return (np.concatenate([q[0] for q in qs], axis=1), np.concatenate([q[1] for q in qs], axis=1))
def put(q, e, v):
    c, s = q[0].reshape(128, -1, 4).copy(), q[1].copy(); c[:, e] = v[0].reshape(128, -1, 4); s[:, e] = v[1]
    return (c.reshape(128, -1), s)
def pk(c, s):
    return (np.ascontiguousarray(c), mx_ref.live(s))
def emit(q):
    return q[0], q[1]
def packed(v, rng):
    q = [mx_ref.quantize(np.ascontiguousarray(v[r])) for r in range(N)]
    return np.stack([a for a, b in q]), np.stack([mx_ref.plane(b, rng) for a, b in q])
def values_of_codes():
    e, c = np.zeros((128, 128, 4), np.float32), np.zeros((128, 2, 4), np.uint8)
    e[np.arange(128), np.arange(128), 0] = 1
    c[:127, :, 0] = np.arange(256).reshape(2, 128).T[:127]
    return mx_ref.matmul(mx_ref.quantize(e.reshape(128, 512).astype(BF)), (c.reshape(128, 8), np.full((16, 2), 127, np.uint8))).T.reshape(-1).astype(np.float64)
CODE_VALUE, SCALE_VALUE = values_of_codes(), 2.0 ** (np.arange(256) - 127.0)
def decode(q):
    return (CODE_VALUE[q[0]].reshape(16, 8, -1, 4) * SCALE_VALUE[q[1]][:, None, :, None] + 0.0).reshape(128, -1).astype(np.float32)
def f(rng, *shape):
    return mx_ref.flush((rng.standard_normal(shape, dtype=np.float32) * np.exp2(rng.integers(-2, 3, shape[:-1] + (1,)))).astype(BF))
def wide(rng, *shape, cols=0):
    v = rng.standard_normal(shape, dtype=np.float32) * np.exp2(rng.integers(-12, 13, shape)).astype(np.float32)
    if cols: v *= np.repeat(np.exp2(rng.integers(-cols, cols + 1, shape[:-2] + (1, shape[-1] // 4))) * (rng.random(shape[:-2] + (1, shape[-1] // 4)) > 0.0625), 4, axis=-1).astype(np.float32)
    return mx_ref.flush(v.astype(BF))
C, K, P, R = 256, 128, 384, 3
ODD = np.arange(1, C, 2)
REFS = np.full((K + 127) // 128 * 128, -1)
REFS[:K] = ODD
def layers(rng):
    return np.array(f(rng, N, 128, 2048)).reshape(N, 8, 16, 4, 8, 16, 4)
def weights(rng, w):
    c, s = packed(np.ascontiguousarray(w).reshape(N, 128, 2048), rng)
    return {"wc": c, "ws": s}
def full(rng, x, w):
    return {"x": np.ascontiguousarray(x).astype(np.float32).reshape(N, 128, 4 * C).astype(BF), "v": np.array(f(rng, N, 128, 512)), **weights(rng, w)}
def apart(rng):
    x = np.array(f(rng, N, 128, 4 * C)).astype(np.float32).reshape(N, 8, 16, C, 4)
    h = rng.permutation(8)[:2]
    x[:, :, :, 1::2] = 0
    x[:, h] = 0
    w = layers(rng)
    w[:, h] = 0
    w[:, :, :, :, h] = 0
    return x, int(h[0]), int(h[1]), w
def setup_inputs(rng):
    return full(rng, np.array(f(rng, N, 128, 4 * C)), layers(rng))
def setup_inputs_ties(rng):
    x, a, b, w = apart(rng)
    x[:, a, :2, ::2] = rng.integers(0, 3, (N, 2, K, 4))
    s = rng.integers(0, 2, (N, 2, K, 4)) * 2.0 ** -8
    s[:, 0, :, 0] = 2.0 ** -8
    x[:, a, :2, 1::2] = s
    for r in range(N):
        k = 2 * int(rng.integers(K)) + 1
        x[r, a, :2, k] = 0
        x[r, a, 0, k, 0] = -2.0 ** -8
    o = rng.permutation(N)
    x[o[0], :, :, 1::2] = 0
    i = [g for g in (2, 4, 6) if g not in (a, b)][0]
    w[o[0], [g for g in range(8) if g != i]] = 0
    x[o[1]] = x[o[1]][:, :, :1].copy()
    return full(rng, x, w)
def setup_inputs_near(rng):
    x, a, b, w = apart(rng)
    c, d = [int(g) for g in rng.permutation(8) if g not in (a, b)][:2]
    x[:, a, 0, ::2, 0] = 1
    x[:, a, 8:12, ::2] = rng.integers(0, 2, (N, 4, K, 4)) * np.exp2(np.arange(4) - 23.0)
    x[:, a, 12, ::2, 0] = 2.0 ** -10
    x[:, b, :4, ::2] = (1 + rng.integers(0, 4, (N, 4, K, 4)) * 0.25) * 2.0 ** -30
    o = rng.permutation(N) % 4
    for r in range(N):
        s = rng.integers(0, 2, (4, K, 4)) * 1.0
        s[0, :, 0] = 1
        if o[r] < 2:
            k = 2.0 ** -8 if o[r] == 0 else 2.0 ** -30
            x[r, a, 0, 1::2, 0] = k
            x[r, a, 12, 1::2, 0] = k
            x[r, a, 8:12, 1::2] = s * k
        else: x[r, b, :4, 1::2] = s * 2.0 ** -30
        if o[r] % 2 == 0: x[r, a, 0, 2 * int(rng.integers(K)), 0] = 2.0 ** 29
    x[:, b, 8, ::2, 0] = 1.96875
    x[:, b, 9:11, ::2] = rng.integers(8, 16, (N, 2, K, 4)) * np.exp2(-13.0 - np.arange(4))
    x[:, :, :, 1:16:2] = 0
    for j in range(8): x[:, b, 9 + j // 4, 2 * j + 1, j % 4] = 1
    x[:, c, :8, ::2] = 0
    x[:, c, 0, ::2, 0] = -3.5
    x[:, d, 8, ::2, :2] = 1
    w[:, :, :, :, d] = 0
    w[:, :, :, :, c, :8] = 0
    w[:, d, 8, :, c, :8, 0] = ((2 * rng.integers(4, 8, (N, 4, 8)) + 1) * np.exp2(-8.0 - np.arange(8) % 4)).astype(np.float32).astype(BF)
    w[:, d, 8, 0, c, 0, 0] = 60
    w[:, d, 8, 0, c, 0, 1] = 3
    return full(rng, x, w)
def setup_inputs_huge(rng):
    x = 0.8 + 0.2 * rng.random((N, 8, 16, C, 4))
    for r in range(N): x[r, :, :, 2 * int(rng.integers(K)) + 1] *= -1.0
    x *= 2.0 ** 30 * float(rng.choice([-1.0, 1.0]))
    w = np.zeros((N, 128, 4, 128, 4), np.float32)
    i = np.arange(128)
    for b in range(4): w[:, i, b, i, b] = -1
    return full(rng, x, w.astype(BF))
def setup_inputs_far(rng):
    x = np.exp2(rng.integers(-14, -7, (N, 16, 8, C, 4))) * (1 + (2 * rng.integers(0, 64, (N, 16, 8, C, 4)) + 1) * 2.0 ** -7) * rng.choice([-1.0, 1.0], (N, 16, 8, C, 4))
    x[:, :, int(rng.integers(8)), :, int(rng.integers(4))] = 1.96875
    x *= np.exp2(-rng.integers(0, 3, (N, 16, 1, C, 1)))
    x *= np.exp2(3.0 * rng.permutation(N))[:, None, None, None, None]
    return full(rng, x, layers(rng))
def setup_inputs_spread(rng):
    return full(rng, wide(rng, N, 128, 4 * C, cols=6), layers(rng))
def check_inputs(d):
    b = []
    for k in ("x", "v"):
        a = np.abs(d[k].astype(np.float32))
        if not (np.isfinite(a).all() and ((a == 0) | (a >= 2.0 ** -30) & (a <= 2.0 ** 30)).all()): b.append("a value of " + k)
    none, least, most = [emit(mx_ref.quantize(np.full((128, 16), k, np.float32).astype(BF)))[1][0, 0] for k in (0.0, 2.0 ** -30, 2.0 ** 30)]
    for r in range(N):
        if ((d["wc"][r] == 0x7F) | (d["wc"][r] == 0xFF)).any(): b.append("wc: a code that is no number")
        s = mx_ref.live(d["ws"][r])
        if ((s != none) & ((s < least) | (s > most))).any(): b.append("ws: a scale out of range")
    return b
def reference(x, v, wc, ws):
    lay = [pk(wc[r], ws[r]) for r in range(N)]
    now = [x[r] for r in range(N)]
    for t in range(R):
        q = [mx_ref.quantize(now[r]) for r in range(N)]
        named, back = [], []
        for r in range(N):
            win = join(q[r], pick(q[(r + 1 + t) % N], np.arange(0, C, 2)))
            s = np.concatenate([mx_ref.matmul(pick(q[r], REFS[i:i + 128]), win) for i in range(0, len(REFS), 128)])[:K] + np.float32(0.0)
            s[np.arange(K), ODD] = -np.inf
            m = np.ascontiguousarray(np.argsort(-s, axis=1, kind="stable")[:, :8].T)
            z = mx_ref.quantize(gcols(decode(win).astype(BF), m))
            h = tile([mx_ref.matmul(pick(lay[r], np.arange(128 * b, 128 * b + 128)), z) * np.float32(0.03125) for b in range(4)])
            named.append(m)
            back.append(mx_ref.quantize(h))
        for r in range(N):
            e = (r - 1 - t) % N
            n = np.full((8, C), -1)
            for k in range(K - 1, -1, -1):
                m = named[e][:, k]
                g = np.nonzero(m >= C)[0]
                n[g, 2 * (m[g] - C)] = K + k
            for k in range(K - 1, -1, -1):
                m = named[r][:, k]
                g = np.nonzero(m < C)[0]
                n[g, m[g]] = k
            a = gcols(decode(join(back[r], back[e])).astype(BF), n)
            now[r] = (decode(q[r]) + a.astype(np.float32)).astype(BF)
    y, op = np.zeros((N, 128, C), np.float32), np.zeros((N, 8, K), np.float32)
    oc, osc = np.zeros((N, 128, 4 * C), np.uint8), np.zeros((N, 16, C), np.uint8)
    for r in range(N):
        last = mx_ref.quantize(now[r])
        y[r] = mx_ref.matmul(mx_ref.quantize(v[r]), last)
        op[r] = named[r]
        oc[r], osc[r] = emit(last)
    return {"y": y, "op": op, "oc": oc, "osc": osc}

@@ -1,0 +1,579 @@
+from concourse.mybir import dt, AluOpType, ActivationFunctionType
+
+C, K, R = 256, 128, 3
+BIG = 1.0e29
+RS = 392
+SW = 136
+GV = 144
+CODES, U8 = "float8_e4m3fn_x4", "uint8"
+F32, BF16, F16, I32, U16 = "float32", "bfloat16", "float16", "int32", "uint16"
+
+SCRATCH = {}
+
+
+def _sb(name, cols, dtype):
+    SCRATCH[name] = ("sbuf", [128, cols], dtype)
+
+
+for _n, _c, _d in [
+    ("xn", 1024, BF16), ("xe", 512, BF16), ("xo", 512, BF16), ("xl", 1024, BF16), ("vt", 512, BF16),
+    ("vq", 128, CODES), ("vs", 128, U8), ("wq", 512, CODES), ("wsc", 512, U8),
+    ("lq", 256, CODES), ("ls", 256, U8), ("yt", 256, F32), ("opt", 32, F32),
+    ("eb", 1540, BF16), ("eq", 1536, CODES), ("es", 1536, U8),
+    ("ij", 128, F32), ("ident", 128, F32), ("pi", 8, I32), ("bi", 8, I32), ("bf", 8, F32), ("xr", 4, F32), ("tm", 8, F32),
+    ("mdiag", 128, F32), ("neg1", 256, BF16), ("cfl", 12, F32), ("cu", 12, U16),
+    ("cr", 16, F32), ("col", 16, BF16), ("ncol", 16, F32), ("tab", 640, BF16),
+    ("dec1", 1024, BF16), ("dec2", 1024, BF16), ("rst", 64, F32),
+    ("so", 256, F32), ("pt", 8 * RS, F32), ("sg", 768, BF16), ("na", 2048, BF16), ("ca", 2048, BF16),
+    ("eqa", 8, F32), ("oa", 8, F32), ("aa", 8, F32), ("ix", 10, F32), ("dd", 8, F32), ("dr", 64, F32),
+    ("sc", SW, F32), ("nb", 8 * SW, BF16), ("cb", 8 * SW, BF16), ("jb", 8 * SW, BF16),
+    ("eqb", 8, F32), ("ob", 8, F32), ("ab", 8, F32), ("zs", 64, F32), ("zp", 64, F32), ("zg", 64, F32),
+    ("wb", 232, F32), ("yb", 64, F32), ("vp", 1536, BF16), ("zt", 512, BF16), ("zq", 128, CODES), ("zsc", 128, U8),
+    ("ht", 520, BF16), ("lb", 256, BF16), ("d1", 1024, BF16), ("d2", 2048, BF16), ("u1", 1024, F16), ("u2", 2048, F16),
+    ("iv1", 64, F32), ("iv2", 64, F32), ("y1", 64, F32), ("y2", 64, F32), ("f1", 16, U16), ("f2", 16, U16),
+]:
+    _sb(_n, _c, _d)
+for _t in range(R):
+    _sb("tq%d" % _t, 384, CODES)
+    _sb("ts%d" % _t, 384, U8)
+    _sb("hq%d" % _t, 288, CODES)
+    _sb("hs%d" % _t, 288, U8)
+    _sb("pq%d" % _t, 512, CODES)
+    _sb("ps%d" % _t, 512, U8)
+    _sb("of%d" % _t, 16, U16)
+    _sb("ol%d" % _t, 8, U16)
+for _b in range(8):
+    SCRATCH["bk%d" % _b] = ("psum", [128, 512], F32)
+
+SEMAPHORES = ["cv", "cs", "ct", "cg", "lx0", "lx1", "lv", "lwc", "lws", "sent", "outs"] + \
+    ["%s%d" % (_k, _t) for _k in ("at", "al", "ah") for _t in range(R)]
+
+A = AluOpType
+AF = ActivationFunctionType
+
+
+def r(name, c0=0, c1=None, st=1, p0=0, p1=128):
+    if c1 is None:
+        c1 = SCRATCH[name][1][1]
+    return (name, p0, p1, c0, c1, st)
+
+
+def _meet(a, b):
+    if a[0] != b[0] or a[2] <= b[1] or b[2] <= a[1] or a[4] <= b[3] or b[4] <= a[3]:
+        return False
+    if a[5] == 1 and b[5] == 1:
+        return True
+    return not set(range(a[3], a[4], a[5])).isdisjoint(range(b[3], b[4], b[5]))
+
+
+def rank_program(g, core, T, topo):
+    rank = T.rank_of(core)
+    if rank is None:
+        return
+    n = len(T.cores)
+    queues = {"v": g.vector, "s": g.scalar, "t": g.tensor, "g": g, "y": g.sync}
+    counter = {"v": "cv", "s": "cs", "t": "ct", "g": "cg"}
+    total = {}
+    known = {q: {} for q in queues}
+    touched = {}
+
+    def ap(x):
+        if x[5] == 1:
+            return T[x[0]][x[1]:x[2], x[3]:x[4]]
+        return T[x[0]][x[1]:x[2], x[3]:x[4]:x[5]]
+
+    def val(x):
+        return ap(x) if isinstance(x, tuple) else x
+
+    def order(q, reads, writes):
+        need = {}
+        for regs, wr in ((reads, False), (writes, True)):
+            for x in regs:
+                bank = SCRATCH[x[0]][0] == "psum"
+                for (y, w, oq, sem, cnt, clock) in touched.get(x[0], ()):
+                    if bank:
+                        hit = oq != q
+                    else:
+                        hit = (w or wr) and _meet(x, y)
+                    if hit and need.get(sem, (0, None))[0] < cnt:
+                        need[sem] = (cnt, clock)
+        kn = known[q]
+        todo = []
+        for sem, (cnt, clock) in need.items():
+            covered = any(o != sem and c2.get(sem, 0) >= cnt for o, (k2, c2) in need.items())
+            if kn.get(sem, 0) < cnt and not covered:
+                todo.append((sem, cnt))
+        for sem, cnt in todo:
+            queues[q].wait_ge(T.sem[sem], cnt)
+        for sem, (cnt, clock) in need.items():
+            kn[sem] = max(kn.get(sem, 0), cnt)
+            for s2, c2 in clock.items():
+                kn[s2] = max(kn.get(s2, 0), c2)
+
+    def note(q, reads, writes, sem, cnt):
+        clock = dict(known[q]) if q in known else {}
+        for regs, wr in ((reads, False), (writes, True)):
+            for x in regs:
+                touched.setdefault(x[0], []).append((x, wr, q, sem, cnt, clock))
+
+    def run(q, call, reads, writes):
+        reads = [x for x in reads if isinstance(x, tuple)]
+        order(q, reads, writes)
+        sem = counter[q]
+        total[sem] = total.get(sem, 0) + 1
+        call(queues[q]).then_inc(T.sem[sem], 1)
+        note(q, reads, writes, sem, total[sem])
+
+    def dma(q, out, in_, reads, writes, sem):
+        order(q, reads, writes)
+        total[sem] = total.get(sem, 0) + 16
+        queues[q].dma_start(out, in_).then_inc(T.sem[sem], 16)
+        note("dma", reads, writes, sem, total[sem])
+
+    def src(x, off):
+        return ap(x) if off is None else ap(x).indirect(ap(off))
+
+    def copy(q, out, in_, off=None, scale=None):
+        if q == "v":
+            if scale is None:
+                run(q, lambda e: e.tensor_copy(ap(out), src(in_, off)), [in_, off], [out])
+            else:
+                ts(out, in_, scale, None, A.mult, off=off)
+        elif scale is not None:
+            run(q, lambda e: e.activation(ap(out), src(in_, off), AF.Copy, scale=scale), [in_, off], [out])
+        else:
+            run(q, lambda e: e.activation(ap(out), src(in_, off), AF.Copy), [in_, off], [out])
+
+    def ts(out, in_, s1, s2, op0, op1=None, off=None):
+        if op1 is None:
+            call = lambda e: e.tensor_scalar(ap(out), src(in_, off), val(s1), None, op0)
+        else:
+            call = lambda e: e.tensor_scalar(ap(out), src(in_, off), val(s1), val(s2), op0, op1)
+        run("v", call, [in_, off, s1, s2], [out])
+
+    def tt(out, a, b, op):
+        run("v", lambda e: e.tensor_tensor(ap(out), ap(a), ap(b), op), [a, b], [out])
+
+    def scan(out, d0, d1, init, op0, op1):
+        run("v", lambda e: e.tensor_tensor_scan(ap(out), ap(d0), ap(d1), val(init), op0, op1), [d0, d1, init], [out])
+
+    def turn(out, in_):
+        run("v", lambda e: e.transpose(ap(out), ap(in_)), [in_], [out])
+
+    def act(out, in_, func, bias, scale, acc=None, off=None):
+        if acc is None:
+            call = lambda e: e.activation(ap(out), src(in_, off), func, bias=val(bias), scale=scale)
+        else:
+            call = lambda e: e.activation(ap(out), ap(in_), func, bias=val(bias), scale=scale, accum_out=ap(acc))
+        run("s", call, [in_, bias, off], [out] + ([acc] if acc else []))
+
+    def lin(out, in_, scale, bias):
+        act(out, in_, AF.Identity, bias, scale)
+
+    def fill(out, c):
+        lin(out, r("ij", 0, len(range(out[3], out[4], out[5]))), 0.0, c)
+
+    def iota(out, pattern, base, mult):
+        if SCRATCH[out[0]][2] == I32:
+            call = lambda e: e.iota(ap(out), pattern, base, mult)
+        else:
+            call = lambda e: e.iota(ap(out), pattern, base, mult, allow_small_or_imprecise_dtypes=True)
+        run("g", call, [], [out])
+
+    def quant(cq, cs, a, b, tile):
+        run("v", lambda e: e.quantize_mx(ap(r(cq, a, b)), ap(r(cs, a, b)), ap(tile)), [tile], [r(cq, a, b), r(cs, a, b)])
+
+    def mm(bank, lq, ls, la, rq, rs_, ra, rb, start=True, stop=True):
+        out = r("bk%d" % bank, 0, rb - ra)
+        ins = [r(lq, la, la + 128), r(ls, la, la + 128), r(rq, ra, rb), r(rs_, ra, rb)]
+        run("t", lambda e: e.matmul_mx(ap(out), ap(ins[0]), ap(ins[1]), ap(ins[2]), ap(ins[3]), start, stop), ins, [out])
+
+    def pick_codes(out, win, off):
+        run("v", lambda e: e.tensor_copy(ap(out).bitcast(dt.uint32), ap(win).bitcast(dt.uint32).indirect(ap(off))),
+            [win, off], [out])
+
+    def send(dst_rank, pairs, sem):
+        dst = T.cores[dst_rank % n]
+        rid, pid, _ = topo.addr(dst)
+        for out, in_ in pairs:
+            order("g", [in_], [])
+            a, b = ap(out), ap(in_)
+            if SCRATCH[in_[0]][2] == CODES:
+                a, b = a.bitcast(dt.uint8), b.bitcast(dt.uint8)
+            total["sent"] = total.get("sent", 0) + lanes
+            g.remote_dma(a, b, T.sem[sem], T.sem["sent"], pid, rid, lane_mask)
+        total[sem] = lanes * len(pairs)
+        note("far", [], [out for out, in_ in pairs], sem, total[sem])
+
+    shared = [e for e in range(16) if all(e in topo.engines(core, c) for c in T.cores if c != core)]
+    lanes = len(shared)
+    lane_mask = sum(1 << e for e in shared)
+
+    def bk(b, a=0, z=128):
+        return r("bk%d" % b, a, z)
+
+    def prow(k, a, z):
+        return r("pt", k * RS + a, k * RS + z)
+
+    def cell(name, j):
+        return r(name, j, j + 1)
+
+    dma("y", T.xn[:, 0:512], T.x[:, 0:512], [], [r("xn", 0, 512)], "lx0")
+    dma("s", T.xn[:, 512:1024], T.x[:, 512:1024], [], [r("xn", 512, 1024)], "lx1")
+    dma("y", T.wq[:].bitcast(dt.uint8), T.wc[:], [r("xn")], [r("wq")], "lwc")
+    dma("y", T.wsc[:], T.ws[:], [], [r("wsc")], "lws")
+    dma("y", T.vt[:], T.v[:], [], [r("vt")], "lv")
+
+    iota(r("ij"), [[1, 128]], 0, -1)
+    for k in range(7):
+        iota(cell("pi", k), [[0, 1]], 0, 1 << (6 - k))
+    iota(r("cr"), [[1, 2], [32, 8]], 0, 0)
+    run("v", lambda e: e.memset(ap(r("eb")), 0.0), [], [r("eb")])
+    ts(r("ident"), r("ij"), 0.0, None, A.is_equal)
+    ts(r("eb", 4, 516, 4), r("ij"), 0.0, None, A.is_equal)
+    for e in range(2):
+        for c in range(4):
+            a = 32 * c + 16 * e
+            copy("s", r("eb", 516 + 512 * e + 4 * a, 580 + 512 * e + 4 * a, 4), r("ident", a, a + 16))
+    fill(r("neg1", 0, 128), -1.0)
+    fill(r("neg1", 128, 256), -1.0)
+    fill(r("pt", 0, 8 * RS, RS), -BIG)
+    fill(cell("eqa", 0), 0.0)
+    fill(cell("eqb", 0), 0.0)
+    fill(r("ix", 8, 10), 256.0)
+    fill(r("cfl", 0, 4), 0.0)
+    fill(r("rst"), 1.0)
+    fill(r("wb", 0, 64), 0.0)
+    fill(r("ht", 512, 520), 0.0)
+    fill(r("iv1", 0, 32), 0.0)
+    fill(r("iv2", 0, 32), 0.0)
+    fill(r("rst", 0, 64, 8), 0.0)
+    copy("s", r("mdiag"), r("ident"), scale=-BIG)
+    for b in range(4):
+        quant("eq", "es", 128 * b, 128 * b + 128, r("eb", 4 - b, 516 - b))
+    quant("eq", "es", 512, 768, r("eb", 516, 1540))
+    ts(r("bi", 0, 7), r("pi", 0, 7), 6, 1, A.logical_shift_right, A.bitwise_and)
+    ts(cell("bi", 7), cell("pi", 6), 15, None, A.bitwise_and)
+    quant("eq", "es", 768, 1024, r("eb", 515, 1539))
+    copy("v", r("bf"), r("bi"))
+
+    for j in range(4):
+        copy("v", r("xe", j, 512, 4), r("xn", j, 1024, 8))
+    quant("tq0", "ts0", 128, 256, r("xe"))
+    for j in range(4):
+        copy("sv"[j // 2], r("xo", j, 512, 4), r("xn", 4 + j, 1024, 8))
+
+    def send_even(t):
+        tq, tsc = "tq%d" % t, "ts%d" % t
+        send(rank - 1 - t, [(r(tq, 256, 384), r(tq, 128, 256)), (r(tsc, 256, 384), r(tsc, 128, 256))], "at%d" % t)
+
+    send_even(0)
+    iota(r("tab", 0, 256), [[1, 256]], 0, 0)
+    iota(r("tab", 256, 512), [[0, 256]], 300, 0)
+    iota(r("tab", 512, 640), [[2, 128]], 0, 0)
+    iota(r("dec1"), [[0, 1024]], -1, 0)
+    iota(r("dec2"), [[0, 1024]], -1, 0)
+    iota(r("dec1", 0, 1024, 128), [[0, 8]], 1024, 0)
+    iota(r("dec2", 0, 1024, 256), [[0, 4]], 1024, 0)
+    iota(r("dec2", 128, 1024, 256), [[0, 4]], 127 - GV, 0)
+    quant("tq0", "ts0", 0, 128, r("xo"))
+
+    def offsets_that_are_constants():
+        for k in range(3):
+            act(cell("xr", k), cell("bf", k), AF.Abs, cell("bf", k + 4), -1.0)
+        act(cell("xr", 3), cell("bf", 3), AF.Abs, cell("bf", 4), -1.0)
+        lin(cell("tm", 0), cell("bf", 5), 2.0, cell("bf", 4))
+        lin(cell("tm", 5), cell("bf", 3), -8.0, cell("bf", 7))
+        lin(cell("tm", 6), cell("bf", 7), 2.0, 0.0)
+        lin(cell("tm", 1), cell("bf", 6), 4.0, cell("tm", 0))
+        lin(cell("tm", 4), cell("bf", 3), float(SW), cell("tm", 5))
+        lin(cell("cfl", 2), cell("xr", 3), 32.0, cell("tm", 5))
+        lin(cell("tm", 2), cell("xr", 0), 64.0, cell("tm", 1))
+        lin(r("cfl", 4, 8), r("cr", 0, 4), 2.0 * SW / 32, cell("tm", 4))
+        lin(cell("tm", 3), cell("xr", 1), 128.0, cell("tm", 2))
+        lin(r("col"), r("cr"), 1.0, cell("tm", 6))
+        lin(cell("cfl", 0), cell("xr", 2), 32.0, cell("tm", 3))
+        lin(r("cfl", 8, 12), r("cr", 0, 4), 0.0, cell("tm", 5))
+        lin(r("ncol"), r("col"), -512.0, 0.0)
+
+    even_banks, odd_banks = (0, 1, 6, 7), (2, 3, 4, 5)
+
+    def odd_planes(t):
+        for b in range(4):
+            mm(2 + b, "eq", "es", 128 * b, "tq%d" % t, "ts%d" % t, 0, 128)
+        for b in range(4):
+            copy("s", r("vp", 384 * b + 1, 384 * b + 256, 2), bk(2 + b))
+
+    for t in range(R):
+        tq, tsc, hq, hs = "tq%d" % t, "ts%d" % t, "hq%d" % t, "hs%d" % t
+        pq, ps, of, ol = "pq%d" % t, "ps%d" % t, "of%d" % t, "ol%d" % t
+        last = t == R - 1
+
+        mm(6, tq, tsc, 0, tq, tsc, 0, 128)
+        mm(0, tq, tsc, 0, tq, tsc, 128, 256)
+        tt(r("so", 1, 256, 2), bk(6), r("mdiag"), A.add)
+        copy("s", r("so", 0, 256, 2), bk(0))
+        if t == 0:
+            offsets_that_are_constants()
+
+        def best_a(k):
+            if k == 0:
+                scan(prow(0, 1, 257), r("so"), r("so"), -BIG, A.max, A.max)
+            else:
+                scan(prow(k, 1, 257), r("so"), prow(k - 1, 0, 256), -BIG, A.max, A.min)
+
+        def match_a(k):
+            ts(r("na", 256 * k, 256 * k + 256), r("so"), prow(k, 256, 257), None, A.not_equal)
+
+        def sign_a(k):
+            act(r("sg", 128 * k - 256, 128 * k), r("so"), AF.Sign, prow(k, 256, 257), -1.0)
+
+        def abs_a(k):
+            act(r("na", 256 * k, 256 * k + 256), r("sg", 128 * k - 256, 128 * k), AF.Abs, 0.0, 1.0)
+
+        def ties(e, at, k0, k1):
+            a = max(k0, 1)
+            tt(r(e, a, k1), r("pt", a * RS + at, k1 * RS, RS), r("pt", (a - 1) * RS + at, (k1 - 1) * RS, RS), A.is_equal)
+
+        def runs(e, o, k0, k1):
+            scan(r(o, k0, k1), r(e, k0, k1), r(e, k0, k1), cell(o, k0 - 1) if k0 else 0.0, A.mult, A.add)
+
+        def left_a(k):
+            scan(r("ca", 256 * k, 256 * k + 256), r("na", 256 * k, 256 * k + 256), r("neg1"), cell("oa", k), A.add, A.add)
+
+        def count_a(k):
+            row = r("ca", 256 * k, 256 * k + 256)
+            act(row, row, AF.Sign, 0.5, 1.0, cell("aa", k))
+
+        best_a(0)
+        act(r("ca", 0, 256), prow(0, 1, 257), AF.Sign, prow(0, 256, 257), -1.0, cell("ix", 0))
+        best_a(1)
+        best_a(2)
+        sign_a(2)
+        match_a(1)
+        best_a(3)
+        abs_a(2)
+        ties("eqa", 256, 0, 4)
+        best_a(4)
+        sign_a(4)
+        runs("eqa", "oa", 0, 4)
+        best_a(5)
+        left_a(1)
+        abs_a(4)
+        best_a(6)
+        left_a(2)
+        count_a(1)
+        best_a(7)
+        sign_a(6)
+        match_a(3)
+        ties("eqa", 256, 4, 8)
+        count_a(2)
+        abs_a(6)
+        match_a(5)
+        runs("eqa", "oa", 4, 8)
+        left_a(3)
+        copy("s", r("sc", 0, 8), r("pt", 256, 8 * RS, RS))
+        match_a(7)
+        count_a(3)
+        for k in (4, 5, 6, 7):
+            left_a(k)
+        if t == 0:
+            copy("v", r("cu"), r("cfl"))
+            for b in range(2, 4):
+                quant("eq", "es", 512 + 256 * b, 768 + 256 * b, r("eb", 516 - b, 1540 - b))
+            quant("vq", "vs", 0, 128, r("vt"))
+        for k in (4, 5, 6, 7):
+            count_a(k)
+        lin(r("ix", 1, 8), r("aa", 1, 8), 0.5, 128.0)
+        if t == 0:
+            odd_planes(0)
+
+        mm(1, tq, tsc, 0, tq, tsc, 256, 384)
+        for b in range(4):
+            mm(2 + b, "eq", "es", 128 * b, tq, tsc, 128, 384)
+
+        def plane(i):
+            b = i // 2
+            if i % 2:
+                copy("s", r("vp", 384 * b + 256, 384 * b + 384), bk(2 + b, 128, 256))
+            else:
+                copy("s", r("vp", 384 * b, 384 * b + 256, 2), bk(2 + b))
+
+        def best_b(k):
+            if k == 0:
+                scan(prow(0, 257, 385), bk(1), r("so", 0, 128), prow(0, 256, 257), A.max, A.max)
+            else:
+                scan(prow(k, 257, 385), bk(1), prow(k - 1, 256, 384), prow(k, 256, 257), A.max, A.min)
+
+        def match_b(k):
+            ts(r("nb", SW * k, SW * k + SW), r("sc"), prow(k, 384, 385), None, A.not_equal)
+
+        def sign_b(k):
+            act(r("sg", SW * k - 2 * SW, SW * k - SW), r("sc"), AF.Sign, prow(k, 384, 385), -1.0)
+
+        def abs_b(k):
+            act(r("nb", SW * k, SW * k + SW), r("sg", SW * k - 2 * SW, SW * k - SW), AF.Abs, 0.0, 1.0)
+
+        def left_b(k):
+            scan(r("cb", SW * k, SW * k + SW), r("nb", SW * k, SW * k + SW), r("neg1", 0, SW), cell("ob", k), A.add, A.add)
+
+        def count_b(k):
+            act(r("jb", SW * k, SW * k + SW), r("cb", SW * k, SW * k + SW), AF.Sign, 0.5, 1.0, cell("ab", k))
+
+        best_b(0)
+        copy("v", r("sc", 8, SW), bk(1))
+        best_b(1)
+        match_b(0)
+        best_b(2)
+        match_b(1)
+        best_b(3)
+        plane(0)
+        match_b(2)
+        best_b(4)
+        sign_b(3)
+        ties("eqb", 384, 0, 4)
+        best_b(5)
+        sign_b(4)
+        abs_b(3)
+        runs("eqb", "ob", 0, 4)
+        tt(r("dd"), r("ix", 1, 9), r("ix", 0, 8), A.subtract)
+        best_b(6)
+        sign_b(5)
+        abs_b(4)
+        abs_b(5)
+        act(r("dr"), r("dd"), AF.Identity, -1.0, 1.0, off=r("cu", 8, 12))
+        left_b(0)
+        left_b(1)
+        best_b(7)
+        left_b(2)
+        left_b(3)
+        ties("eqb", 384, 4, 8)
+        match_b(6)
+        runs("eqb", "ob", 4, 8)
+        match_b(7)
+        for k in range(4, 8):
+            left_b(k)
+        for k in range(8):
+            count_b(k)
+        plane(1)
+        ts(r("zs"), r("cb"), 0.0, -2.0, A.is_lt, A.mult, off=r("cu", 4, 8))
+        tt(r("zp"), r("zs"), r("dr"), A.mult)
+        scan(r("zg"), r("rst"), r("zp"), 0.0, A.mult, A.add)
+        tt(r("wb", 0, 8), r("zg", 7, 64, 8), r("ab"), A.add)
+
+        turn(r("yb", 0, 32), r("wb", 0, 32))
+        turn(r("yb", 32, 64), r("wb", 0, 32))
+        plane(2)
+        plane(3)
+        copy("s", r("wb", 32, 40, p1=64), r("wb", 0, 8, p0=64))
+        copy("s", r("wb", 32, 40, p0=64), r("wb", 0, 8, p1=64))
+        turn(r("wb", 96, 128, p1=64), r("yb", 16, 48, p0=64))
+        turn(r("wb", 96, 128, p0=64), r("yb", 16, 48, p1=64))
+        turn(r("wb", 64, 96), r("yb", 16, 48))
+        plane(4)
+        plane(5)
+        for q in range(4):
+            o = q ^ 1
+            copy("vs"[q % 2], r("wb", 128, 232, p0=32 * q, p1=32 * q + 32), r("wb", 0, 104, p0=32 * o, p1=32 * o + 32))
+        ts(r(of), r("wb"), float(496 + SW), 0.5, A.add, A.mult, off=cell("cu", 0))
+        plane(6)
+        plane(7)
+        send(rank + 1 + t, [(r(ol), r(of, 0, 8))], "al%d" % t)
+
+        for b in range(4):
+            copy("vvss"[b], r("zt", b, 512, 4), r("vp", 384 * b, 384 * b + 384), off=r(of, 0, 8))
+        quant("zq", "zsc", 0, 128, r("zt"))
+        copy("s", r("lb", 0, 128), r("tab", 0, 384), off=r(of, 0, 8))
+        for b in range(4):
+            mm(2 + b, "wq", "wsc", 128 * b, "zq", "zsc", 0, 128)
+        for b in range(4):
+            mm(even_banks[b], "eq", "es", 128 * b, tq, tsc, 128, 256, True, False)
+
+        def row(q, name, j, width, cj):
+            out = r(name, width * j, width * j + width)
+            if q == "v":
+                ts(out, r("lb", 0, width), cell("col", cj), 512.0, A.not_equal, A.mult)
+            else:
+                act(out, r("lb", 0, width), AF.Abs, cell("ncol", cj), 512.0)
+
+        for j in range(3):
+            row("v", "d1", j, 128, 8 + j)
+        for b in range(4):
+            copy("svvs"[b], r("ht", b, 512, 4), bk(2 + b), scale=0.03125)
+        row("v", "d1", 3, 128, 11)
+        quant(hq, hs, 0, 130, r("ht"))
+        send(rank + 1 + t, [(r(hq, GV, GV + 130), r(hq, 0, 130)), (r(hs, GV, GV + 130), r(hs, 0, 130))], "ah%d" % t)
+        for b in range(4):
+            mm(odd_banks[b], "eq", "es", 128 * b, tq, tsc, 0, 128, True, False)
+
+        def add_picks(banks, a):
+            for e in range(2):
+                for b in range(4):
+                    mm(banks[b], "eq", "es", 512 + 256 * b + 128 * e, pq, ps, a + 128 * e, a + 128 * e + 128, False, e == 1)
+
+        def state(q, banks, b, odd):
+            if last:
+                copy(q, r("xl", 4 * odd + b, 1024, 8), bk(banks[b]))
+            else:
+                copy(q, r("xo" if odd else "xe", b, 512, 4), bk(banks[b]))
+
+        row("s", "d1", 6, 128, 14)
+        row("s", "d1", 7, 128, 15)
+        row("v", "d1", 4, 128, 12)
+        row("v", "d1", 5, 128, 13)
+        if last:
+            lin(r("opt"), r("yb", 0, 32), 0.5, (496 + SW) / 2)
+            for a in range(4):
+                dma("y", T.op[:, 32 * a:32 * a + 32], T.opt[32 * a:32 * a + 8, :], [r("opt")], [], "outs")
+        scan(r("u1"), r("dec1"), r("d1"), 0.0, A.add, A.min)
+        copy("s", r("lb", 128, 256), r("tab", 256, 640), off=r(ol))
+        copy("v", r("iv1", 0, 8), r("u1", 127, 1024, 128))
+        turn(r("y1", 0, 32), r("iv1", 0, 32))
+        turn(r("y1", 32, 64), r("iv1", 0, 32))
+        row("v", "d2", 0, 256, 0)
+        turn(r("iv1", 32, 64), r("y1", 16, 48))
+        row("v", "d2", 1, 256, 1)
+        ts(r("f1"), r("iv1"), 127.0, 128.0, A.add, A.min, off=cell("cu", 2))
+        row("v", "d2", 7, 256, 7)
+        for j in (2, 3, 4, 5, 6):
+            row("s", "d2", j, 256, j)
+        pick_codes(r(pq, 256, 512), r(hq, 0, 130), r("f1"))
+        copy("s", r(ps, 256, 512), r(hs, 0, 130), off=r("f1"))
+        add_picks(odd_banks, 256)
+        scan(r("u2", 0, 1024), r("dec2"), r("d2", 0, 1024), 0.0, A.add, A.min)
+        scan(r("u2", 1024, 2048), r("dec2"), r("d2", 1024, 2048), 0.0, A.add, A.min)
+        copy("v", r("iv2", 0, 8), r("u2", 255, 2048, 256))
+        turn(r("y2", 0, 32), r("iv2", 0, 32))
+        turn(r("y2", 32, 64), r("iv2", 0, 32))
+        turn(r("iv2", 32, 64), r("y2", 16, 48))
+        ts(r("f2"), r("iv2"), float(GV + 127), float(GV + 128), A.add, A.min, off=cell("cu", 2))
+        for b in range(4):
+            state("s", odd_banks, b, 1)
+        for e in range(2):
+            pick_codes(r(pq, 128 * e, 128 * e + 128), r(hq, 0, GV + 130), r("f2", 8 * e, 8 * e + 8))
+            copy("s", r(ps, 128 * e, 128 * e + 128), r(hs, 0, GV + 130), off=r("f2", 8 * e, 8 * e + 8))
+        add_picks(even_banks, 0)
+        if not last:
+            quant("tq%d" % (t + 1), "ts%d" % (t + 1), 0, 128, r("xo"))
+        for b in range(4):
+            state("svvs"[b], even_banks, b, 0)
+        if not last:
+            odd_planes(t + 1)
+            quant("tq%d" % (t + 1), "ts%d" % (t + 1), 128, 256, r("xe"))
+            send_even(t + 1)
+
+    quant("lq", "ls", 0, 256, r("xl"))
+    mm(2, "vq", "vs", 0, "lq", "ls", 0, 128)
+    mm(3, "vq", "vs", 0, "lq", "ls", 128, 256)
+    dma("y", T.oc[:], T.lq[:].bitcast(dt.uint8), [r("lq")], [], "outs")
+    for k in range(2):
+        dma("s", T.osc[4 * k:4 * k + 4, :], T.ls[32 * k:32 * k + 4, :], [r("ls")], [], "outs")
+    copy("v", r("yt", 0, 128), bk(2))
+    copy("s", r("yt", 128, 256), bk(3))
+    for k in range(2, 4):
+        dma("y", T.osc[4 * k:4 * k + 4, :], T.ls[32 * k:32 * k + 4, :], [r("ls")], [], "outs")
+    dma("y", T.y[:, 0:128], T.yt[:, 0:128], [r("yt", 0, 128)], [], "outs")
+    dma("s", T.y[:, 128:256], T.yt[:, 128:256], [r("yt", 128, 256)], [], "outs")
+    for sem, cnt in total.items():
+        if known["g"].get(sem, 0) < cnt:
+            g.wait_ge(T.sem[sem], cnt)

@@ -6,7 +6,11 @@ RS = 392
 SW = 136
 GV = 144
 CODES, U8 = "float8_e4m3fn_x4", "uint8"
-F32, BF16, F16, I32, U16 = "float32", "bfloat16", "float16", "int32", "uint16"
+F32, BF16, I32, U16 = "float32", "bfloat16", "int32", "uint16"
+FIRST = ("u0 u1 u2 v0 s0 u3 v1 s1 u4 v2 m0 u5 v3 u6 s2 m1 s3 v4 t0 u7 v5 r0 m4 m2 m3 v6 l0 s6 l1 v7 k1 l2 k2 m6 l3 "
+         "t1 m7 r1 m5 k3").split()
+SECOND = ("B0 l4 B1 k0 l7 k4 l6 B2 c2 B3 l5 B4 T0 c1 M0 k7 B5 k6 S1 R0 M2 k5 S3 S4 B6 c3 S5 L0 L2 M1 B7 M6 M3 M4 T1 "
+          "L1 K2 L3 R1 c4 M5 K1 K3 c5 M7 L4 K4 L6 L5 L7 K5 K0 K7 c6 K6 p0 p1").split()
 
 SCRATCH = {}
 
@@ -23,14 +27,14 @@ for _n, _c, _d in [
     ("ij", 128, F32), ("ident", 128, F32), ("pi", 8, I32), ("bi", 8, I32), ("bf", 8, F32), ("xr", 4, F32), ("tm", 8, F32),
     ("mdiag", 128, F32), ("neg1", 256, BF16), ("cfl", 12, F32), ("cu", 12, U16),
     ("cr", 16, F32), ("col", 16, BF16), ("ncol", 16, F32), ("tab", 640, BF16),
-    ("dec1", 1024, BF16), ("dec2", 1024, BF16), ("rst", 64, F32),
-    ("so", 256, F32), ("pt", 8 * RS, F32), ("sg", 768, BF16), ("na", 2048, BF16), ("ca", 2048, BF16),
+    ("dec1", 1024, BF16), ("rst", 64, F32),
+    ("so", 256, F32), ("pt", 8 * RS, F32), ("sg", 2048, BF16), ("na", 2048, BF16), ("ca", 2048, BF16),
     ("eqa", 8, F32), ("oa", 8, F32), ("aa", 8, F32), ("ix", 10, F32), ("dd", 8, F32), ("dr", 64, F32),
-    ("sc", SW, F32), ("nb", 8 * SW, BF16), ("cb", 8 * SW, BF16), ("jb", 8 * SW, BF16),
+    ("sc", SW, F32), ("sh", 8 * SW, BF16), ("nb", 8 * SW, BF16), ("cb", 8 * SW, BF16), ("jb", 8 * SW, BF16),
     ("eqb", 8, F32), ("ob", 8, F32), ("ab", 8, F32), ("zs", 64, F32), ("zp", 64, F32), ("zg", 64, F32),
     ("wb", 232, F32), ("yb", 64, F32), ("vp", 1536, BF16), ("zt", 512, BF16), ("zq", 128, CODES), ("zsc", 128, U8),
-    ("ht", 520, BF16), ("lb", 256, BF16), ("d1", 1024, BF16), ("d2", 2048, BF16), ("u1", 1024, F16), ("u2", 2048, F16),
-    ("iv1", 64, F32), ("iv2", 64, F32), ("y1", 64, F32), ("y2", 64, F32), ("f1", 16, U16), ("f2", 16, U16),
+    ("ht", 520, BF16), ("lb", 256, BF16), ("d1", 1024, BF16), ("d2", 2048, BF16), ("u1", 1024, BF16), ("u2", 2048, BF16),
+    ("iv0", 8, F32), ("iv1", 64, F32), ("iv2", 64, F32), ("y1", 64, F32), ("y2", 64, F32), ("f1", 16, U16), ("f2", 16, U16),
 ]:
     _sb(_n, _c, _d)
 for _t in range(R):
@@ -192,22 +196,22 @@ def rank_program(g, core, T, topo):
         run("v", lambda e: e.tensor_copy(ap(out).bitcast(dt.uint32), ap(win).bitcast(dt.uint32).indirect(ap(off))),
             [win, off], [out])
 
-    def send(dst_rank, pairs, sem):
+    shared = [e for e in range(16) if all(e in topo.engines(core, c) for c in T.cores if c != core)]
+
+    def send(dst_rank, pairs, sem, apart=False):
         dst = T.cores[dst_rank % n]
         rid, pid, _ = topo.addr(dst)
-        for out, in_ in pairs:
+        total[sem] = 0
+        for i, (out, in_) in enumerate(pairs):
+            lanes = shared[i::len(pairs)] if apart else shared
             order("g", [in_], [])
             a, b = ap(out), ap(in_)
             if SCRATCH[in_[0]][2] == CODES:
                 a, b = a.bitcast(dt.uint8), b.bitcast(dt.uint8)
-            total["sent"] = total.get("sent", 0) + lanes
-            g.remote_dma(a, b, T.sem[sem], T.sem["sent"], pid, rid, lane_mask)
-        total[sem] = lanes * len(pairs)
+            total["sent"] = total.get("sent", 0) + len(lanes)
+            total[sem] += len(lanes)
+            g.remote_dma(a, b, T.sem[sem], T.sem["sent"], pid, rid, sum(1 << e for e in lanes))
         note("far", [], [out for out, in_ in pairs], sem, total[sem])
-
-    shared = [e for e in range(16) if all(e in topo.engines(core, c) for c in T.cores if c != core)]
-    lanes = len(shared)
-    lane_mask = sum(1 << e for e in shared)
 
     def bk(b, a=0, z=128):
         return r("bk%d" % b, a, z)
@@ -217,6 +221,9 @@ def rank_program(g, core, T, topo):
 
     def cell(name, j):
         return r(name, j, j + 1)
+
+    def part(name, width, k):
+        return r(name, width * k, width * k + width)
 
     dma("y", T.xn[:, 0:512], T.x[:, 0:512], [], [r("xn", 0, 512)], "lx0")
     dma("s", T.xn[:, 512:1024], T.x[:, 512:1024], [], [r("xn", 512, 1024)], "lx1")
@@ -256,6 +263,7 @@ def rank_program(g, core, T, topo):
     ts(cell("bi", 7), cell("pi", 6), 15, None, A.bitwise_and)
     quant("eq", "es", 768, 1024, r("eb", 515, 1539))
     copy("v", r("bf"), r("bi"))
+    quant("eq", "es", 1024, 1280, r("eb", 514, 1538))
 
     for j in range(4):
         copy("v", r("xe", j, 512, 4), r("xn", j, 1024, 8))
@@ -265,28 +273,27 @@ def rank_program(g, core, T, topo):
 
     def send_even(t):
         tq, tsc = "tq%d" % t, "ts%d" % t
-        send(rank - 1 - t, [(r(tq, 256, 384), r(tq, 128, 256)), (r(tsc, 256, 384), r(tsc, 128, 256))], "at%d" % t)
+        send(rank - 1 - t, [(r(tq, 256, 384), r(tq, 128, 256)), (r(tsc, 256, 384), r(tsc, 128, 256))], "at%d" % t, t == 0)
 
     send_even(0)
     iota(r("tab", 0, 256), [[1, 256]], 0, 0)
     iota(r("tab", 256, 512), [[0, 256]], 300, 0)
     iota(r("tab", 512, 640), [[2, 128]], 0, 0)
     iota(r("dec1"), [[0, 1024]], -1, 0)
-    iota(r("dec2"), [[0, 1024]], -1, 0)
     iota(r("dec1", 0, 1024, 128), [[0, 8]], 1024, 0)
-    iota(r("dec2", 0, 1024, 256), [[0, 4]], 1024, 0)
-    iota(r("dec2", 128, 1024, 256), [[0, 4]], 127 - GV, 0)
     quant("tq0", "ts0", 0, 128, r("xo"))
+    quant("eq", "es", 1280, 1536, r("eb", 513, 1537))
 
-    def offsets_that_are_constants():
-        for k in range(3):
-            act(cell("xr", k), cell("bf", k), AF.Abs, cell("bf", k + 4), -1.0)
-        act(cell("xr", 3), cell("bf", 3), AF.Abs, cell("bf", 4), -1.0)
-        lin(cell("tm", 0), cell("bf", 5), 2.0, cell("bf", 4))
-        lin(cell("tm", 5), cell("bf", 3), -8.0, cell("bf", 7))
-        lin(cell("tm", 6), cell("bf", 7), 2.0, 0.0)
-        lin(cell("tm", 1), cell("bf", 6), 4.0, cell("tm", 0))
-        lin(cell("tm", 4), cell("bf", 3), float(SW), cell("tm", 5))
+    for k in range(3):
+        act(cell("xr", k), cell("bf", k), AF.Abs, cell("bf", k + 4), -1.0)
+    act(cell("xr", 3), cell("bf", 3), AF.Abs, cell("bf", 4), -1.0)
+    lin(cell("tm", 0), cell("bf", 5), 2.0, cell("bf", 4))
+    lin(cell("tm", 5), cell("bf", 3), -8.0, cell("bf", 7))
+    lin(cell("tm", 6), cell("bf", 7), 2.0, 0.0)
+    lin(cell("tm", 1), cell("bf", 6), 4.0, cell("tm", 0))
+    lin(cell("tm", 4), cell("bf", 3), float(SW), cell("tm", 5))
+
+    def more_constants():
         lin(cell("cfl", 2), cell("xr", 3), 32.0, cell("tm", 5))
         lin(cell("tm", 2), cell("xr", 0), 64.0, cell("tm", 1))
         lin(r("cfl", 4, 8), r("cr", 0, 4), 2.0 * SW / 32, cell("tm", 4))
@@ -304,159 +311,87 @@ def rank_program(g, core, T, topo):
         for b in range(4):
             copy("s", r("vp", 384 * b + 1, 384 * b + 256, 2), bk(2 + b))
 
+    def odd_scores(t):
+        mm(5, "tq%d" % t, "ts%d" % t, 0, "tq%d" % t, "ts%d" % t, 0, 128)
+        tt(r("so", 1, 256, 2), bk(5), r("mdiag"), A.add)
+
+    def plane(i):
+        b = i // 2
+        if i % 2:
+            copy("s", r("vp", 384 * b + 256, 384 * b + 384), bk(2 + b, 128, 256))
+        else:
+            copy("s", r("vp", 384 * b, 384 * b + 256, 2), bk(2 + b))
+
+    def step(word):
+        c, k = word[0], int(word[1])
+        own = c.islower()
+        sco, wd, at = (r("so"), 256, 256) if own else (r("sc"), SW, 384)
+        sg, na, ca, eq, oo = ("sg", "na", "ca", "eqa", "oa") if own else ("sh", "nb", "cb", "eqb", "ob")
+        odd = r("so", 1, 256, 2)
+        if c == "u":
+            scan(prow(k, 1, 129), odd, prow(k - 1, 0, 128) if k else odd, -BIG, A.max, A.min if k else A.max)
+        elif c == "v":
+            scan(prow(k, 129, 257), bk(0), prow(k - 1, 128, 256) if k else odd, prow(k, 128, 129),
+                 A.max, A.min if k else A.max)
+        elif c == "B":
+            scan(prow(k, 257, 385), bk(1), prow(k - 1, 256, 384) if k else r("so", 0, 128), prow(k, 256, 257),
+                 A.max, A.min if k else A.max)
+        elif c in "sS":
+            act(part(sg, wd, k), sco, AF.Sign, prow(k, at, at + 1), -1.0)
+        elif c in "mM":
+            if ("s%d" if own else "S%d") % k in FIRST + SECOND:
+                act(part(na, wd, k), part(sg, wd, k), AF.Abs, 0.0, 1.0)
+            else:
+                ts(part(na, wd, k), sco, prow(k, at, at + 1), None, A.not_equal)
+        elif c in "lL":
+            scan(part(ca, wd, k), part(na, wd, k), r("neg1", 0, wd), cell(oo, k), A.add, A.add)
+        elif c in "kK":
+            act(part("ca" if own else "jb", wd, k), part(ca, wd, k), AF.Sign, 0.5, 1.0, cell("aa" if own else "ab", k))
+        elif c in "tT":
+            a, z = max(4 * k, 1), 4 * k + 4
+            tt(r(eq, a, z), r("pt", a * RS + at, z * RS, RS), r("pt", (a - 1) * RS + at, (z - 1) * RS, RS), A.is_equal)
+        elif c in "rR":
+            a, z = 4 * k, 4 * k + 4
+            scan(r(oo, a, z), r(eq, a, z), r(eq, a, z), cell(oo, a - 1) if a else 0.0, A.mult, A.add)
+        elif c == "p":
+            plane(k)
+        elif k == 1:
+            copy("s", r("sc", 0, 8), r("pt", 256, 8 * RS, RS))
+        elif k == 2:
+            copy("v", r("sc", 8, SW), bk(1))
+        elif k == 3:
+            lin(r("ix", 0, 8), r("aa"), 0.5, 128.0)
+        elif k == 4:
+            tt(r("dd"), r("ix", 1, 9), r("ix", 0, 8), A.subtract)
+        elif k == 5:
+            act(r("dr"), r("dd"), AF.Identity, -1.0, 1.0, off=r("cu", 8, 12))
+        else:
+            ts(r("zs"), r("cb"), 0.0, -2.0, A.is_lt, A.mult, off=r("cu", 4, 8))
+
     for t in range(R):
         tq, tsc, hq, hs = "tq%d" % t, "ts%d" % t, "hq%d" % t, "hs%d" % t
         pq, ps, of, ol = "pq%d" % t, "ps%d" % t, "of%d" % t, "ol%d" % t
         last = t == R - 1
 
-        mm(6, tq, tsc, 0, tq, tsc, 0, 128)
+        if t == 0:
+            odd_scores(0)
         mm(0, tq, tsc, 0, tq, tsc, 128, 256)
-        tt(r("so", 1, 256, 2), bk(6), r("mdiag"), A.add)
-        copy("s", r("so", 0, 256, 2), bk(0))
+        mm(6, tq, tsc, 0, tq, tsc, 128, 256)
+        copy("s", r("so", 0, 256, 2), bk(6))
         if t == 0:
-            offsets_that_are_constants()
-
-        def best_a(k):
-            if k == 0:
-                scan(prow(0, 1, 257), r("so"), r("so"), -BIG, A.max, A.max)
-            else:
-                scan(prow(k, 1, 257), r("so"), prow(k - 1, 0, 256), -BIG, A.max, A.min)
-
-        def match_a(k):
-            ts(r("na", 256 * k, 256 * k + 256), r("so"), prow(k, 256, 257), None, A.not_equal)
-
-        def sign_a(k):
-            act(r("sg", 128 * k - 256, 128 * k), r("so"), AF.Sign, prow(k, 256, 257), -1.0)
-
-        def abs_a(k):
-            act(r("na", 256 * k, 256 * k + 256), r("sg", 128 * k - 256, 128 * k), AF.Abs, 0.0, 1.0)
-
-        def ties(e, at, k0, k1):
-            a = max(k0, 1)
-            tt(r(e, a, k1), r("pt", a * RS + at, k1 * RS, RS), r("pt", (a - 1) * RS + at, (k1 - 1) * RS, RS), A.is_equal)
-
-        def runs(e, o, k0, k1):
-            scan(r(o, k0, k1), r(e, k0, k1), r(e, k0, k1), cell(o, k0 - 1) if k0 else 0.0, A.mult, A.add)
-
-        def left_a(k):
-            scan(r("ca", 256 * k, 256 * k + 256), r("na", 256 * k, 256 * k + 256), r("neg1"), cell("oa", k), A.add, A.add)
-
-        def count_a(k):
-            row = r("ca", 256 * k, 256 * k + 256)
-            act(row, row, AF.Sign, 0.5, 1.0, cell("aa", k))
-
-        best_a(0)
-        act(r("ca", 0, 256), prow(0, 1, 257), AF.Sign, prow(0, 256, 257), -1.0, cell("ix", 0))
-        best_a(1)
-        best_a(2)
-        sign_a(2)
-        match_a(1)
-        best_a(3)
-        abs_a(2)
-        ties("eqa", 256, 0, 4)
-        best_a(4)
-        sign_a(4)
-        runs("eqa", "oa", 0, 4)
-        best_a(5)
-        left_a(1)
-        abs_a(4)
-        best_a(6)
-        left_a(2)
-        count_a(1)
-        best_a(7)
-        sign_a(6)
-        match_a(3)
-        ties("eqa", 256, 4, 8)
-        count_a(2)
-        abs_a(6)
-        match_a(5)
-        runs("eqa", "oa", 4, 8)
-        left_a(3)
-        copy("s", r("sc", 0, 8), r("pt", 256, 8 * RS, RS))
-        match_a(7)
-        count_a(3)
-        for k in (4, 5, 6, 7):
-            left_a(k)
-        if t == 0:
-            copy("v", r("cu"), r("cfl"))
-            for b in range(2, 4):
-                quant("eq", "es", 512 + 256 * b, 768 + 256 * b, r("eb", 516 - b, 1540 - b))
-            quant("vq", "vs", 0, 128, r("vt"))
-        for k in (4, 5, 6, 7):
-            count_a(k)
-        lin(r("ix", 1, 8), r("aa", 1, 8), 0.5, 128.0)
+            more_constants()
+        for i, word in enumerate(FIRST):
+            step(word)
+            if t == 0 and i == 20:
+                copy("v", r("cu"), r("cfl"))
         if t == 0:
             odd_planes(0)
 
         mm(1, tq, tsc, 0, tq, tsc, 256, 384)
         for b in range(4):
             mm(2 + b, "eq", "es", 128 * b, tq, tsc, 128, 384)
-
-        def plane(i):
-            b = i // 2
-            if i % 2:
-                copy("s", r("vp", 384 * b + 256, 384 * b + 384), bk(2 + b, 128, 256))
-            else:
-                copy("s", r("vp", 384 * b, 384 * b + 256, 2), bk(2 + b))
-
-        def best_b(k):
-            if k == 0:
-                scan(prow(0, 257, 385), bk(1), r("so", 0, 128), prow(0, 256, 257), A.max, A.max)
-            else:
-                scan(prow(k, 257, 385), bk(1), prow(k - 1, 256, 384), prow(k, 256, 257), A.max, A.min)
-
-        def match_b(k):
-            ts(r("nb", SW * k, SW * k + SW), r("sc"), prow(k, 384, 385), None, A.not_equal)
-
-        def sign_b(k):
-            act(r("sg", SW * k - 2 * SW, SW * k - SW), r("sc"), AF.Sign, prow(k, 384, 385), -1.0)
-
-        def abs_b(k):
-            act(r("nb", SW * k, SW * k + SW), r("sg", SW * k - 2 * SW, SW * k - SW), AF.Abs, 0.0, 1.0)
-
-        def left_b(k):
-            scan(r("cb", SW * k, SW * k + SW), r("nb", SW * k, SW * k + SW), r("neg1", 0, SW), cell("ob", k), A.add, A.add)
-
-        def count_b(k):
-            act(r("jb", SW * k, SW * k + SW), r("cb", SW * k, SW * k + SW), AF.Sign, 0.5, 1.0, cell("ab", k))
-
-        best_b(0)
-        copy("v", r("sc", 8, SW), bk(1))
-        best_b(1)
-        match_b(0)
-        best_b(2)
-        match_b(1)
-        best_b(3)
-        plane(0)
-        match_b(2)
-        best_b(4)
-        sign_b(3)
-        ties("eqb", 384, 0, 4)
-        best_b(5)
-        sign_b(4)
-        abs_b(3)
-        runs("eqb", "ob", 0, 4)
-        tt(r("dd"), r("ix", 1, 9), r("ix", 0, 8), A.subtract)
-        best_b(6)
-        sign_b(5)
-        abs_b(4)
-        abs_b(5)
-        act(r("dr"), r("dd"), AF.Identity, -1.0, 1.0, off=r("cu", 8, 12))
-        left_b(0)
-        left_b(1)
-        best_b(7)
-        left_b(2)
-        left_b(3)
-        ties("eqb", 384, 4, 8)
-        match_b(6)
-        runs("eqb", "ob", 4, 8)
-        match_b(7)
-        for k in range(4, 8):
-            left_b(k)
-        for k in range(8):
-            count_b(k)
-        plane(1)
-        ts(r("zs"), r("cb"), 0.0, -2.0, A.is_lt, A.mult, off=r("cu", 4, 8))
+        for word in SECOND:
+            step(word)
         tt(r("zp"), r("zs"), r("dr"), A.mult)
         scan(r("zg"), r("rst"), r("zp"), 0.0, A.mult, A.add)
         tt(r("wb", 0, 8), r("zg", 7, 64, 8), r("ab"), A.add)
@@ -489,18 +424,20 @@ def rank_program(g, core, T, topo):
         for b in range(4):
             mm(even_banks[b], "eq", "es", 128 * b, tq, tsc, 128, 256, True, False)
 
-        def row(q, name, j, width, cj):
-            out = r(name, width * j, width * j + width)
+        def row(q, name, j, cj, giver=0):
+            out = r(name, 128 * j, 128 * j + 128)
+            lst = r("lb", 128 * giver, 128 * giver + 128)
             if q == "v":
-                ts(out, r("lb", 0, width), cell("col", cj), 512.0, A.not_equal, A.mult)
+                ts(out, lst, cell("col", cj), 512.0, A.not_equal, A.mult)
             else:
-                act(out, r("lb", 0, width), AF.Abs, cell("ncol", cj), 512.0)
+                act(out, lst, AF.Abs, cell("ncol", cj), 512.0)
 
-        for j in range(3):
-            row("v", "d1", j, 128, 8 + j)
+        for j in range(5):
+            row("v", "d1", j, 8 + j)
         for b in range(4):
             copy("svvs"[b], r("ht", b, 512, 4), bk(2 + b), scale=0.03125)
-        row("v", "d1", 3, 128, 11)
+        for j in range(5, 8):
+            row("v", "d1", j, 8 + j)
         quant(hq, hs, 0, 130, r("ht"))
         send(rank + 1 + t, [(r(hq, GV, GV + 130), r(hq, 0, 130)), (r(hs, GV, GV + 130), r(hs, 0, 130))], "ah%d" % t)
         for b in range(4):
@@ -517,32 +454,31 @@ def rank_program(g, core, T, topo):
             else:
                 copy(q, r("xo" if odd else "xe", b, 512, 4), bk(banks[b]))
 
-        row("s", "d1", 6, 128, 14)
-        row("s", "d1", 7, 128, 15)
-        row("v", "d1", 4, 128, 12)
-        row("v", "d1", 5, 128, 13)
         if last:
             lin(r("opt"), r("yb", 0, 32), 0.5, (496 + SW) / 2)
             for a in range(4):
                 dma("y", T.op[:, 32 * a:32 * a + 32], T.opt[32 * a:32 * a + 8, :], [r("opt")], [], "outs")
+        for j in range(5):
+            row("s", "d2", j, j)
         scan(r("u1"), r("dec1"), r("d1"), 0.0, A.add, A.min)
-        copy("s", r("lb", 128, 256), r("tab", 256, 640), off=r(ol))
+        for j in (5, 6, 7):
+            row("v", "d2", j, j)
         copy("v", r("iv1", 0, 8), r("u1", 127, 1024, 128))
         turn(r("y1", 0, 32), r("iv1", 0, 32))
         turn(r("y1", 32, 64), r("iv1", 0, 32))
-        row("v", "d2", 0, 256, 0)
+        scan(r("u2", 0, 512), r("dec1", 0, 512), r("d2", 0, 512), 0.0, A.add, A.min)
         turn(r("iv1", 32, 64), r("y1", 16, 48))
-        row("v", "d2", 1, 256, 1)
+        scan(r("u2", 512, 1024), r("dec1", 0, 512), r("d2", 512, 1024), 0.0, A.add, A.min)
         ts(r("f1"), r("iv1"), 127.0, 128.0, A.add, A.min, off=cell("cu", 2))
-        row("v", "d2", 7, 256, 7)
-        for j in (2, 3, 4, 5, 6):
-            row("s", "d2", j, 256, j)
+        copy("s", r("lb", 128, 256), r("tab", 256, 640), off=r(ol))
+        for j in range(8):
+            row("s", "d2", 8 + j, j, 1)
+        ts(r("iv0"), r("u2", 127, 1024, 128), float(-GV), None, A.add)
         pick_codes(r(pq, 256, 512), r(hq, 0, 130), r("f1"))
         copy("s", r(ps, 256, 512), r(hs, 0, 130), off=r("f1"))
         add_picks(odd_banks, 256)
-        scan(r("u2", 0, 1024), r("dec2"), r("d2", 0, 1024), 0.0, A.add, A.min)
-        scan(r("u2", 1024, 2048), r("dec2"), r("d2", 1024, 2048), 0.0, A.add, A.min)
-        copy("v", r("iv2", 0, 8), r("u2", 255, 2048, 256))
+        scan(r("u2", 1024, 2048), r("dec1"), r("d2", 1024, 2048), 0.0, A.add, A.min)
+        tt(r("iv2", 0, 8), r("u2", 1024 + 127, 2048, 128), r("iv0"), A.min)
         turn(r("y2", 0, 32), r("iv2", 0, 32))
         turn(r("y2", 32, 64), r("iv2", 0, 32))
         turn(r("iv2", 32, 64), r("y2", 16, 48))
@@ -553,11 +489,14 @@ def rank_program(g, core, T, topo):
             pick_codes(r(pq, 128 * e, 128 * e + 128), r(hq, 0, GV + 130), r("f2", 8 * e, 8 * e + 8))
             copy("s", r(ps, 128 * e, 128 * e + 128), r(hs, 0, GV + 130), off=r("f2", 8 * e, 8 * e + 8))
         add_picks(even_banks, 0)
-        if not last:
+        if last:
+            quant("vq", "vs", 0, 128, r("vt"))
+        else:
             quant("tq%d" % (t + 1), "ts%d" % (t + 1), 0, 128, r("xo"))
         for b in range(4):
             state("svvs"[b], even_banks, b, 0)
         if not last:
+            odd_scores(t + 1)
             odd_planes(t + 1)
             quant("tq%d" % (t + 1), "ts%d" % (t + 1), 128, 256, r("xe"))
             send_even(t + 1)

@@ -2,17 +2,24 @@ from concourse.mybir import dt, AluOpType, ActivationFunctionType
 
 C, K, R = 256, 128, 3
 BIG = 1.0e29
-RS = 392
+RS = 385
 SW = 136
-GV = 144
+GV, EW = 144, 288
+STEP = 2.0 ** -13
+TRI = 576
 CODES, U8 = "float8_e4m3fn_x4", "uint8"
 F32, BF16, I32, U16 = "float32", "bfloat16", "int32", "uint16"
-FIRST = ("u0 u1 u2 v0 s0 u3 v1 s1 u4 v2 m0 u5 v3 u6 s2 m1 s3 v4 t0 u7 v5 r0 m4 m2 m3 v6 l0 s6 l1 v7 k1 l2 k2 m6 l3 "
-         "t1 m7 r1 m5 k3").split()
-SECOND = ("B0 l4 B1 k0 l7 k4 l6 B2 c2 B3 l5 B4 T0 c1 M0 k7 B5 k6 S1 R0 M2 k5 S3 S4 B6 c3 S5 L0 L2 M1 B7 M6 M3 M4 T1 "
-          "L1 K2 L3 R1 c4 M5 K1 K3 c5 M7 L4 K4 L6 L5 L7 K5 K0 K7 c6 K6 p0 p1").split()
+CYCLE, WAKE, LOAD, FLIGHT, HOP = 0.83e-3, 0.175, 2.0, 2.2, 1.6
+FIX, FIRST, ODD = 0.05, 1.5, 0.0
+SLACK, SPARE = 0.1, {"v": 0.1}
+BY_SIGN = (0, 1, 2, 3)
+BY_SCAN = ()
+ROWS_S = (0, 1, 2, 3)
+TIES = ((1, 4), (4, 7), (7, 8))
+HALVES, LIST, LEAD = 1, 23, 0.0
 
 SCRATCH = {}
+PLAN = []
 
 
 def _sb(name, cols, dtype):
@@ -23,29 +30,32 @@ for _n, _c, _d in [
     ("xn", 1024, BF16), ("xe", 512, BF16), ("xo", 512, BF16), ("xl", 1024, BF16), ("vt", 512, BF16),
     ("vq", 128, CODES), ("vs", 128, U8), ("wq", 512, CODES), ("wsc", 512, U8),
     ("lq", 256, CODES), ("ls", 256, U8), ("yt", 256, F32), ("opt", 32, F32),
-    ("eb", 1540, BF16), ("eq", 1536, CODES), ("es", 1536, U8),
-    ("ij", 128, F32), ("ident", 128, F32), ("pi", 8, I32), ("bi", 8, I32), ("bf", 8, F32), ("xr", 4, F32), ("tm", 8, F32),
-    ("mdiag", 128, F32), ("neg1", 256, BF16), ("cfl", 12, F32), ("cu", 12, U16),
-    ("cr", 16, F32), ("col", 16, BF16), ("ncol", 16, F32), ("tab", 640, BF16),
-    ("dec1", 1024, BF16), ("rst", 64, F32),
-    ("so", 256, F32), ("pt", 8 * RS, F32), ("sg", 2048, BF16), ("na", 2048, BF16), ("ca", 2048, BF16),
-    ("eqa", 8, F32), ("oa", 8, F32), ("aa", 8, F32), ("ix", 10, F32), ("dd", 8, F32), ("dr", 64, F32),
-    ("sc", SW, F32), ("sh", 8 * SW, BF16), ("nb", 8 * SW, BF16), ("cb", 8 * SW, BF16), ("jb", 8 * SW, BF16),
-    ("eqb", 8, F32), ("ob", 8, F32), ("ab", 8, F32), ("zs", 64, F32), ("zp", 64, F32), ("zg", 64, F32),
-    ("wb", 232, F32), ("yb", 64, F32), ("vp", 1536, BF16), ("zt", 512, BF16), ("zq", 128, CODES), ("zsc", 128, U8),
-    ("ht", 520, BF16), ("lb", 256, BF16), ("d1", 1024, BF16), ("d2", 2048, BF16), ("u1", 1024, BF16), ("u2", 2048, BF16),
-    ("iv0", 8, F32), ("iv1", 64, F32), ("iv2", 64, F32), ("y1", 64, F32), ("y2", 64, F32), ("f1", 16, U16), ("f2", 16, U16),
+    ("eb", 516, BF16), ("eq", 512, CODES), ("es", 512, U8),
+    ("ij", 128, F32), ("ii", 128, F32), ("pi", 8, I32), ("bi", 8, I32), ("bf", 8, F32),
+    ("xr", 4, F32), ("tm", 8, F32), ("qc", 8, F32), ("tb", 160, F32), ("tc", 160, F32),
+    ("mdiag", 128, F32), ("neg1", 256, BF16), ("one", SW, BF16), ("cfl", 22, F32), ("cu", 22, U16),
+    ("tab", 384, BF16), ("kk", 128, BF16), ("dm", 128, F32), ("rst", 128, BF16), ("stp", 8, BF16),
+    ("vr", 48, F32), ("ac", 8, F32), ("nme", 16, F32),
+    ("wrow", TRI, BF16),
+    ("so", 256, F32), ("pt", 8 * RS, F32), ("xg", 256, BF16), ("xh", 256, BF16), ("ma", 256, BF16), ("mb", 256, BF16),
+    ("ya", 8, F32), ("ta", 8, F32), ("junk", 1024, F32), ("sums", 1024, F32), ("wi", 8, I32), ("pu", 8, U16),
+    ("gv", 128, F32), ("vv", 128, F32), ("pf", 16, BF16), ("pr", 128, BF16),
+    ("sg", 256, BF16), ("sc", SW, F32), ("sh", 8 * SW, BF16), ("nb", 8 * SW, BF16), ("cb", 8 * SW, BF16), ("jb", 1024, BF16),
+    ("eqb", 8, F32), ("zc", 8, F32), ("et", 128, BF16), ("yy", 128, BF16), ("zz", 128, BF16), ("ab", 8, F32),
+    ("wb", 232, BF16), ("yb", 64, BF16), ("vp", 1536, BF16), ("zt", 512, BF16), ("zq", 128, CODES), ("zsc", 128, U8),
+    ("ht", 512, BF16), ("lb", 128, BF16), ("me", 16, BF16), ("dd", TRI, BF16), ("du", TRI, BF16),
+    ("da", 16, F32), ("sf", 16, U16), ("win", 65536, BF16), ("ro", 288, BF16), ("rv", 288, BF16), ("rp", 288, BF16),
+    ("fe", 16, BF16), ("fm", 8, F32), ("f1", 16, U16), ("f2", 8, U16), ("ep", 4 * EW, BF16),
 ]:
     _sb(_n, _c, _d)
 for _t in range(R):
     _sb("tq%d" % _t, 384, CODES)
     _sb("ts%d" % _t, 384, U8)
-    _sb("hq%d" % _t, 288, CODES)
-    _sb("hs%d" % _t, 288, U8)
-    _sb("pq%d" % _t, 512, CODES)
-    _sb("ps%d" % _t, 512, U8)
+    _sb("hq%d" % _t, 256, CODES)
+    _sb("hs%d" % _t, 256, U8)
     _sb("of%d" % _t, 16, U16)
-    _sb("ol%d" % _t, 8, U16)
+    _sb("gl%d" % _t, 16, BF16)
+    _sb("gr%d" % _t, 8, BF16)
 for _b in range(8):
     SCRATCH["bk%d" % _b] = ("psum", [128, 512], F32)
 
@@ -54,6 +64,7 @@ SEMAPHORES = ["cv", "cs", "ct", "cg", "lx0", "lx1", "lv", "lwc", "lws", "sent", 
 
 A = AluOpType
 AF = ActivationFunctionType
+WIDTH = {F32: 4, I32: 4, CODES: 4, BF16: 2, U16: 2, U8: 1}
 
 
 def r(name, c0=0, c1=None, st=1, p0=0, p1=128):
@@ -62,12 +73,75 @@ def r(name, c0=0, c1=None, st=1, p0=0, p1=128):
     return (name, p0, p1, c0, c1, st)
 
 
-def _meet(a, b):
+def cols(x):
+    return len(range(x[3], x[4], x[5]))
+
+
+def is_bank(x):
+    return SCRATCH[x[0]][0] == "psum"
+
+
+def meet(a, b):
     if a[0] != b[0] or a[2] <= b[1] or b[2] <= a[1] or a[4] <= b[3] or b[4] <= a[3]:
         return False
     if a[5] == 1 and b[5] == 1:
         return True
     return not set(range(a[3], a[4], a[5])).isdisjoint(range(b[3], b[4], b[5]))
+
+
+def arrange(calls):
+    before, after, seen = [], [[] for c in calls], {}
+    for i, (forms, reads, writes, delay, urgency) in enumerate(calls):
+        deps = {}
+        for regs, wr in ((reads, False), (writes, True)):
+            for x in regs:
+                for (y, w, j) in seen.get(x[0], ()):
+                    if is_bank(x):
+                        alone = len(forms) == 1 and list(forms) == list(calls[j][0])
+                        if w or wr or not alone:
+                            deps[j] = max(deps.get(j, 0.0), 0.0 if alone else WAKE)
+                    elif (w or wr) and meet(x, y):
+                        deps[j] = (calls[j][3] if w else 0.0) + WAKE
+        before.append(deps)
+        for j in deps:
+            after[j].append(i)
+        for regs, wr in ((reads, False), (writes, True)):
+            for x in regs:
+                seen.setdefault(x[0], []).append((x, wr, i))
+    way = [0.0] * len(calls)
+    for i in range(len(calls) - 1, -1, -1):
+        forms, reads, writes, delay, extra = calls[i]
+        way[i] = min(c for c, f in forms.values()) + max([way[j] + before[j][i] for j in after[i]] + [delay])
+    urgent = [-w - c[4] for w, c in zip(way, calls)]
+    got, free = {}, {q: 0.0 for q in "vstgy"}
+    left = [len(deps) for deps in before]
+    ready = {i: 0.0 for i in range(len(calls)) if not left[i]}
+    while ready:
+        q = min(free, key=free.get)
+        now = free[q]
+
+        def fits(i):
+            forms = calls[i][0]
+            return q in forms and all(max(now, ready[i]) + forms[q][0] + SPARE.get(q, 0.0) <=
+                                      max(free[o], ready[i]) + forms[o][0] + SPARE.get(o, 0.0) for o in forms)
+        mine = sorted((i for i in ready if fits(i)), key=lambda i: (urgent[i], i))
+        until, chosen = float("inf"), None
+        for i in mine:
+            if ready[i] <= now and now + calls[i][0][q][0] <= until:
+                chosen = i
+                break
+            until = min(until, ready[i] + SLACK)
+        if chosen is None:
+            free[q] = min([ready[i] for i in mine if ready[i] > now] + [t for t in free.values() if t > now] + [now + 0.05])
+            continue
+        free[q] = now + calls[chosen][0][q][0]
+        got[chosen] = (now, free[q], q)
+        del ready[chosen]
+        for j in after[chosen]:
+            left[j] -= 1
+            if not left[j]:
+                ready[j] = max(got[k][1] + gap for k, gap in before[j].items())
+    return [(i, got[i][2]) for i in sorted(got, key=lambda i: (got[i][0], i))]
 
 
 def rank_program(g, core, T, topo):
@@ -80,6 +154,9 @@ def rank_program(g, core, T, topo):
     total = {}
     known = {q: {} for q in queues}
     touched = {}
+    calls = []
+    bonus = [0.0]
+    level = [10 ** 6]
 
     def ap(x):
         if x[5] == 1:
@@ -93,22 +170,15 @@ def rank_program(g, core, T, topo):
         need = {}
         for regs, wr in ((reads, False), (writes, True)):
             for x in regs:
-                bank = SCRATCH[x[0]][0] == "psum"
                 for (y, w, oq, sem, cnt, clock) in touched.get(x[0], ()):
-                    if bank:
-                        hit = oq != q
-                    else:
-                        hit = (w or wr) and _meet(x, y)
+                    hit = oq != q if is_bank(x) else (w or wr) and meet(x, y)
                     if hit and need.get(sem, (0, None))[0] < cnt:
                         need[sem] = (cnt, clock)
         kn = known[q]
-        todo = []
         for sem, (cnt, clock) in need.items():
             covered = any(o != sem and c2.get(sem, 0) >= cnt for o, (k2, c2) in need.items())
             if kn.get(sem, 0) < cnt and not covered:
-                todo.append((sem, cnt))
-        for sem, cnt in todo:
-            queues[q].wait_ge(T.sem[sem], cnt)
+                queues[q].wait_ge(T.sem[sem], cnt)
         for sem, (cnt, clock) in need.items():
             kn[sem] = max(kn.get(sem, 0), cnt)
             for s2, c2 in clock.items():
@@ -120,98 +190,129 @@ def rank_program(g, core, T, topo):
             for x in regs:
                 touched.setdefault(x[0], []).append((x, wr, q, sem, cnt, clock))
 
-    def run(q, call, reads, writes):
+    def add(forms, reads, writes):
         reads = [x for x in reads if isinstance(x, tuple)]
-        order(q, reads, writes)
-        sem = counter[q]
-        total[sem] = total.get(sem, 0) + 1
-        call(queues[q]).then_inc(T.sem[sem], 1)
-        note(q, reads, writes, sem, total[sem])
 
-    def dma(q, out, in_, reads, writes, sem):
-        order(q, reads, writes)
-        total[sem] = total.get(sem, 0) + 16
-        queues[q].dma_start(out, in_).then_inc(T.sem[sem], 16)
-        note("dma", reads, writes, sem, total[sem])
+        def issue(q, call):
+            def go():
+                order(q, reads, writes)
+                sem = counter[q]
+                total[sem] = total.get(sem, 0) + 1
+                call(queues[q]).then_inc(T.sem[sem], 1)
+                note(q, reads, writes, sem, total[sem])
+            return go
+        calls.append(({q: (c, issue(q, f)) for q, (c, f) in forms.items()}, reads, writes, 0.0, bonus[0]))
+
+    def dma(q, out, in_, reads, writes, sem, delay=LOAD):
+        def go():
+            order(q, reads, writes)
+            total[sem] = total.get(sem, 0) + 16
+            queues[q].dma_start(out, in_).then_inc(T.sem[sem], 16)
+            note("dma", reads, writes, sem, total[sem])
+        calls.append(({q: (0.06, go)}, reads, writes, delay, 0.0))
 
     def src(x, off):
         return ap(x) if off is None else ap(x).indirect(ap(off))
 
-    def copy(q, out, in_, off=None, scale=None):
-        if q == "v":
-            if scale is None:
-                run(q, lambda e: e.tensor_copy(ap(out), src(in_, off)), [in_, off], [out])
-            else:
-                ts(out, in_, scale, None, A.mult, off=off)
-        elif scale is not None:
-            run(q, lambda e: e.activation(ap(out), src(in_, off), AF.Copy, scale=scale), [in_, off], [out])
-        else:
-            run(q, lambda e: e.activation(ap(out), src(in_, off), AF.Copy), [in_, off], [out])
+    def vcost(out, ins, off=None, rate=None):
+        if off is not None:
+            return 0.05 + 1.5 * 16 * cols(off) * CYCLE
+        sides = [x for x in [out] + ins if isinstance(x, tuple)]
+        if rate is None:
+            rate = 0.5 if all(WIDTH[SCRATCH[x[0]][2]] == 2 for x in sides) else 1.0
+        return FIX + rate * cols(out) * CYCLE
 
-    def ts(out, in_, s1, s2, op0, op1=None, off=None):
+    def scost(out, off=None):
+        return FIX + (1.0 if off is None else 1.5) * cols(out) * CYCLE
+
+    def ts_form(out, in_, s1, s2, op0, op1=None, off=None):
         if op1 is None:
-            call = lambda e: e.tensor_scalar(ap(out), src(in_, off), val(s1), None, op0)
-        else:
-            call = lambda e: e.tensor_scalar(ap(out), src(in_, off), val(s1), val(s2), op0, op1)
-        run("v", call, [in_, off, s1, s2], [out])
+            return vcost(out, [in_], off), lambda e: e.tensor_scalar(ap(out), src(in_, off), val(s1), None, op0)
+        return vcost(out, [in_], off), lambda e: e.tensor_scalar(ap(out), src(in_, off), val(s1), val(s2), op0, op1)
 
-    def tt(out, a, b, op):
-        run("v", lambda e: e.tensor_tensor(ap(out), ap(a), ap(b), op), [a, b], [out])
-
-    def scan(out, d0, d1, init, op0, op1):
-        run("v", lambda e: e.tensor_tensor_scan(ap(out), ap(d0), ap(d1), val(init), op0, op1), [d0, d1, init], [out])
-
-    def turn(out, in_):
-        run("v", lambda e: e.transpose(ap(out), ap(in_)), [in_], [out])
-
-    def act(out, in_, func, bias, scale, acc=None, off=None):
-        if acc is None:
+    def act_form(out, in_, func, bias, scale, acc=None, off=None):
+        if func is AF.Copy:
+            call = lambda e: e.activation(ap(out), src(in_, off), func) if scale == 1.0 else \
+                e.activation(ap(out), src(in_, off), func, scale=scale)
+        elif acc is None:
             call = lambda e: e.activation(ap(out), src(in_, off), func, bias=val(bias), scale=scale)
         else:
             call = lambda e: e.activation(ap(out), ap(in_), func, bias=val(bias), scale=scale, accum_out=ap(acc))
-        run("s", call, [in_, bias, off], [out] + ([acc] if acc else []))
+        return scost(out, off) + (0.02 if acc else 0.0), call
 
-    def lin(out, in_, scale, bias):
-        act(out, in_, AF.Identity, bias, scale)
+    def copy(qs, out, in_, off=None, scale=1.0):
+        forms = {}
+        if "v" in qs and scale == 1.0:
+            forms["v"] = (vcost(out, [in_], off), lambda e: e.tensor_copy(ap(out), src(in_, off)))
+        elif "v" in qs:
+            forms["v"] = ts_form(out, in_, scale, None, A.mult, off=off)
+        if "s" in qs:
+            forms["s"] = act_form(out, in_, AF.Copy, 0.0, scale, off=off)
+        add(forms, [in_, off], [out])
+
+    def ts(out, in_, s1, s2, op0, op1=None, off=None):
+        add({"v": ts_form(out, in_, s1, s2, op0, op1, off)}, [in_, off, s1, s2], [out])
+
+    def tt(out, a, b, op, off=None):
+        cost = vcost(out, [a, b], off, 1.0 if is_bank(a) or is_bank(b) else 2.0)
+        add({"v": (cost, lambda e: e.tensor_tensor(ap(out), src(a, off), ap(b), op))}, [a, b, off], [out])
+
+    def scan(out, d0, d1, init, op0, op1):
+        add({"v": (vcost(out, [d0, d1]), lambda e: e.tensor_tensor_scan(ap(out), ap(d0), ap(d1), val(init), op0, op1))},
+            [d0, d1, init], [out])
+
+    def turn(out, in_):
+        add({"v": (vcost(out, [in_]), lambda e: e.transpose(ap(out), ap(in_)))}, [in_], [out])
+
+    def act(out, in_, func, bias, scale, acc=None, off=None):
+        add({"s": act_form(out, in_, func, bias, scale, acc, off)}, [in_, bias, off], [out] + ([acc] if acc else []))
+
+    def lin(out, in_, scale, bias, qs="s"):
+        forms = {"s": act_form(out, in_, AF.Identity, bias, scale), "v": ts_form(out, in_, scale, bias, A.mult, A.add)}
+        add({q: forms[q] for q in qs}, [in_, bias], [out])
 
     def fill(out, c):
-        lin(out, r("ij", 0, len(range(out[3], out[4], out[5]))), 0.0, c)
+        forms = {"v": (vcost(out, []), lambda e: e.memset(ap(out), c))}
+        if cols(out) <= 128:
+            forms["s"] = act_form(out, r("ij", 0, cols(out)), AF.Identity, c, 0.0)
+        add(forms, [r("ij")] if "s" in forms else [], [out])
 
     def iota(out, pattern, base, mult):
         if SCRATCH[out[0]][2] == I32:
             call = lambda e: e.iota(ap(out), pattern, base, mult)
         else:
             call = lambda e: e.iota(ap(out), pattern, base, mult, allow_small_or_imprecise_dtypes=True)
-        run("g", call, [], [out])
+        add({"g": (0.13 + 2 * cols(out) * CYCLE, call)}, [], [out])
 
     def quant(cq, cs, a, b, tile):
-        run("v", lambda e: e.quantize_mx(ap(r(cq, a, b)), ap(r(cs, a, b)), ap(tile)), [tile], [r(cq, a, b), r(cs, a, b)])
+        add({"v": (0.012 + 0.00022 * cols(tile), lambda e: e.quantize_mx(ap(r(cq, a, b)), ap(r(cs, a, b)), ap(tile)))},
+            [tile], [r(cq, a, b), r(cs, a, b)])
 
     def mm(bank, lq, ls, la, rq, rs_, ra, rb, start=True, stop=True):
         out = r("bk%d" % bank, 0, rb - ra)
         ins = [r(lq, la, la + 128), r(ls, la, la + 128), r(rq, ra, rb), r(rs_, ra, rb)]
-        run("t", lambda e: e.matmul_mx(ap(out), ap(ins[0]), ap(ins[1]), ap(ins[2]), ap(ins[3]), start, stop), ins, [out])
-
-    def pick_codes(out, win, off):
-        run("v", lambda e: e.tensor_copy(ap(out).bitcast(dt.uint32), ap(win).bitcast(dt.uint32).indirect(ap(off))),
-            [win, off], [out])
+        add({"t": ((rb - ra + 16) * CYCLE,
+                   lambda e: e.matmul_mx(ap(out), ap(ins[0]), ap(ins[1]), ap(ins[2]), ap(ins[3]), start, stop))}, ins, [out])
 
     shared = [e for e in range(16) if all(e in topo.engines(core, c) for c in T.cores if c != core)]
 
     def send(dst_rank, pairs, sem, apart=False):
-        dst = T.cores[dst_rank % n]
-        rid, pid, _ = topo.addr(dst)
-        total[sem] = 0
-        for i, (out, in_) in enumerate(pairs):
-            lanes = shared[i::len(pairs)] if apart else shared
-            order("g", [in_], [])
-            a, b = ap(out), ap(in_)
-            if SCRATCH[in_[0]][2] == CODES:
-                a, b = a.bitcast(dt.uint8), b.bitcast(dt.uint8)
-            total["sent"] = total.get("sent", 0) + len(lanes)
-            total[sem] += len(lanes)
-            g.remote_dma(a, b, T.sem[sem], T.sem["sent"], pid, rid, sum(1 << e for e in lanes))
-        note("far", [], [out for out, in_ in pairs], sem, total[sem])
+        rid, pid, _ = topo.addr(T.cores[dst_rank % n])
+
+        def go():
+            total[sem] = 0
+            for i, (out, in_) in enumerate(pairs):
+                lanes = shared[i::len(pairs)] if apart else shared
+                order("g", [in_], [])
+                a, b = ap(out), ap(in_)
+                if SCRATCH[in_[0]][2] == CODES:
+                    a, b = a.bitcast(dt.uint8), b.bitcast(dt.uint8)
+                total["sent"] = total.get("sent", 0) + len(lanes)
+                total[sem] += len(lanes)
+                g.remote_dma(a, b, T.sem[sem], T.sem["sent"], pid, rid, sum(1 << e for e in lanes))
+            note("far", [], [out for out, in_ in pairs], sem, total[sem])
+        calls.append(({"g": (0.2 * len(pairs), go)}, [i for o, i in pairs], [o for o, i in pairs],
+                      (FLIGHT if len(pairs) > 1 else HOP) + FIRST * apart, 0.0))
 
     def bk(b, a=0, z=128):
         return r("bk%d" % b, a, z)
@@ -219,300 +320,290 @@ def rank_program(g, core, T, topo):
     def prow(k, a, z):
         return r("pt", k * RS + a, k * RS + z)
 
+    def best(at, a=0, z=8):
+        return r("pt", a * RS + at, z * RS, RS)
+
     def cell(name, j):
         return r(name, j, j + 1)
 
-    def part(name, width, k):
-        return r(name, width * k, width * k + width)
-
+    level[0] = 0
     dma("y", T.xn[:, 0:512], T.x[:, 0:512], [], [r("xn", 0, 512)], "lx0")
     dma("s", T.xn[:, 512:1024], T.x[:, 512:1024], [], [r("xn", 512, 1024)], "lx1")
-    dma("y", T.wq[:].bitcast(dt.uint8), T.wc[:], [r("xn")], [r("wq")], "lwc")
-    dma("y", T.wsc[:], T.ws[:], [], [r("wsc")], "lws")
-    dma("y", T.vt[:], T.v[:], [], [r("vt")], "lv")
 
+    level[0] = 10 ** 6
     iota(r("ij"), [[1, 128]], 0, -1)
     for k in range(7):
         iota(cell("pi", k), [[0, 1]], 0, 1 << (6 - k))
-    iota(r("cr"), [[1, 2], [32, 8]], 0, 0)
-    run("v", lambda e: e.memset(ap(r("eb")), 0.0), [], [r("eb")])
-    ts(r("ident"), r("ij"), 0.0, None, A.is_equal)
+    fill(r("eb"), 0.0)
+    ts(r("mdiag"), r("ij"), 0.0, -BIG, A.is_equal, A.mult)
     ts(r("eb", 4, 516, 4), r("ij"), 0.0, None, A.is_equal)
-    for e in range(2):
-        for c in range(4):
-            a = 32 * c + 16 * e
-            copy("s", r("eb", 516 + 512 * e + 4 * a, 580 + 512 * e + 4 * a, 4), r("ident", a, a + 16))
-    fill(r("neg1", 0, 128), -1.0)
-    fill(r("neg1", 128, 256), -1.0)
-    fill(r("pt", 0, 8 * RS, RS), -BIG)
-    fill(cell("eqa", 0), 0.0)
-    fill(cell("eqb", 0), 0.0)
-    fill(r("ix", 8, 10), 256.0)
-    fill(r("cfl", 0, 4), 0.0)
-    fill(r("rst"), 1.0)
-    fill(r("wb", 0, 64), 0.0)
-    fill(r("ht", 512, 520), 0.0)
-    fill(r("iv1", 0, 32), 0.0)
-    fill(r("iv2", 0, 32), 0.0)
-    fill(r("rst", 0, 64, 8), 0.0)
-    copy("s", r("mdiag"), r("ident"), scale=-BIG)
     for b in range(4):
         quant("eq", "es", 128 * b, 128 * b + 128, r("eb", 4 - b, 516 - b))
-    quant("eq", "es", 512, 768, r("eb", 516, 1540))
+    for name, a, z, st, c in [
+            ("ep", K, 4 * EW, GV, 0.0),
+            ("neg1", 0, 256, 1, -1.0), ("one", 0, SW, 1, 1.0),
+            ("pt", 0, 8 * RS, RS, -BIG), ("ya", 0, 1, 1, 1.0), ("cfl", 0, 22, 1, 0.0),
+            ("rst", 0, 128, 1, 1.0), ("rst", 0, 128, 16, 0.0), ("stp", 0, 8, 1, STEP),
+            ("wb", 0, 64, 1, 0.0), ("et", 0, 128, 1, 0.0), ("pf", 8, 16, 1, 0.0), ("tb", 0, 32, 1, 0.0)]:
+        fill(r(name, a, z, st), c)
     ts(r("bi", 0, 7), r("pi", 0, 7), 6, 1, A.logical_shift_right, A.bitwise_and)
     ts(cell("bi", 7), cell("pi", 6), 15, None, A.bitwise_and)
-    quant("eq", "es", 768, 1024, r("eb", 515, 1539))
     copy("v", r("bf"), r("bi"))
-    quant("eq", "es", 1024, 1280, r("eb", 514, 1538))
+    iota(r("ii"), [[1, 128]], 0, 0)
+    iota(r("kk"), [[1, 128]], 0, 0)
+    iota(r("tab", 0, 192), [[2, 192]], -384, 0)
+    iota(r("tab", 192, 384), [[2, 192]], 0, 0)
+    iota(r("dm"), [[0, 8], [1, 16]], 0, 0)
+    ts(r("dm"), r("dm"), cell("bf", 7), None, A.is_equal)
+    iota(r("qc"), [[16, 8]], 0, 0)
+    ts(r("qc"), r("qc"), cell("bf", 7), None, A.add)
 
-    for j in range(4):
-        copy("v", r("xe", j, 512, 4), r("xn", j, 1024, 8))
-    quant("tq0", "ts0", 128, 256, r("xe"))
-    for j in range(4):
-        copy("sv"[j // 2], r("xo", j, 512, 4), r("xn", 4 + j, 1024, 8))
+    def tri(c):
+        a = 144 * c if c < 4 else 144 * (7 - c) + 16 * (8 - c)
+        return a, a + 16 * c + 16
 
-    def send_even(t):
-        tq, tsc = "tq%d" % t, "ts%d" % t
-        send(rank - 1 - t, [(r(tq, 256, 384), r(tq, 128, 256)), (r(tsc, 256, 384), r(tsc, 128, 256))], "at%d" % t, t == 0)
-
-    send_even(0)
-    iota(r("tab", 0, 256), [[1, 256]], 0, 0)
-    iota(r("tab", 256, 512), [[0, 256]], 300, 0)
-    iota(r("tab", 512, 640), [[2, 128]], 0, 0)
-    iota(r("dec1"), [[0, 1024]], -1, 0)
-    iota(r("dec1", 0, 1024, 128), [[0, 8]], 1024, 0)
-    quant("tq0", "ts0", 0, 128, r("xo"))
-    quant("eq", "es", 1280, 1536, r("eb", 513, 1537))
+    for c in range(8):
+        a, z = tri(c)
+        ts(r("wrow", a, z), r("ii", 0, z - a), cell("qc", c), -1024.0, A.is_le, A.mult)
+    fill(r("wrow", 0, TRI, 144), 2.0 ** 30)
+    fill(r("wrow", 16, TRI, 160), 2.0 ** 30)
 
     for k in range(3):
         act(cell("xr", k), cell("bf", k), AF.Abs, cell("bf", k + 4), -1.0)
-    act(cell("xr", 3), cell("bf", 3), AF.Abs, cell("bf", 4), -1.0)
     lin(cell("tm", 0), cell("bf", 5), 2.0, cell("bf", 4))
-    lin(cell("tm", 5), cell("bf", 3), -8.0, cell("bf", 7))
-    lin(cell("tm", 6), cell("bf", 7), 2.0, 0.0)
     lin(cell("tm", 1), cell("bf", 6), 4.0, cell("tm", 0))
-    lin(cell("tm", 4), cell("bf", 3), float(SW), cell("tm", 5))
+    lin(cell("tm", 2), cell("xr", 0), 64.0, cell("tm", 1))
+    lin(cell("tm", 3), cell("xr", 1), 128.0, cell("tm", 2))
+    lin(cell("cfl", 0), cell("xr", 2), 32.0, cell("tm", 3))
+    iota(r("tb", 0, 4), [[160, 4]], 15, 0)
+    iota(r("tb", 4, 8), [[-144, 4]], 575, 0)
+    copy("sv", r("tb", 16, 24), r("tb", 0, 8))
+    for h in range(2):
+        for c0 in range(2):
+            iota(r("tb", 32 + 16 * h + c0, 48 + 16 * h, 2), [[0, 2], [32, 4]], (128 + 32 * c0) * (h ^ c0) + 16 * h, 0)
+    for o in range(2):
+        iota(r("tb", 64 + o, 96, 2), [[0, 2], [1, 8]], o, 0)
+    iota(r("tb", 96, 128), [[0, 2], [RS, 2], [0, 8]], 384, 0)
+    iota(r("tb", 128, 160), [[0, 4], [16, 8]], 15, 0)
+    turn(r("tc"), r("tb"))
+    copy("sv", r("cfl", 2, 6, 2), r("tc", 0, 64, 32))
+    lin(r("cfl", 6, 9), r("ii", 0, 3), 2.0 * RS, cell("tc", 96))
+    lin(r("cfl", 10, 13), r("ii", 0, 3), 0.0, cell("tc", 128))
+    lin(r("cfl", 14, 22), r("ii", 0, 8), 0.0, cell("tc", 64))
+    copy("v", r("cu"), r("cfl"))
 
-    def more_constants():
-        lin(cell("cfl", 2), cell("xr", 3), 32.0, cell("tm", 5))
-        lin(cell("tm", 2), cell("xr", 0), 64.0, cell("tm", 1))
-        lin(r("cfl", 4, 8), r("cr", 0, 4), 2.0 * SW / 32, cell("tm", 4))
-        lin(cell("tm", 3), cell("xr", 1), 128.0, cell("tm", 2))
-        lin(r("col"), r("cr"), 1.0, cell("tm", 6))
-        lin(cell("cfl", 0), cell("xr", 2), 32.0, cell("tm", 3))
-        lin(r("cfl", 8, 12), r("cr", 0, 4), 0.0, cell("tm", 5))
-        lin(r("ncol"), r("col"), -512.0, 0.0)
+    ev, od = (0, 1, 6, 7), (2, 3, 4, 5)
+    odd = r("so", 1, 256, 2)
 
-    even_banks, odd_banks = (0, 1, 6, 7), (2, 3, 4, 5)
-
-    def odd_planes(t):
+    def planes(t, a, out):
         for b in range(4):
-            mm(2 + b, "eq", "es", 128 * b, "tq%d" % t, "ts%d" % t, 0, 128)
-        for b in range(4):
-            copy("s", r("vp", 384 * b + 1, 384 * b + 256, 2), bk(2 + b))
+            mm(od[b], "eq", "es", 128 * b, "tq%d" % t, "ts%d" % t, a, a + 128)
+            copy("s", r("vp", 384 * b + out[0], 384 * b + out[1], out[2]), bk(od[b]))
 
-    def odd_scores(t):
-        mm(5, "tq%d" % t, "ts%d" % t, 0, "tq%d" % t, "ts%d" % t, 0, 128)
-        tt(r("so", 1, 256, 2), bk(5), r("mdiag"), A.add)
+    def levels(at, data, low, parts=1):
+        wide = 128 // parts
+        for k, a in sorted(((k, a) for k in range(8) for a in range(0, 128, wide)), key=lambda s: (s[0] + s[1] // wide, s[1])):
+            cut = lambda x: r(x[0], x[3] + a * x[5], x[3] + (a + wide - 1) * x[5] + 1, x[5])
+            scan(prow(k, at + a + 1, at + a + wide + 1), cut(data), prow(k - 1, at + a, at + a + wide) if k else cut(low),
+                 prow(k, at + a, at + a + 1), A.max, A.min if k else A.max)
 
-    def plane(i):
-        b = i // 2
-        if i % 2:
-            copy("s", r("vp", 384 * b + 256, 384 * b + 384), bk(2 + b, 128, 256))
-        else:
-            copy("s", r("vp", 384 * b, 384 * b + 256, 2), bk(2 + b))
+    def odd_part(t):
+        tq, tsc = "tq%d" % t, "ts%d" % t
+        quant(tq, tsc, 0, 128, r("xo"))
+        mm(od[3], tq, tsc, 0, tq, tsc, 0, 128)
+        tt(odd, bk(od[3]), r("mdiag"), A.add)
+        bonus[0] = 0.0
+        levels(0, odd, odd)
+        planes(t, 0, (1, 256, 2))
 
-    def step(word):
-        c, k = word[0], int(word[1])
-        own = c.islower()
-        sco, wd, at = (r("so"), 256, 256) if own else (r("sc"), SW, 384)
-        sg, na, ca, eq, oo = ("sg", "na", "ca", "eqa", "oa") if own else ("sh", "nb", "cb", "eqb", "ob")
-        odd = r("so", 1, 256, 2)
-        if c == "u":
-            scan(prow(k, 1, 129), odd, prow(k - 1, 0, 128) if k else odd, -BIG, A.max, A.min if k else A.max)
-        elif c == "v":
-            scan(prow(k, 129, 257), bk(0), prow(k - 1, 128, 256) if k else odd, prow(k, 128, 129),
-                 A.max, A.min if k else A.max)
-        elif c == "B":
-            scan(prow(k, 257, 385), bk(1), prow(k - 1, 256, 384) if k else r("so", 0, 128), prow(k, 256, 257),
-                 A.max, A.min if k else A.max)
-        elif c in "sS":
-            act(part(sg, wd, k), sco, AF.Sign, prow(k, at, at + 1), -1.0)
-        elif c in "mM":
-            if ("s%d" if own else "S%d") % k in FIRST + SECOND:
-                act(part(na, wd, k), part(sg, wd, k), AF.Abs, 0.0, 1.0)
-            else:
-                ts(part(na, wd, k), sco, prow(k, at, at + 1), None, A.not_equal)
-        elif c in "lL":
-            scan(part(ca, wd, k), part(na, wd, k), r("neg1", 0, wd), cell(oo, k), A.add, A.add)
-        elif c in "kK":
-            act(part("ca" if own else "jb", wd, k), part(ca, wd, k), AF.Sign, 0.5, 1.0, cell("aa" if own else "ab", k))
-        elif c in "tT":
-            a, z = max(4 * k, 1), 4 * k + 4
-            tt(r(eq, a, z), r("pt", a * RS + at, z * RS, RS), r("pt", (a - 1) * RS + at, (z - 1) * RS, RS), A.is_equal)
-        elif c in "rR":
-            a, z = 4 * k, 4 * k + 4
-            scan(r(oo, a, z), r(eq, a, z), r(eq, a, z), cell(oo, a - 1) if a else 0.0, A.mult, A.add)
-        elif c == "p":
-            plane(k)
-        elif k == 1:
-            copy("s", r("sc", 0, 8), r("pt", 256, 8 * RS, RS))
-        elif k == 2:
-            copy("v", r("sc", 8, SW), bk(1))
-        elif k == 3:
-            lin(r("ix", 0, 8), r("aa"), 0.5, 128.0)
-        elif k == 4:
-            tt(r("dd"), r("ix", 1, 9), r("ix", 0, 8), A.subtract)
-        elif k == 5:
-            act(r("dr"), r("dd"), AF.Identity, -1.0, 1.0, off=r("cu", 8, 12))
-        else:
-            ts(r("zs"), r("cb"), 0.0, -2.0, A.is_lt, A.mult, off=r("cu", 4, 8))
+    def even_part(t):
+        tq, tsc = "tq%d" % t, "ts%d" % t
+        quant(tq, tsc, 128, 256, r("xe"))
+        send(rank - 1 - t, [(r(tq, 256, 384), r(tq, 128, 256)), (r(tsc, 256, 384), r(tsc, 128, 256))], "at%d" % t, t == 0)
+
+    level[0] = 1
+    for j in range(4):
+        copy("vs", r("xe", j, 512, 4), r("xn", j, 1024, 8))
+    even_part(0)
+    level[0] = 2
+    for j in range(4):
+        copy("vs", r("xo", j, 512, 4), r("xn", 4 + j, 1024, 8))
+    odd_part(0)
 
     for t in range(R):
         tq, tsc, hq, hs = "tq%d" % t, "ts%d" % t, "hq%d" % t, "hs%d" % t
-        pq, ps, of, ol = "pq%d" % t, "ps%d" % t, "of%d" % t, "ol%d" % t
+        of = "of%d" % t
         last = t == R - 1
 
-        if t == 0:
-            odd_scores(0)
-        mm(0, tq, tsc, 0, tq, tsc, 128, 256)
-        mm(6, tq, tsc, 0, tq, tsc, 128, 256)
-        copy("s", r("so", 0, 256, 2), bk(6))
-        if t == 0:
-            more_constants()
-        for i, word in enumerate(FIRST):
-            step(word)
-            if t == 0 and i == 20:
-                copy("v", r("cu"), r("cfl"))
-        if t == 0:
-            odd_planes(0)
+        def now(u):
+            level[0] = 100 * t + u
 
-        mm(1, tq, tsc, 0, tq, tsc, 256, 384)
-        for b in range(4):
-            mm(2 + b, "eq", "es", 128 * b, tq, tsc, 128, 384)
-        for word in SECOND:
-            step(word)
-        tt(r("zp"), r("zs"), r("dr"), A.mult)
-        scan(r("zg"), r("rst"), r("zp"), 0.0, A.mult, A.add)
-        tt(r("wb", 0, 8), r("zg", 7, 64, 8), r("ab"), A.add)
+        now(19)
+        iota(r("win", 0, 432), [[0, 216], [-GV, 2]], GV + K, 0)
 
+        now(10)
+        mm(ev[0], tq, tsc, 0, tq, tsc, 128, 256)
+        mm(ev[1], tq, tsc, 0, tq, tsc, 128, 256)
+        copy("s", r("so", 0, 256, 2), bk(ev[1]))
+        levels(128, bk(ev[0]), odd, HALVES)
+        edge = prow(7, 256, 257)
+        tt(r("ya", 1, 8), best(256, 1, 8), best(256, 0, 7), A.not_equal)
+        ts(r("xg"), r("so"), edge, STEP, A.is_le, A.max)
+        act(r("sg"), r("so"), AF.Sign, edge, -1.0)
+        scan(r("ta"), r("ya"), r("stp"), 1.0, A.max, A.mult)
+        scan(r("ma"), r("xg"), r("neg1"), cell("ta", 7), A.mult, A.max)
+        ts(r("xh"), r("sg"), STEP, None, A.max)
+        scan(r("mb"), r("xh"), r("ma"), 1.0, A.mult, A.max)
+        for j in range(4):
+            part = r("junk", 256 * j, 256 * j + 256)
+            if j in BY_SCAN:
+                ts(part, r("mb"), STEP ** -(2 * j + 1), 4097.0, A.mult, A.min)
+                scan(r("sums", 256 * j, 256 * j + 256), r("neg1"), part, 4098.0 * 256, A.add, A.subtract)
+            else:
+                act(part, r("mb"), AF.Relu, 4097.0, -STEP ** -(2 * j + 1), cell("sums", 256 * j + 255))
+        sums = r("sums", 255, 1024, 256)
+        ts(r("wi", 0, 4), sums, -1.0, 4097.0 * 256, A.mult, A.add)
+        ts(r("pu", 0, 8, 2), sums, -1.0 / 4096, 4097.0 / 16, A.mult, A.add)
+        ts(r("wi", 4, 8), r("wi", 0, 4), 4095, None, A.bitwise_and)
+        copy("v", r("pu", 1, 8, 2), r("wi", 4, 8))
+        tt(r("gv"), r("so"), r("dm"), A.mult, off=r("pu"))
+        scan(r("vv"), r("rst"), r("gv"), 0.0, A.mult, A.add)
+        ts(r("pf", 0, 8), r("pu"), 1.0 / 256, -1.0, A.mult, A.add)
+        copy("s", r("pr"), r("pf"), off=r("cu", 14, 22))
+        now(17)
+        planes(t, 128, (0, 256, 2))
+
+        now(11)
+        if t == 0:
+            dma("y", T.wq[:].bitcast(dt.uint8), T.wc[:], [r(tq, 256, 384)], [r("wq")], "lwc")
+            dma("y", T.wsc[:], T.ws[:], [r(tq, 256, 384)], [r("wsc")], "lws")
+            dma("y", T.vt[:], T.v[:], [r("wq")], [r("vt")], "lv", 4 * LOAD)
+        mm(ev[2], tq, tsc, 0, tq, tsc, 256, 384)
+        mm(ev[3], tq, tsc, 0, tq, tsc, 256, 384)
+        copy("s", r("sc", 0, 8), best(256))
+        copy("s", r("sc", 8, SW), bk(ev[3]))
+        levels(256, bk(ev[2]), r("so", 0, 128))
+        for a, z in TIES:
+            if z - a > 1:
+                tt(r("eqb", a, z), best(384, a, z), best(384, a - 1, z - 1), A.is_equal)
+                scan(r("et", 16 * a, 16 * z, 16), r("neg1", a, z), r("eqb", a, z), cell("et", 16 * a - 16), A.add, A.mult)
+            else:
+                lin(cell("zc", a), cell("et", 16 * a - 16), 1.0, -1.0, "sv")
+                ts(cell("et", 16 * a), best(384, a, z), best(384, a - 1, a), cell("zc", a), A.is_equal, A.mult)
+        for k in range(8):
+            bonus[0] = LEAD * (7 - k)
+            top = prow(k, 384, 385)
+            row = lambda name, a=0: r(name, SW * k + a, SW * k + SW)
+            if k in BY_SIGN:
+                act(row("sh"), r("sc"), AF.Sign, top, -1.0)
+                act(row("nb"), row("sh"), AF.Abs, 0.0, 1.0)
+            else:
+                ts(row("nb"), r("sc"), top, None, A.not_equal)
+            scan(row("cb"), r("one"), row("nb"), cell("et", 16 * k), A.add, A.subtract)
+            act(r("jb", 128 * k, 128 * k + 128), row("cb", 8), AF.Sign, 0.5, -1.0, cell("ab", k))
+        bonus[0] = 0.0
+        lin(r("ac"), r("ab"), 1.0 / 512, 0.5)
+        copy("s", r("vr"), r("pt", 0, 6 * RS), off=r("cu", 6, 9))
+        tt(r("et", 1, 96, 2), r("vv"), r("vr"), A.is_equal, off=r("cu", 10, 13))
+        for k in (6, 7):
+            ts(r("et", 16 * k + 1, 16 * k + 16, 2), r("vv", 15, 128, 16), prow(k, 384, 385), None, A.is_equal)
+        scan(r("yy"), r("rst"), r("et"), 0.0, A.mult, A.subtract)
+        scan(r("zz"), r("yy"), r("pr"), 0.0, A.max, A.min)
+        tt(r("wb", 0, 8), r("zz", 15, 128, 16), r("ac"), A.add)
+        now(18)
+        planes(t, 256, (256, 384, 1))
+
+        now(14)
         turn(r("yb", 0, 32), r("wb", 0, 32))
         turn(r("yb", 32, 64), r("wb", 0, 32))
-        plane(2)
-        plane(3)
-        copy("s", r("wb", 32, 40, p1=64), r("wb", 0, 8, p0=64))
-        copy("s", r("wb", 32, 40, p0=64), r("wb", 0, 8, p1=64))
+        copy("sv", r("wb", 32, 40, p1=64), r("wb", 0, 8, p0=64))
+        copy("sv", r("wb", 32, 40, p0=64), r("wb", 0, 8, p1=64))
         turn(r("wb", 96, 128, p1=64), r("yb", 16, 48, p0=64))
         turn(r("wb", 96, 128, p0=64), r("yb", 16, 48, p1=64))
         turn(r("wb", 64, 96), r("yb", 16, 48))
-        plane(4)
-        plane(5)
         for q in range(4):
             o = q ^ 1
-            copy("vs"[q % 2], r("wb", 128, 232, p0=32 * q, p1=32 * q + 32), r("wb", 0, 104, p0=32 * o, p1=32 * o + 32))
-        ts(r(of), r("wb"), float(496 + SW), 0.5, A.add, A.mult, off=cell("cu", 0))
-        plane(6)
-        plane(7)
-        send(rank + 1 + t, [(r(ol), r(of, 0, 8))], "al%d" % t)
+            copy("svvv"[q], r("wb", 128, 232, p0=32 * q, p1=32 * q + 32), r("wb", 0, 104, p0=32 * o, p1=32 * o + 32))
+        ts(r(of), r("wb"), 256.0, 192.0, A.mult, A.add, off=cell("cu", 0))
 
+        now(22)
         for b in range(4):
-            copy("vvss"[b], r("zt", b, 512, 4), r("vp", 384 * b, 384 * b + 384), off=r(of, 0, 8))
+            copy("vs", r("zt", b, 512, 4), r("vp", 384 * b, 384 * b + 384), off=r(of, 0, 8))
         quant("zq", "zsc", 0, 128, r("zt"))
-        copy("s", r("lb", 0, 128), r("tab", 0, 384), off=r(of, 0, 8))
         for b in range(4):
-            mm(2 + b, "wq", "wsc", 128 * b, "zq", "zsc", 0, 128)
-        for b in range(4):
-            mm(even_banks[b], "eq", "es", 128 * b, tq, tsc, 128, 256, True, False)
+            mm(od[b], "wq", "wsc", 128 * b, "zq", "zsc", 0, 128)
+            copy("vs", r("ht", b, 512, 4), bk(od[b]), scale=0.03125)
+        quant(hq, hs, 0, 128, r("ht"))
+        send(rank + 1 + t, [(r(hq, 128, 256), r(hq, 0, 128)), (r(hs, 128, 256), r(hs, 0, 128))], "ah%d" % t)
 
-        def row(q, name, j, cj, giver=0):
-            out = r(name, 128 * j, 128 * j + 128)
-            lst = r("lb", 128 * giver, 128 * giver + 128)
-            if q == "v":
-                ts(out, lst, cell("col", cj), 512.0, A.not_equal, A.mult)
+        now(21)
+        copy("s", r("lb"), r("tab"), off=r(of, 0, 8))
+        now(LIST)
+        copy("s", r("me"), r("wb"), off=cell("cu", 0), scale=512.0)
+        copy("s", r("nme"), r("wb"), off=cell("cu", 0), scale=-2.0 ** 27)
+        for c in range(7, -1, -1):
+            a, z = tri(c)
+            out, lst = r("dd", a, z), r("lb", 0, z - a)
+            if c in ROWS_S:
+                act(out, lst, AF.Abs, cell("nme", c), 2.0 ** 18)
             else:
-                act(out, lst, AF.Abs, cell("ncol", cj), 512.0)
+                ts(out, lst, cell("me", c), 2.0 ** 19, A.not_equal, A.mult)
+        scan(r("du"), r("wrow"), r("dd"), 0.0, A.add, A.min)
+        tt(r("da"), r("du"), r("me"), A.subtract, off=cell("cu", 2))
+        ts(r("sf"), r("da"), -0.5, 224.0, A.mult, A.add)
+        add({"v": (0.05 + 3.5 * 128 * CYCLE, lambda e: e.tensor_copy(ap(r("win")).indirect(ap(r("sf", 0, 8))), ap(r("kk"))))},
+            [r("kk"), r("sf", 0, 8)], [r("win")])
 
-        for j in range(5):
-            row("v", "d1", j, 8 + j)
-        for b in range(4):
-            copy("svvs"[b], r("ht", b, 512, 4), bk(2 + b), scale=0.03125)
-        for j in range(5, 8):
-            row("v", "d1", j, 8 + j)
-        quant(hq, hs, 0, 130, r("ht"))
-        send(rank + 1 + t, [(r(hq, GV, GV + 130), r(hq, 0, 130)), (r(hs, GV, GV + 130), r(hs, 0, 130))], "ah%d" % t)
-        for b in range(4):
-            mm(odd_banks[b], "eq", "es", 128 * b, tq, tsc, 0, 128, True, False)
+        def inverse(name, a, st):
+            turn(r(name, 0, 128), r("win", a, a + 128 * st, st))
+            turn(r(name, 128, 288), r("win", a - 16 * st, a + 144 * st, st))
 
-        def add_picks(banks, a):
-            for e in range(2):
-                for b in range(4):
-                    mm(banks[b], "eq", "es", 512 + 256 * b + 128 * e, pq, ps, a + 128 * e, a + 128 * e + 128, False, e == 1)
-
-        def state(q, banks, b, odd):
-            if last:
-                copy(q, r("xl", 4 * odd + b, 1024, 8), bk(banks[b]))
-            else:
-                copy(q, r("xo" if odd else "xe", b, 512, 4), bk(banks[b]))
-
+        inverse("rp", 288, 1)
+        copy("vs", r("gl%d" % t), r("rp"), off=cell("cu", 4))
+        send(rank + 1 + t, [(r("gr%d" % t), r("gl%d" % t, 0, 8))], "al%d" % t)
+        bonus[0] = ODD
+        inverse("ro", 33, 2)
+        copy("v", r("f1"), r("ro"), off=cell("cu", 4))
+        bonus[0] = 0.0
+        inverse("rv", 32, 2)
+        act(r("fe"), r("rv"), AF.Identity, float(-GV), 1.0, off=cell("cu", 4))
         if last:
-            lin(r("opt"), r("yb", 0, 32), 0.5, (496 + SW) / 2)
+            now(40)
+            lin(r("opt"), r("yb", 0, 32), 256.0, 192.0)
             for a in range(4):
                 dma("y", T.op[:, 32 * a:32 * a + 32], T.opt[32 * a:32 * a + 8, :], [r("opt")], [], "outs")
-        for j in range(5):
-            row("s", "d2", j, j)
-        scan(r("u1"), r("dec1"), r("d1"), 0.0, A.add, A.min)
-        for j in (5, 6, 7):
-            row("v", "d2", j, j)
-        copy("v", r("iv1", 0, 8), r("u1", 127, 1024, 128))
-        turn(r("y1", 0, 32), r("iv1", 0, 32))
-        turn(r("y1", 32, 64), r("iv1", 0, 32))
-        scan(r("u2", 0, 512), r("dec1", 0, 512), r("d2", 0, 512), 0.0, A.add, A.min)
-        turn(r("iv1", 32, 64), r("y1", 16, 48))
-        scan(r("u2", 512, 1024), r("dec1", 0, 512), r("d2", 512, 1024), 0.0, A.add, A.min)
-        ts(r("f1"), r("iv1"), 127.0, 128.0, A.add, A.min, off=cell("cu", 2))
-        copy("s", r("lb", 128, 256), r("tab", 256, 640), off=r(ol))
-        for j in range(8):
-            row("s", "d2", 8 + j, j, 1)
-        ts(r("iv0"), r("u2", 127, 1024, 128), float(-GV), None, A.add)
-        pick_codes(r(pq, 256, 512), r(hq, 0, 130), r("f1"))
-        copy("s", r(ps, 256, 512), r(hs, 0, 130), off=r("f1"))
-        add_picks(odd_banks, 256)
-        scan(r("u2", 1024, 2048), r("dec1"), r("d2", 1024, 2048), 0.0, A.add, A.min)
-        tt(r("iv2", 0, 8), r("u2", 1024 + 127, 2048, 128), r("iv0"), A.min)
-        turn(r("y2", 0, 32), r("iv2", 0, 32))
-        turn(r("y2", 32, 64), r("iv2", 0, 32))
-        turn(r("iv2", 32, 64), r("y2", 16, 48))
-        ts(r("f2"), r("iv2"), float(GV + 127), float(GV + 128), A.add, A.min, off=cell("cu", 2))
-        for b in range(4):
-            state("s", odd_banks, b, 1)
-        for e in range(2):
-            pick_codes(r(pq, 128 * e, 128 * e + 128), r(hq, 0, GV + 130), r("f2", 8 * e, 8 * e + 8))
-            copy("s", r(ps, 128 * e, 128 * e + 128), r(hs, 0, GV + 130), off=r("f2", 8 * e, 8 * e + 8))
-        add_picks(even_banks, 0)
-        if last:
             quant("vq", "vs", 0, 128, r("vt"))
-        else:
-            quant("tq%d" % (t + 1), "ts%d" % (t + 1), 0, 128, r("xo"))
-        for b in range(4):
-            state("svvs"[b], even_banks, b, 0)
-        if not last:
-            odd_scores(t + 1)
-            odd_planes(t + 1)
-            quant("tq%d" % (t + 1), "ts%d" % (t + 1), 128, 256, r("xe"))
-            send_even(t + 1)
+
+        for a, banks, lst, tile in ((1, od, "f1", "xo"), (0, ev, "f2", "xe")):
+            bonus[0] = ODD * a
+            for b in range(4):
+                mm(banks[b], "eq", "es", 128 * b, hq, hs, 128 - 128 * a, 256 - 128 * a)
+                copy("sv", r("ep", EW * b + GV - GV * a, EW * b + GV - GV * a + 128), bk(banks[b]))
+            now(32 if a else 30)
+            if not a:
+                tt(r("fm"), r("fe", 0, 8), r("gr%d" % t), A.min)
+                ts(r("f2"), r("fm"), float(GV), None, A.add)
+            for b in range(4):
+                tt(r("xl", 4 * a + b, 1024, 8) if last else r(tile, b, 512, 4), r("ep", EW * b, EW * b + (GV if a else EW)),
+                   r("vp", 384 * b + a, 384 * b + 256, 2), A.add, off=r(lst, 0, 8))
+            if not last:
+                (odd_part if a else even_part)(t + 1)
 
     quant("lq", "ls", 0, 256, r("xl"))
     mm(2, "vq", "vs", 0, "lq", "ls", 0, 128)
     mm(3, "vq", "vs", 0, "lq", "ls", 128, 256)
     dma("y", T.oc[:], T.lq[:].bitcast(dt.uint8), [r("lq")], [], "outs")
-    for k in range(2):
-        dma("s", T.osc[4 * k:4 * k + 4, :], T.ls[32 * k:32 * k + 4, :], [r("ls")], [], "outs")
+    for k in range(4):
+        dma("sy"[k // 2], T.osc[4 * k:4 * k + 4, :], T.ls[32 * k:32 * k + 4, :], [r("ls")], [], "outs")
     copy("v", r("yt", 0, 128), bk(2))
     copy("s", r("yt", 128, 256), bk(3))
-    for k in range(2, 4):
-        dma("y", T.osc[4 * k:4 * k + 4, :], T.ls[32 * k:32 * k + 4, :], [r("ls")], [], "outs")
     dma("y", T.y[:, 0:128], T.yt[:, 0:128], [r("yt", 0, 128)], [], "outs")
     dma("s", T.y[:, 128:256], T.yt[:, 128:256], [r("yt", 128, 256)], [], "outs")
+
+    if not PLAN:
+        PLAN.extend(arrange(calls))
+    for i, q in PLAN:
+        calls[i][0][q][1]()
     for sem, cnt in total.items():
         if known["g"].get(sem, 0) < cnt:
             g.wait_ge(T.sem[sem], cnt)

@@ -6,17 +6,18 @@ RS = 385
 SW = 136
 GV, EW = 144, 288
 STEP = 2.0 ** -13
-TRI = 576
 CODES, U8 = "float8_e4m3fn_x4", "uint8"
 F32, BF16, I32, U16 = "float32", "bfloat16", "int32", "uint16"
-CYCLE, WAKE, LOAD, FLIGHT, HOP = 0.83e-3, 0.175, 2.0, 2.2, 1.6
-FIX, FIRST, ODD = 0.05, 1.5, 0.0
-SLACK, SPARE = 0.1, {"v": 0.1}
-BY_SIGN = (0, 1, 2, 3)
-BY_SCAN = ()
-ROWS_S = (0, 1, 2, 3)
-TIES = ((1, 4), (4, 7), (7, 8))
-HALVES, LIST, LEAD = 1, 23, 0.0
+CYCLE, WAKE, LOAD, FLIGHT, HOP = 0.83e-3, 0.175, 2.0, 2.1, 1.0
+FIX, FIRST, ODD, AHEAD = 0.05, 1.2, 0.5, 2.1
+LATE, LEAD = 4, 0.05
+RULES = [(own, weight, slack, spare) for own in (0.0, 0.5, 1.0) for weight in (0.6, 1.0, 1.6)
+         for slack in (0.06, 0.08, 0.1, 0.12) for spare in (0.1, 0.15)]
+MARK, SUMS, PICK, HT, EP = 0.0, 0.0, 0.0, "svss", "ssss"
+BY_SIGN = (1, 2, 3)
+CUT, HALVES, QUICK = (2, 2, 2), 1, 0
+ROWS = [["vs"] * 8, ["vs"] * 8, ["vs"] * 8]
+TIES = ((1, 7), (7, 8))
 
 SCRATCH = {}
 PLAN = []
@@ -31,21 +32,19 @@ for _n, _c, _d in [
     ("vq", 128, CODES), ("vs", 128, U8), ("wq", 512, CODES), ("wsc", 512, U8),
     ("lq", 256, CODES), ("ls", 256, U8), ("yt", 256, F32), ("opt", 32, F32),
     ("eb", 516, BF16), ("eq", 512, CODES), ("es", 512, U8),
-    ("ij", 128, F32), ("ii", 128, F32), ("pi", 8, I32), ("bi", 8, I32), ("bf", 8, F32),
-    ("xr", 4, F32), ("tm", 8, F32), ("qc", 8, F32), ("tb", 160, F32), ("tc", 160, F32),
-    ("mdiag", 128, F32), ("neg1", 256, BF16), ("one", SW, BF16), ("cfl", 22, F32), ("cu", 22, U16),
-    ("tab", 384, BF16), ("kk", 128, BF16), ("dm", 128, F32), ("rst", 128, BF16), ("stp", 8, BF16),
-    ("vr", 48, F32), ("ac", 8, F32), ("nme", 16, F32),
-    ("wrow", TRI, BF16),
+    ("ij", 128, F32), ("ii", 8, F32), ("pi", 8, I32), ("bi", 8, I32), ("bf", 8, F32),
+    ("xr", 4, F32), ("tm", 8, F32), ("qc", 8, F32), ("tb", 96, F32), ("tc", 96, F32),
+    ("mdiag", 128, F32), ("neg1", 256, BF16), ("one", SW, BF16), ("cfl", 18, F32), ("cu", 18, U16),
+    ("tab", 384, BF16), ("dm", 128, F32), ("rst", 128, BF16), ("stp", 8, BF16),
+    ("dec", 1024 // min(CUT), BF16), ("col", 24, BF16), ("ncol", 24, F32),
     ("so", 256, F32), ("pt", 8 * RS, F32), ("xg", 256, BF16), ("xh", 256, BF16), ("ma", 256, BF16), ("mb", 256, BF16),
-    ("ya", 8, F32), ("ta", 8, F32), ("junk", 1024, F32), ("sums", 1024, F32), ("wi", 8, I32), ("pu", 8, U16),
-    ("gv", 128, F32), ("vv", 128, F32), ("pf", 16, BF16), ("pr", 128, BF16),
+    ("ya", 8, F32), ("ta", 8, F32), ("junk", 1024, F32), ("sums", 4, F32), ("wi", 8, I32), ("pu", 8, U16),
+    ("gv", 128, F32), ("vv", 128, F32), ("pf", 16, BF16), ("pr", 128, BF16), ("vr", 64, F32),
     ("sg", 256, BF16), ("sc", SW, F32), ("sh", 8 * SW, BF16), ("nb", 8 * SW, BF16), ("cb", 8 * SW, BF16), ("jb", 1024, BF16),
-    ("eqb", 8, F32), ("zc", 8, F32), ("et", 128, BF16), ("yy", 128, BF16), ("zz", 128, BF16), ("ab", 8, F32),
+    ("eqb", 8, F32), ("zc", 8, F32), ("wv", 8, BF16), ("ab", 8, F32), ("et", 128, BF16), ("yy", 128, BF16), ("zz", 512, BF16),
     ("wb", 232, BF16), ("yb", 64, BF16), ("vp", 1536, BF16), ("zt", 512, BF16), ("zq", 128, CODES), ("zsc", 128, U8),
-    ("ht", 512, BF16), ("lb", 128, BF16), ("me", 16, BF16), ("dd", TRI, BF16), ("du", TRI, BF16),
-    ("da", 16, F32), ("sf", 16, U16), ("win", 65536, BF16), ("ro", 288, BF16), ("rv", 288, BF16), ("rp", 288, BF16),
-    ("fe", 16, BF16), ("fm", 8, F32), ("f1", 16, U16), ("f2", 8, U16), ("ep", 4 * EW, BF16),
+    ("ht", 512, BF16), ("lb", 128, BF16), ("lg", 128, BF16), ("d1", 3072, BF16), ("u1", 3072, BF16),
+    ("fe", 8, F32), ("fm", 8, F32), ("f1", 8, U16), ("f2", 8, U16), ("ep", 4 * EW, BF16),
 ]:
     _sb(_n, _c, _d)
 for _t in range(R):
@@ -54,12 +53,11 @@ for _t in range(R):
     _sb("hq%d" % _t, 256, CODES)
     _sb("hs%d" % _t, 256, U8)
     _sb("of%d" % _t, 16, U16)
-    _sb("gl%d" % _t, 16, BF16)
-    _sb("gr%d" % _t, 8, BF16)
+    _sb("ol%d" % _t, 8, U16)
 for _b in range(8):
     SCRATCH["bk%d" % _b] = ("psum", [128, 512], F32)
 
-SEMAPHORES = ["cv", "cs", "ct", "cg", "lx0", "lx1", "lv", "lwc", "lws", "sent", "outs"] + \
+SEMAPHORES = ["cv", "cs", "ct", "cg", "lx", "lv", "lwc", "lws", "sent", "outs"] + \
     ["%s%d" % (_k, _t) for _k in ("at", "al", "ah") for _t in range(R)]
 
 A = AluOpType
@@ -91,7 +89,7 @@ def meet(a, b):
 
 def arrange(calls):
     before, after, seen = [], [[] for c in calls], {}
-    for i, (forms, reads, writes, delay, urgency) in enumerate(calls):
+    for i, (forms, reads, writes, delay, extra) in enumerate(calls):
         deps = {}
         for regs, wr in ((reads, False), (writes, True)):
             for x in regs:
@@ -112,35 +110,39 @@ def arrange(calls):
     for i in range(len(calls) - 1, -1, -1):
         forms, reads, writes, delay, extra = calls[i]
         way[i] = min(c for c, f in forms.values()) + max([way[j] + before[j][i] for j in after[i]] + [delay])
-    urgent = [-w - c[4] for w, c in zip(way, calls)]
-    got, free = {}, {q: 0.0 for q in "vstgy"}
-    left = [len(deps) for deps in before]
-    ready = {i: 0.0 for i in range(len(calls)) if not left[i]}
-    while ready:
-        q = min(free, key=free.get)
-        now = free[q]
 
-        def fits(i):
-            forms = calls[i][0]
-            return q in forms and all(max(now, ready[i]) + forms[q][0] + SPARE.get(q, 0.0) <=
-                                      max(free[o], ready[i]) + forms[o][0] + SPARE.get(o, 0.0) for o in forms)
-        mine = sorted((i for i in ready if fits(i)), key=lambda i: (urgent[i], i))
-        until, chosen = float("inf"), None
-        for i in mine:
-            if ready[i] <= now and now + calls[i][0][q][0] <= until:
-                chosen = i
-                break
-            until = min(until, ready[i] + SLACK)
-        if chosen is None:
-            free[q] = min([ready[i] for i in mine if ready[i] > now] + [t for t in free.values() if t > now] + [now + 0.05])
-            continue
-        free[q] = now + calls[chosen][0][q][0]
-        got[chosen] = (now, free[q], q)
-        del ready[chosen]
-        for j in after[chosen]:
-            left[j] -= 1
-            if not left[j]:
-                ready[j] = max(got[k][1] + gap for k, gap in before[j].items())
+    def place(own, weight, slack, spare):
+        urgent = [own * min(x for x, f in c[0].values()) - w - weight * c[4] for w, c in zip(way, calls)]
+        got, free = {}, {q: 0.0 for q in "vstgy"}
+        left = [len(deps) for deps in before]
+        ready = {i: 0.0 for i in range(len(calls)) if not left[i]}
+        while ready:
+            q = min(free, key=free.get)
+            now = free[q]
+
+            def fits(i):
+                ends = {o: max(free[o], ready[i]) + c + spare * (o == "v") for o, (c, f) in calls[i][0].items()}
+                return q in ends and ends[q] <= min(ends.values())
+            mine = sorted((i for i in ready if fits(i)), key=lambda i: (urgent[i], i))
+            until, chosen = float("inf"), None
+            for i in mine:
+                if ready[i] <= now and now + calls[i][0][q][0] <= until:
+                    chosen = i
+                    break
+                until = min(until, ready[i] + slack)
+            if chosen is None:
+                free[q] = min([ready[i] for i in mine if ready[i] > now] + [t for t in free.values() if t > now] + [now + 0.05])
+                continue
+            free[q] = now + calls[chosen][0][q][0]
+            got[chosen] = (now, free[q], q)
+            del ready[chosen]
+            for j in after[chosen]:
+                left[j] -= 1
+                if not left[j]:
+                    ready[j] = max(got[k][1] + gap for k, gap in before[j].items())
+        return max(got[i][1] + calls[i][3] for i in got), got
+
+    end, got = min((place(*rule) for rule in RULES), key=lambda x: x[0])
     return [(i, got[i][2]) for i in sorted(got, key=lambda i: (got[i][0], i))]
 
 
@@ -156,7 +158,6 @@ def rank_program(g, core, T, topo):
     touched = {}
     calls = []
     bonus = [0.0]
-    level = [10 ** 6]
 
     def ap(x):
         if x[5] == 1:
@@ -216,7 +217,7 @@ def rank_program(g, core, T, topo):
 
     def vcost(out, ins, off=None, rate=None):
         if off is not None:
-            return 0.05 + 1.5 * 16 * cols(off) * CYCLE
+            return FIX + 1.5 * 16 * cols(off) * CYCLE
         sides = [x for x in [out] + ins if isinstance(x, tuple)]
         if rate is None:
             rate = 0.5 if all(WIDTH[SCRATCH[x[0]][2]] == 2 for x in sides) else 1.0
@@ -240,7 +241,7 @@ def rank_program(g, core, T, topo):
             call = lambda e: e.activation(ap(out), ap(in_), func, bias=val(bias), scale=scale, accum_out=ap(acc))
         return scost(out, off) + (0.02 if acc else 0.0), call
 
-    def copy(qs, out, in_, off=None, scale=1.0):
+    def copy(qs, out, in_, off=None, scale=1.0, also=()):
         forms = {}
         if "v" in qs and scale == 1.0:
             forms["v"] = (vcost(out, [in_], off), lambda e: e.tensor_copy(ap(out), src(in_, off)))
@@ -248,7 +249,7 @@ def rank_program(g, core, T, topo):
             forms["v"] = ts_form(out, in_, scale, None, A.mult, off=off)
         if "s" in qs:
             forms["s"] = act_form(out, in_, AF.Copy, 0.0, scale, off=off)
-        add(forms, [in_, off], [out])
+        add(forms, [in_, off] + list(also), [out])
 
     def ts(out, in_, s1, s2, op0, op1=None, off=None):
         add({"v": ts_form(out, in_, s1, s2, op0, op1, off)}, [in_, off, s1, s2], [out])
@@ -288,11 +289,11 @@ def rank_program(g, core, T, topo):
         add({"v": (0.012 + 0.00022 * cols(tile), lambda e: e.quantize_mx(ap(r(cq, a, b)), ap(r(cs, a, b)), ap(tile)))},
             [tile], [r(cq, a, b), r(cs, a, b)])
 
-    def mm(bank, lq, ls, la, rq, rs_, ra, rb, start=True, stop=True):
+    def mm(bank, lq, ls, la, rq, rs_, ra, rb):
         out = r("bk%d" % bank, 0, rb - ra)
         ins = [r(lq, la, la + 128), r(ls, la, la + 128), r(rq, ra, rb), r(rs_, ra, rb)]
         add({"t": ((rb - ra + 16) * CYCLE,
-                   lambda e: e.matmul_mx(ap(out), ap(ins[0]), ap(ins[1]), ap(ins[2]), ap(ins[3]), start, stop))}, ins, [out])
+                   lambda e: e.matmul_mx(ap(out), ap(ins[0]), ap(ins[1]), ap(ins[2]), ap(ins[3]), True, True))}, ins, [out])
 
     shared = [e for e in range(16) if all(e in topo.engines(core, c) for c in T.cores if c != core)]
 
@@ -312,7 +313,7 @@ def rank_program(g, core, T, topo):
                 g.remote_dma(a, b, T.sem[sem], T.sem["sent"], pid, rid, sum(1 << e for e in lanes))
             note("far", [], [out for out, in_ in pairs], sem, total[sem])
         calls.append(({"g": (0.2 * len(pairs), go)}, [i for o, i in pairs], [o for o, i in pairs],
-                      (FLIGHT if len(pairs) > 1 else HOP) + FIRST * apart, 0.0))
+                      {"at": AHEAD, "ah": FLIGHT, "al": HOP}[sem[:2]] + FIRST * apart, 0.0))
 
     def bk(b, a=0, z=128):
         return r("bk%d" % b, a, z)
@@ -326,11 +327,8 @@ def rank_program(g, core, T, topo):
     def cell(name, j):
         return r(name, j, j + 1)
 
-    level[0] = 0
-    dma("y", T.xn[:, 0:512], T.x[:, 0:512], [], [r("xn", 0, 512)], "lx0")
-    dma("s", T.xn[:, 512:1024], T.x[:, 512:1024], [], [r("xn", 512, 1024)], "lx1")
+    dma("y", T.xn[:], T.x[:], [], [r("xn")], "lx")
 
-    level[0] = 10 ** 6
     iota(r("ij"), [[1, 128]], 0, -1)
     for k in range(7):
         iota(cell("pi", k), [[0, 1]], 0, 1 << (6 - k))
@@ -340,33 +338,27 @@ def rank_program(g, core, T, topo):
     for b in range(4):
         quant("eq", "es", 128 * b, 128 * b + 128, r("eb", 4 - b, 516 - b))
     for name, a, z, st, c in [
-            ("ep", K, 4 * EW, GV, 0.0),
-            ("neg1", 0, 256, 1, -1.0), ("one", 0, SW, 1, 1.0),
-            ("pt", 0, 8 * RS, RS, -BIG), ("ya", 0, 1, 1, 1.0), ("cfl", 0, 22, 1, 0.0),
-            ("rst", 0, 128, 1, 1.0), ("rst", 0, 128, 16, 0.0), ("stp", 0, 8, 1, STEP),
-            ("wb", 0, 64, 1, 0.0), ("et", 0, 128, 1, 0.0), ("pf", 8, 16, 1, 0.0), ("tb", 0, 32, 1, 0.0)]:
+            ("ep", K, 4 * EW, GV, 0.0), ("neg1", 0, 256, 1, -1.0), ("one", 0, SW, 1, 1.0),
+            ("pt", 0, 8 * RS, RS, -BIG), ("ya", 0, 1, 1, -1.0), ("cfl", 1, 2, 1, 0.0),
+            ("rst", 0, 128, 1, 1.0), ("rst", 0, 128, 16, 0.0), ("stp", 0, 7, 1, STEP), ("stp", 7, 8, 1, -STEP),
+            ("wb", 0, 64, 1, 0.0), ("et", 0, 128, 1, 0.0), ("pf", 8, 16, 1, 0.0), ("wv", 0, 1, 1, 0.0),
+            ("zz", 128, 512, 1, 0.0)]:
         fill(r(name, a, z, st), c)
     ts(r("bi", 0, 7), r("pi", 0, 7), 6, 1, A.logical_shift_right, A.bitwise_and)
     ts(cell("bi", 7), cell("pi", 6), 15, None, A.bitwise_and)
     copy("v", r("bf"), r("bi"))
-    iota(r("ii"), [[1, 128]], 0, 0)
-    iota(r("kk"), [[1, 128]], 0, 0)
+    iota(r("ii"), [[1, 8]], 0, 0)
     iota(r("tab", 0, 192), [[2, 192]], -384, 0)
     iota(r("tab", 192, 384), [[2, 192]], 0, 0)
     iota(r("dm"), [[0, 8], [1, 16]], 0, 0)
     ts(r("dm"), r("dm"), cell("bf", 7), None, A.is_equal)
     iota(r("qc"), [[16, 8]], 0, 0)
     ts(r("qc"), r("qc"), cell("bf", 7), None, A.add)
-
-    def tri(c):
-        a = 144 * c if c < 4 else 144 * (7 - c) + 16 * (8 - c)
-        return a, a + 16 * c + 16
-
-    for c in range(8):
-        a, z = tri(c)
-        ts(r("wrow", a, z), r("ii", 0, z - a), cell("qc", c), -1024.0, A.is_le, A.mult)
-    fill(r("wrow", 0, TRI, 144), 2.0 ** 30)
-    fill(r("wrow", 16, TRI, 160), 2.0 ** 30)
+    for kind, (step, base) in enumerate(((4.0, -382.0), (4.0, -384.0), (2.0, 128.0))):
+        lin(r("col", 8 * kind, 8 * kind + 8), r("qc"), step, base)
+    lin(r("ncol"), r("col"), -256.0, 0.0)
+    iota(r("dec"), [[0, cols(r("dec"))]], -1, 0)
+    fill(r("dec", 0, None, 128), 1024.0)
 
     for k in range(3):
         act(cell("xr", k), cell("bf", k), AF.Abs, cell("bf", k + 4), -1.0)
@@ -375,30 +367,23 @@ def rank_program(g, core, T, topo):
     lin(cell("tm", 2), cell("xr", 0), 64.0, cell("tm", 1))
     lin(cell("tm", 3), cell("xr", 1), 128.0, cell("tm", 2))
     lin(cell("cfl", 0), cell("xr", 2), 32.0, cell("tm", 3))
-    iota(r("tb", 0, 4), [[160, 4]], 15, 0)
-    iota(r("tb", 4, 8), [[-144, 4]], 575, 0)
-    copy("sv", r("tb", 16, 24), r("tb", 0, 8))
-    for h in range(2):
-        for c0 in range(2):
-            iota(r("tb", 32 + 16 * h + c0, 48 + 16 * h, 2), [[0, 2], [32, 4]], (128 + 32 * c0) * (h ^ c0) + 16 * h, 0)
+    iota(r("tb", 0, 32), [[0, 2], [RS, 2], [0, 8]], 384, 0)
+    iota(r("tb", 32, 64), [[0, 4], [16, 8]], 15, 0)
     for o in range(2):
         iota(r("tb", 64 + o, 96, 2), [[0, 2], [1, 8]], o, 0)
-    iota(r("tb", 96, 128), [[0, 2], [RS, 2], [0, 8]], 384, 0)
-    iota(r("tb", 128, 160), [[0, 4], [16, 8]], 15, 0)
     turn(r("tc"), r("tb"))
-    copy("sv", r("cfl", 2, 6, 2), r("tc", 0, 64, 32))
-    lin(r("cfl", 6, 9), r("ii", 0, 3), 2.0 * RS, cell("tc", 96))
-    lin(r("cfl", 10, 13), r("ii", 0, 3), 0.0, cell("tc", 128))
-    lin(r("cfl", 14, 22), r("ii", 0, 8), 0.0, cell("tc", 64))
+    lin(r("cfl", 2, 6), r("ii", 0, 4), 2.0 * RS, cell("tc", 0))
+    lin(r("cfl", 6, 10), r("ii", 0, 4), 0.0, cell("tc", 32))
+    lin(r("cfl", 10, 18), r("ii", 0, 8), 0.0, cell("tc", 64))
     copy("v", r("cu"), r("cfl"))
 
     ev, od = (0, 1, 6, 7), (2, 3, 4, 5)
     odd = r("so", 1, 256, 2)
 
-    def planes(t, a, out):
+    def planes(t, a, out, also=()):
         for b in range(4):
             mm(od[b], "eq", "es", 128 * b, "tq%d" % t, "ts%d" % t, a, a + 128)
-            copy("s", r("vp", 384 * b + out[0], 384 * b + out[1], out[2]), bk(od[b]))
+            copy("s", r("vp", 384 * b + out[0], 384 * b + out[1], out[2]), bk(od[b]), also=also)
 
     def levels(at, data, low, parts=1):
         wide = 128 // parts
@@ -421,59 +406,51 @@ def rank_program(g, core, T, topo):
         quant(tq, tsc, 128, 256, r("xe"))
         send(rank - 1 - t, [(r(tq, 256, 384), r(tq, 128, 256)), (r(tsc, 256, 384), r(tsc, 128, 256))], "at%d" % t, t == 0)
 
-    level[0] = 1
     for j in range(4):
         copy("vs", r("xe", j, 512, 4), r("xn", j, 1024, 8))
     even_part(0)
-    level[0] = 2
     for j in range(4):
         copy("vs", r("xo", j, 512, 4), r("xn", 4 + j, 1024, 8))
     odd_part(0)
 
     for t in range(R):
         tq, tsc, hq, hs = "tq%d" % t, "ts%d" % t, "hq%d" % t, "hs%d" % t
-        of = "of%d" % t
+        of, ol = "of%d" % t, "ol%d" % t
         last = t == R - 1
 
-        def now(u):
-            level[0] = 100 * t + u
-
-        now(19)
-        iota(r("win", 0, 432), [[0, 216], [-GV, 2]], GV + K, 0)
-
-        now(10)
         mm(ev[0], tq, tsc, 0, tq, tsc, 128, 256)
         mm(ev[1], tq, tsc, 0, tq, tsc, 128, 256)
         copy("s", r("so", 0, 256, 2), bk(ev[1]))
         levels(128, bk(ev[0]), odd, HALVES)
         edge = prow(7, 256, 257)
-        tt(r("ya", 1, 8), best(256, 1, 8), best(256, 0, 7), A.not_equal)
+        bonus[0] = MARK
+        act(r("ya", 1, 8), best(256, 0, 7), AF.Sign, edge, -1.0)
         ts(r("xg"), r("so"), edge, STEP, A.is_le, A.max)
         act(r("sg"), r("so"), AF.Sign, edge, -1.0)
-        scan(r("ta"), r("ya"), r("stp"), 1.0, A.max, A.mult)
+        scan(r("ta"), r("ya"), r("stp"), 0.0, A.min, A.mult)
         scan(r("ma"), r("xg"), r("neg1"), cell("ta", 7), A.mult, A.max)
         ts(r("xh"), r("sg"), STEP, None, A.max)
         scan(r("mb"), r("xh"), r("ma"), 1.0, A.mult, A.max)
+        bonus[0] = SUMS
         for j in range(4):
-            part = r("junk", 256 * j, 256 * j + 256)
-            if j in BY_SCAN:
-                ts(part, r("mb"), STEP ** -(2 * j + 1), 4097.0, A.mult, A.min)
-                scan(r("sums", 256 * j, 256 * j + 256), r("neg1"), part, 4098.0 * 256, A.add, A.subtract)
-            else:
-                act(part, r("mb"), AF.Relu, 4097.0, -STEP ** -(2 * j + 1), cell("sums", 256 * j + 255))
-        sums = r("sums", 255, 1024, 256)
-        ts(r("wi", 0, 4), sums, -1.0, 4097.0 * 256, A.mult, A.add)
-        ts(r("pu", 0, 8, 2), sums, -1.0 / 4096, 4097.0 / 16, A.mult, A.add)
-        ts(r("wi", 4, 8), r("wi", 0, 4), 4095, None, A.bitwise_and)
-        copy("v", r("pu", 1, 8, 2), r("wi", 4, 8))
+            act(r("junk", 256 * j, 256 * j + 256), r("mb"), AF.Relu, 4097.0, -STEP ** -(2 * j + 1), cell("sums", j))
+        bonus[0] = PICK
+        m = 4 - QUICK
+        ts(r("wi", 0, m), r("sums", 0, m), -1.0, 4097.0 * 256, A.mult, A.add)
+        ts(r("pu", 0, 2 * m, 2), r("sums", 0, m), -1.0 / 4096, 4097.0 / 16, A.mult, A.add)
+        ts(r("wi", 4, 4 + m), r("wi", 0, m), 4095, None, A.bitwise_and)
+        copy("v", r("pu", 1, 2 * m, 2), r("wi", 4, 4 + m))
+        if QUICK:
+            ts(cell("pu", 6), cell("sums", 3), -1.0 / 4096, 4097.0 / 16, A.mult, A.add)
+            lin(cell("zc", 0), cell("sums", 3), -1.0, 4097.0 * 256)
+            ts(cell("pu", 7), cell("pu", 6), -4096.0, cell("zc", 0), A.mult, A.add)
         tt(r("gv"), r("so"), r("dm"), A.mult, off=r("pu"))
         scan(r("vv"), r("rst"), r("gv"), 0.0, A.mult, A.add)
-        ts(r("pf", 0, 8), r("pu"), 1.0 / 256, -1.0, A.mult, A.add)
-        copy("s", r("pr"), r("pf"), off=r("cu", 14, 22))
-        now(17)
+        ts(r("pf", 0, 8), r("pu"), 1.0 / 512, -0.375, A.mult, A.add)
+        copy("s", r("pr"), r("pf"), off=r("cu", 10, 18))
+        bonus[0] = 0.0
         planes(t, 128, (0, 256, 2))
 
-        now(11)
         if t == 0:
             dma("y", T.wq[:].bitcast(dt.uint8), T.wc[:], [r(tq, 256, 384)], [r("wq")], "lwc")
             dma("y", T.wsc[:], T.ws[:], [r(tq, 256, 384)], [r("wsc")], "lws")
@@ -486,10 +463,12 @@ def rank_program(g, core, T, topo):
         for a, z in TIES:
             if z - a > 1:
                 tt(r("eqb", a, z), best(384, a, z), best(384, a - 1, z - 1), A.is_equal)
-                scan(r("et", 16 * a, 16 * z, 16), r("neg1", a, z), r("eqb", a, z), cell("et", 16 * a - 16), A.add, A.mult)
+                scan(r("wv", a, z), r("neg1", a, z), r("eqb", a, z), cell("wv", a - 1), A.add, A.mult)
             else:
-                lin(cell("zc", a), cell("et", 16 * a - 16), 1.0, -1.0, "sv")
-                ts(cell("et", 16 * a), best(384, a, z), best(384, a - 1, a), cell("zc", a), A.is_equal, A.mult)
+                lin(cell("zc", a), cell("wv", a - 1), 1.0, -1.0, "sv")
+                ts(cell("wv", a), best(384, a, z), best(384, a - 1, a), cell("zc", a), A.is_equal, A.mult)
+        bonus[0] = 2.0
+        lin(r("et", 0, 128, 16), r("wv"), 1.0, -0.5)
         for k in range(8):
             bonus[0] = LEAD * (7 - k)
             top = prow(k, 384, 385)
@@ -499,77 +478,61 @@ def rank_program(g, core, T, topo):
                 act(row("nb"), row("sh"), AF.Abs, 0.0, 1.0)
             else:
                 ts(row("nb"), r("sc"), top, None, A.not_equal)
-            scan(row("cb"), r("one"), row("nb"), cell("et", 16 * k), A.add, A.subtract)
+            scan(row("cb"), r("one"), row("nb"), cell("wv", k), A.add, A.subtract)
             act(r("jb", 128 * k, 128 * k + 128), row("cb", 8), AF.Sign, 0.5, -1.0, cell("ab", k))
         bonus[0] = 0.0
-        lin(r("ac"), r("ab"), 1.0 / 512, 0.5)
-        copy("s", r("vr"), r("pt", 0, 6 * RS), off=r("cu", 6, 9))
-        tt(r("et", 1, 96, 2), r("vv"), r("vr"), A.is_equal, off=r("cu", 10, 13))
-        for k in (6, 7):
-            ts(r("et", 16 * k + 1, 16 * k + 16, 2), r("vv", 15, 128, 16), prow(k, 384, 385), None, A.is_equal)
+        lin(r("pr", 15, 128, 16), r("ab"), 1.0 / 1024, 0.25)
+        copy("s", r("vr"), r("pt"), off=r("cu", 2, 6))
+        tt(r("et", 1, 128, 2), r("vv"), r("vr"), A.is_equal, off=r("cu", 6, 10))
         scan(r("yy"), r("rst"), r("et"), 0.0, A.mult, A.subtract)
-        scan(r("zz"), r("yy"), r("pr"), 0.0, A.max, A.min)
-        tt(r("wb", 0, 8), r("zz", 15, 128, 16), r("ac"), A.add)
-        now(18)
-        planes(t, 256, (256, 384, 1))
+        scan(r("zz", 0, 128), r("yy"), r("pr"), 0.0, A.max, A.min)
+        named = lambda p0=0, p1=128: r("zz", 15, 128, 16, p0, p1)
+        planes(t, 256, (256, 384, 1), [cell("ab", LATE)] if LATE < 8 else [])
 
-        now(14)
-        turn(r("yb", 0, 32), r("wb", 0, 32))
-        turn(r("yb", 32, 64), r("wb", 0, 32))
-        copy("sv", r("wb", 32, 40, p1=64), r("wb", 0, 8, p0=64))
-        copy("sv", r("wb", 32, 40, p0=64), r("wb", 0, 8, p1=64))
+        turn(r("yb", 0, 32), r("zz", 15, 512, 16))
+        turn(r("yb", 32, 64), r("zz", 15, 512, 16))
+        copy("s", r("wb", 0, 8), named())
+        copy("s", r("wb", 32, 40, p1=64), named(p0=64))
+        copy("s", r("wb", 32, 40, p0=64), named(p1=64))
         turn(r("wb", 96, 128, p1=64), r("yb", 16, 48, p0=64))
         turn(r("wb", 96, 128, p0=64), r("yb", 16, 48, p1=64))
         turn(r("wb", 64, 96), r("yb", 16, 48))
         for q in range(4):
             o = q ^ 1
             copy("svvv"[q], r("wb", 128, 232, p0=32 * q, p1=32 * q + 32), r("wb", 0, 104, p0=32 * o, p1=32 * o + 32))
-        ts(r(of), r("wb"), 256.0, 192.0, A.mult, A.add, off=cell("cu", 0))
+        ts(r(of), r("wb"), 512.0, 192.0, A.mult, A.add, off=cell("cu", 0))
 
-        now(22)
         for b in range(4):
             copy("vs", r("zt", b, 512, 4), r("vp", 384 * b, 384 * b + 384), off=r(of, 0, 8))
         quant("zq", "zsc", 0, 128, r("zt"))
         for b in range(4):
             mm(od[b], "wq", "wsc", 128 * b, "zq", "zsc", 0, 128)
-            copy("vs", r("ht", b, 512, 4), bk(od[b]), scale=0.03125)
+            copy(HT[b], r("ht", b, 512, 4), bk(od[b]), scale=0.03125)
         quant(hq, hs, 0, 128, r("ht"))
         send(rank + 1 + t, [(r(hq, 128, 256), r(hq, 0, 128)), (r(hs, 128, 256), r(hs, 0, 128))], "ah%d" % t)
 
-        now(21)
+        def first(kind, lst):
+            for c in range(8):
+                row, j = r("d1", 1024 * kind + 128 * c, 1024 * kind + 128 * c + 128), 8 * kind + c
+                forms = {"s": act_form(row, lst, AF.Abs, cell("ncol", j), 256.0),
+                         "v": ts_form(row, lst, cell("col", j), 512.0, A.not_equal, A.mult)}
+                add({q: forms[q] for q in ROWS[kind][c]}, [lst, cell("col", j), cell("ncol", j)], [row])
+            step = 1024 // CUT[kind]
+            for a in range(1024 * kind, 1024 * kind + 1024, step):
+                scan(r("u1", a, a + step), r("dec", 0, step), r("d1", a, a + step), 0.0, A.add, A.min)
+            return r("u1", 1024 * kind + 127, 1024 * kind + 1024, 128)
+
         copy("s", r("lb"), r("tab"), off=r(of, 0, 8))
-        now(LIST)
-        copy("s", r("me"), r("wb"), off=cell("cu", 0), scale=512.0)
-        copy("s", r("nme"), r("wb"), off=cell("cu", 0), scale=-2.0 ** 27)
-        for c in range(7, -1, -1):
-            a, z = tri(c)
-            out, lst = r("dd", a, z), r("lb", 0, z - a)
-            if c in ROWS_S:
-                act(out, lst, AF.Abs, cell("nme", c), 2.0 ** 18)
-            else:
-                ts(out, lst, cell("me", c), 2.0 ** 19, A.not_equal, A.mult)
-        scan(r("du"), r("wrow"), r("dd"), 0.0, A.add, A.min)
-        tt(r("da"), r("du"), r("me"), A.subtract, off=cell("cu", 2))
-        ts(r("sf"), r("da"), -0.5, 224.0, A.mult, A.add)
-        add({"v": (0.05 + 3.5 * 128 * CYCLE, lambda e: e.tensor_copy(ap(r("win")).indirect(ap(r("sf", 0, 8))), ap(r("kk"))))},
-            [r("kk"), r("sf", 0, 8)], [r("win")])
-
-        def inverse(name, a, st):
-            turn(r(name, 0, 128), r("win", a, a + 128 * st, st))
-            turn(r(name, 128, 288), r("win", a - 16 * st, a + 144 * st, st))
-
-        inverse("rp", 288, 1)
-        copy("vs", r("gl%d" % t), r("rp"), off=cell("cu", 4))
-        send(rank + 1 + t, [(r("gr%d" % t), r("gl%d" % t, 0, 8))], "al%d" % t)
+        send(rank + 1 + t, [(r(ol), r(of, 0, 8))], "al%d" % t)
         bonus[0] = ODD
-        inverse("ro", 33, 2)
-        copy("v", r("f1"), r("ro"), off=cell("cu", 4))
+        ts(r("f1"), first(0, r("lb")), 127.0, 128.0, A.add, A.min)
         bonus[0] = 0.0
-        inverse("rv", 32, 2)
-        act(r("fe"), r("rv"), AF.Identity, float(-GV), 1.0, off=cell("cu", 4))
+        lin(r("fe"), first(1, r("lb")), 1.0, float(-GV), "sv")
+        copy("s", r("lg"), r("tab"), off=r(ol))
+        tt(r("fm"), r("fe"), first(2, r("lg")), A.min)
+        ts(r("f2"), r("fm"), GV + 127.0, GV + 128.0, A.add, A.min)
         if last:
-            now(40)
-            lin(r("opt"), r("yb", 0, 32), 256.0, 192.0)
+            lin(r("opt"), r("yb", 0, 32), 512.0, 192.0)
             for a in range(4):
                 dma("y", T.op[:, 32 * a:32 * a + 32], T.opt[32 * a:32 * a + 8, :], [r("opt")], [], "outs")
             quant("vq", "vs", 0, 128, r("vt"))
@@ -578,11 +541,7 @@ def rank_program(g, core, T, topo):
             bonus[0] = ODD * a
             for b in range(4):
                 mm(banks[b], "eq", "es", 128 * b, hq, hs, 128 - 128 * a, 256 - 128 * a)
-                copy("sv", r("ep", EW * b + GV - GV * a, EW * b + GV - GV * a + 128), bk(banks[b]))
-            now(32 if a else 30)
-            if not a:
-                tt(r("fm"), r("fe", 0, 8), r("gr%d" % t), A.min)
-                ts(r("f2"), r("fm"), float(GV), None, A.add)
+                copy("sv" if a else EP[b], r("ep", EW * b + GV - GV * a, EW * b + GV - GV * a + 128), bk(banks[b]))
             for b in range(4):
                 tt(r("xl", 4 * a + b, 1024, 8) if last else r(tile, b, 512, 4), r("ep", EW * b, EW * b + (GV if a else EW)),
                    r("vp", 384 * b + a, 384 * b + 256, 2), A.add, off=r(lst, 0, 8))
@@ -597,8 +556,7 @@ def rank_program(g, core, T, topo):
         dma("sy"[k // 2], T.osc[4 * k:4 * k + 4, :], T.ls[32 * k:32 * k + 4, :], [r("ls")], [], "outs")
     copy("v", r("yt", 0, 128), bk(2))
     copy("s", r("yt", 128, 256), bk(3))
-    dma("y", T.y[:, 0:128], T.yt[:, 0:128], [r("yt", 0, 128)], [], "outs")
-    dma("s", T.y[:, 128:256], T.yt[:, 128:256], [r("yt", 128, 256)], [], "outs")
+    dma("s", T.y[:], T.yt[:], [r("yt")], [], "outs")
 
     if not PLAN:
         PLAN.extend(arrange(calls))

@@ -3,21 +3,25 @@ from concourse.mybir import dt, AluOpType, ActivationFunctionType
 C, K, R = 256, 128, 3
 BIG = 1.0e29
 RS = 385
-SW = 136
+SW = 137
 GV, EW = 144, 288
 STEP = 2.0 ** -13
 CODES, U8 = "float8_e4m3fn_x4", "uint8"
 F32, BF16, I32, U16 = "float32", "bfloat16", "int32", "uint16"
-CYCLE, WAKE, LOAD, FLIGHT, HOP = 0.83e-3, 0.175, 2.0, 2.1, 1.0
-FIX, FIRST, ODD, AHEAD = 0.05, 1.2, 0.5, 2.1
-LATE, LEAD = 4, 0.05
-RULES = [(own, weight, slack, spare) for own in (0.0, 0.5, 1.0) for weight in (0.6, 1.0, 1.6)
-         for slack in (0.06, 0.08, 0.1, 0.12) for spare in (0.1, 0.15)]
-MARK, SUMS, PICK, HT, EP = 0.0, 0.0, 0.0, "svss", "ssss"
-BY_SIGN = (1, 2, 3)
+CYCLE, WAKE, LOAD, FLIGHT, HOP = 0.83e-3, 0.175, 1.7, 2.0, 1.2
+FIX, FIRST, ODD, AHEAD = 0.05, 0.8, 0.0, 2.0
+LATE, LEAD, XE, XO, APART = 6, 0.0, "vvvs", "svvs", True
+LB, ODD1, ZH, ZT = 0.0, 0.0, 0.0, ["vs"] * 4
+RULES = [(0, 1.0, 0.1, 0.1)]
+URGE = {'wv': 2.0, 'nb6': 1.0, 'eqb': 1.0, 'nb7': -0.5, 'cb7': -0.5, 'cb3': 0.2, 'pu0': -0.5, 'jb0': -2.0, 'u12': -0.5, 'wi4': -0.5, 'f2': -0.2, 'sh2': 0.2, 'pf': -2.0, 'pt2': 1.0, 'et0': -2.0, 'd11': -1.0, 'sh1': 0.2, 'cb1': 0.5, 'cb2': 2.0}
+WAIT = {'ht': 0.0, 'd12': 0.25, 'pr0': 0.25}
+SIDE = {'zt': 0.0, 'd10': 0.0, 'ep0': 1.0, 'd11': 0.0, 'd12': 0.25, 'ep1': 1.0, 'ht': 0.05}
+MARK, SUMS, PICK, HT, EP = 0.0, 0.0, 0.0, ["vs"] * 4, ["vs"] * 4
+BY_SIGN = (0, 1, 2)
 CUT, HALVES, QUICK = (2, 2, 2), 1, 0
 ROWS = [["vs"] * 8, ["vs"] * 8, ["vs"] * 8]
 TIES = ((1, 7), (7, 8))
+JOINT = (3, 4, 5)
 
 SCRATCH = {}
 PLAN = []
@@ -32,17 +36,17 @@ for _n, _c, _d in [
     ("vq", 128, CODES), ("vs", 128, U8), ("wq", 512, CODES), ("wsc", 512, U8),
     ("lq", 256, CODES), ("ls", 256, U8), ("yt", 256, F32), ("opt", 32, F32),
     ("eb", 516, BF16), ("eq", 512, CODES), ("es", 512, U8),
-    ("ij", 128, F32), ("ii", 8, F32), ("pi", 8, I32), ("bi", 8, I32), ("bf", 8, F32),
+    ("ij", 128, F32), ("ii", 8, F32), ("pw", 16, F32), ("pi", 8, I32), ("bi", 8, I32), ("bf", 8, F32),
     ("xr", 4, F32), ("tm", 8, F32), ("qc", 8, F32), ("tb", 96, F32), ("tc", 96, F32),
-    ("mdiag", 128, F32), ("neg1", 256, BF16), ("one", SW, BF16), ("cfl", 18, F32), ("cu", 18, U16),
+    ("mdiag", 128, F32), ("neg1", 256, BF16), ("one", SW - 1, BF16), ("rs2", SW * max(len(JOINT), 1), BF16), ("cfl", 18, F32), ("cu", 18, U16),
     ("tab", 384, BF16), ("dm", 128, F32), ("rst", 128, BF16), ("stp", 8, BF16),
     ("dec", 1024 // min(CUT), BF16), ("col", 24, BF16), ("ncol", 24, F32),
     ("so", 256, F32), ("pt", 8 * RS, F32), ("xg", 256, BF16), ("xh", 256, BF16), ("ma", 256, BF16), ("mb", 256, BF16),
     ("ya", 8, F32), ("ta", 8, F32), ("junk", 1024, F32), ("sums", 4, F32), ("wi", 8, I32), ("pu", 8, U16),
     ("gv", 128, F32), ("vv", 128, F32), ("pf", 16, BF16), ("pr", 128, BF16), ("vr", 64, F32),
-    ("sg", 256, BF16), ("sc", SW, F32), ("sh", 8 * SW, BF16), ("nb", 8 * SW, BF16), ("cb", 8 * SW, BF16), ("jb", 1024, BF16),
+    ("sg", 256, BF16), ("sc", SW - 1, F32), ("sh", 8 * SW, BF16), ("nb", 8 * SW, BF16), ("cb", 8 * SW, BF16), ("jb", 1024, BF16),
     ("eqb", 8, F32), ("zc", 8, F32), ("wv", 8, BF16), ("ab", 8, F32), ("et", 128, BF16), ("yy", 128, BF16), ("zz", 512, BF16),
-    ("wb", 232, BF16), ("yb", 64, BF16), ("vp", 1536, BF16), ("zt", 512, BF16), ("zq", 128, CODES), ("zsc", 128, U8),
+    ("wb", 160, BF16), ("yb", 96, BF16), ("vp", 1536, BF16), ("zt", 512, BF16), ("zq", 128, CODES), ("zsc", 128, U8),
     ("ht", 512, BF16), ("lb", 128, BF16), ("lg", 128, BF16), ("d1", 3072, BF16), ("u1", 3072, BF16),
     ("fe", 8, F32), ("fm", 8, F32), ("f1", 8, U16), ("f2", 8, U16), ("ep", 4 * EW, BF16),
 ]:
@@ -87,6 +91,14 @@ def meet(a, b):
     return not set(range(a[3], a[4], a[5])).isdisjoint(range(b[3], b[4], b[5]))
 
 
+def kind(call):
+    name, p0, p1, c0, c1, st = (call[2] or call[1])[0]
+    part = {"d1": c0 // 1024, "u1": c0 // 1024, "ep": c0 % EW // GV, "pt": c0 % RS // 128, "so": c0, "wb": c0 // 64,
+            "vp": (c0 % 384 + 127) // 128, "tq": c0 // 128, "hq": c0 // 128, "pr": c0, "et": c0, "sc": c0,
+            "nb": c0 // SW, "cb": c0 // SW, "sh": c0 // SW, "jb": c0 // 128, "wi": c0, "pu": c0}.get(name[:2])
+    return name if part is None else "%s%d" % (name[:2], part)
+
+
 def arrange(calls):
     before, after, seen = [], [[] for c in calls], {}
     for i, (forms, reads, writes, delay, extra) in enumerate(calls):
@@ -112,7 +124,8 @@ def arrange(calls):
         way[i] = min(c for c, f in forms.values()) + max([way[j] + before[j][i] for j in after[i]] + [delay])
 
     def place(own, weight, slack, spare):
-        urgent = [own * min(x for x, f in c[0].values()) - w - weight * c[4] for w, c in zip(way, calls)]
+        urgent = [own * min(x for x, f in c[0].values()) - w - weight * c[4] - URGE.get(kind(c), 0.0) for w, c in zip(way, calls)]
+        spared = [SIDE.get(kind(c), spare) for c in calls]
         got, free = {}, {q: 0.0 for q in "vstgy"}
         left = [len(deps) for deps in before]
         ready = {i: 0.0 for i in range(len(calls)) if not left[i]}
@@ -121,7 +134,7 @@ def arrange(calls):
             now = free[q]
 
             def fits(i):
-                ends = {o: max(free[o], ready[i]) + c + spare * (o == "v") for o, (c, f) in calls[i][0].items()}
+                ends = {o: max(free[o], ready[i]) + c + spared[i] * (o == "v") for o, (c, f) in calls[i][0].items()}
                 return q in ends and ends[q] <= min(ends.values())
             mine = sorted((i for i in ready if fits(i)), key=lambda i: (urgent[i], i))
             until, chosen = float("inf"), None
@@ -129,7 +142,7 @@ def arrange(calls):
                 if ready[i] <= now and now + calls[i][0][q][0] <= until:
                     chosen = i
                     break
-                until = min(until, ready[i] + slack)
+                until = min(until, ready[i] + WAIT.get(kind(calls[i]), slack))
             if chosen is None:
                 free[q] = min([ready[i] for i in mine if ready[i] > now] + [t for t in free.values() if t > now] + [now + 0.05])
                 continue
@@ -303,7 +316,7 @@ def rank_program(g, core, T, topo):
         def go():
             total[sem] = 0
             for i, (out, in_) in enumerate(pairs):
-                lanes = shared[i::len(pairs)] if apart else shared
+                lanes = shared[i::len(pairs)] if apart and APART else shared
                 order("g", [in_], [])
                 a, b = ap(out), ap(in_)
                 if SCRATCH[in_[0]][2] == CODES:
@@ -330,18 +343,20 @@ def rank_program(g, core, T, topo):
     dma("y", T.xn[:], T.x[:], [], [r("xn")], "lx")
 
     iota(r("ij"), [[1, 128]], 0, -1)
-    for k in range(7):
-        iota(cell("pi", k), [[0, 1]], 0, 1 << (6 - k))
+    fill(r("pw", 0, 8), 0.5)
+    scan(r("pw", 8, 15), r("pw", 0, 7), r("pw", 0, 7), -128.0, A.mult, A.min)
+    ts(r("pi", 0, 7), r("pw", 8, 15), cell("ij", 0), None, A.mult)
     fill(r("eb"), 0.0)
     ts(r("mdiag"), r("ij"), 0.0, -BIG, A.is_equal, A.mult)
     ts(r("eb", 4, 516, 4), r("ij"), 0.0, None, A.is_equal)
     for b in range(4):
         quant("eq", "es", 128 * b, 128 * b + 128, r("eb", 4 - b, 516 - b))
     for name, a, z, st, c in [
-            ("ep", K, 4 * EW, GV, 0.0), ("neg1", 0, 256, 1, -1.0), ("one", 0, SW, 1, 1.0),
+            ("ep", K, 4 * EW, GV, 0.0), ("neg1", 0, 256, 1, -1.0), ("one", 0, None, 1, 1.0),
+            ("rs2", 0, None, 1, 1.0), ("rs2", 0, None, SW, 0.0),
             ("pt", 0, 8 * RS, RS, -BIG), ("ya", 0, 1, 1, -1.0), ("cfl", 1, 2, 1, 0.0),
             ("rst", 0, 128, 1, 1.0), ("rst", 0, 128, 16, 0.0), ("stp", 0, 7, 1, STEP), ("stp", 7, 8, 1, -STEP),
-            ("wb", 0, 64, 1, 0.0), ("et", 0, 128, 1, 0.0), ("pf", 8, 16, 1, 0.0), ("wv", 0, 1, 1, 0.0),
+            ("et", 0, 128, 1, 0.0), ("pf", 8, 16, 1, 0.0), ("wv", 0, 1, 1, 0.0),
             ("zz", 128, 512, 1, 0.0)]:
         fill(r(name, a, z, st), c)
     ts(r("bi", 0, 7), r("pi", 0, 7), 6, 1, A.logical_shift_right, A.bitwise_and)
@@ -364,9 +379,13 @@ def rank_program(g, core, T, topo):
         act(cell("xr", k), cell("bf", k), AF.Abs, cell("bf", k + 4), -1.0)
     lin(cell("tm", 0), cell("bf", 5), 2.0, cell("bf", 4))
     lin(cell("tm", 1), cell("bf", 6), 4.0, cell("tm", 0))
-    lin(cell("tm", 2), cell("xr", 0), 64.0, cell("tm", 1))
-    lin(cell("tm", 3), cell("xr", 1), 128.0, cell("tm", 2))
-    lin(cell("cfl", 0), cell("xr", 2), 32.0, cell("tm", 3))
+    act(cell("xr", 3), cell("xr", 1), AF.Abs, cell("bf", 4), -1.0)
+    lin(cell("tm", 2), cell("xr", 2), 2.0, cell("xr", 1))
+    lin(cell("tm", 3), cell("xr", 2), 2.0, cell("xr", 3))
+    lin(cell("tm", 4), cell("tm", 3), 32.0, 32.0)
+    lin(cell("tm", 5), cell("tm", 2), -8.0, cell("tm", 4))
+    lin(cell("tm", 6), cell("tm", 2), 8.0, cell("tm", 1))
+    ts(cell("cfl", 0), cell("tm", 5), cell("xr", 0), cell("tm", 6), A.mult, A.add)
     iota(r("tb", 0, 32), [[0, 2], [RS, 2], [0, 8]], 384, 0)
     iota(r("tb", 32, 64), [[0, 4], [16, 8]], 15, 0)
     for o in range(2):
@@ -406,11 +425,13 @@ def rank_program(g, core, T, topo):
         quant(tq, tsc, 128, 256, r("xe"))
         send(rank - 1 - t, [(r(tq, 256, 384), r(tq, 128, 256)), (r(tsc, 256, 384), r(tsc, 128, 256))], "at%d" % t, t == 0)
 
+    bonus[0] = 5.0
     for j in range(4):
-        copy("vs", r("xe", j, 512, 4), r("xn", j, 1024, 8))
+        copy(XE[j], r("xe", j, 512, 4), r("xn", j, 1024, 8))
     even_part(0)
+    bonus[0] = 4.0
     for j in range(4):
-        copy("vs", r("xo", j, 512, 4), r("xn", 4 + j, 1024, 8))
+        copy(XO[j], r("xo", j, 512, 4), r("xn", 4 + j, 1024, 8))
     odd_part(0)
 
     for t in range(R):
@@ -458,7 +479,7 @@ def rank_program(g, core, T, topo):
         mm(ev[2], tq, tsc, 0, tq, tsc, 256, 384)
         mm(ev[3], tq, tsc, 0, tq, tsc, 256, 384)
         copy("s", r("sc", 0, 8), best(256))
-        copy("s", r("sc", 8, SW), bk(ev[3]))
+        copy("s", r("sc", 8, 136), bk(ev[3]))
         levels(256, bk(ev[2]), r("so", 0, 128))
         for a, z in TIES:
             if z - a > 1:
@@ -472,14 +493,20 @@ def rank_program(g, core, T, topo):
         for k in range(8):
             bonus[0] = LEAD * (7 - k)
             top = prow(k, 384, 385)
-            row = lambda name, a=0: r(name, SW * k + a, SW * k + SW)
+            row = lambda name, a=1, k=k: r(name, SW * k + a, SW * k + SW)
             if k in BY_SIGN:
                 act(row("sh"), r("sc"), AF.Sign, top, -1.0)
                 act(row("nb"), row("sh"), AF.Abs, 0.0, 1.0)
             else:
-                ts(row("nb"), r("sc"), top, None, A.not_equal)
-            scan(row("cb"), r("one"), row("nb"), cell("wv", k), A.add, A.subtract)
-            act(r("jb", 128 * k, 128 * k + 128), row("cb", 8), AF.Sign, 0.5, -1.0, cell("ab", k))
+                ts(row("nb"), r("sc"), top, None, A.is_equal if k in JOINT else A.not_equal)
+            if k not in JOINT:
+                scan(row("cb"), r("one"), row("nb"), cell("wv", k), A.add, A.subtract)
+            elif k == JOINT[-1]:
+                a, z = SW * JOINT[0], SW * k + SW
+                copy("s", r("nb", a, z, SW), r("wv", JOINT[0], k + 1))
+                scan(r("cb", a, z), r("rs2"), r("nb", a, z), 0.0, A.mult, A.add)
+            for j in ([k] if k not in JOINT else JOINT if k == JOINT[-1] else []):
+                act(r("jb", 128 * j, 128 * j + 128), row("cb", 9, j), AF.Sign, 0.5, -1.0, cell("ab", j))
         bonus[0] = 0.0
         lin(r("pr", 15, 128, 16), r("ab"), 1.0 / 1024, 0.25)
         copy("s", r("vr"), r("pt"), off=r("cu", 2, 6))
@@ -489,21 +516,25 @@ def rank_program(g, core, T, topo):
         named = lambda p0=0, p1=128: r("zz", 15, 128, 16, p0, p1)
         planes(t, 256, (256, 384, 1), [cell("ab", LATE)] if LATE < 8 else [])
 
-        turn(r("yb", 0, 32), r("zz", 15, 512, 16))
-        turn(r("yb", 32, 64), r("zz", 15, 512, 16))
-        copy("s", r("wb", 0, 8), named())
-        copy("s", r("wb", 32, 40, p1=64), named(p0=64))
-        copy("s", r("wb", 32, 40, p0=64), named(p1=64))
-        turn(r("wb", 96, 128, p1=64), r("yb", 16, 48, p0=64))
-        turn(r("wb", 96, 128, p0=64), r("yb", 16, 48, p1=64))
-        turn(r("wb", 64, 96), r("yb", 16, 48))
+        wide = lambda p0=0, p1=128: r("zz", 15, 512, 16, p0, p1)
+        turn(r("yb", 0, 32), wide())
+        turn(r("yb", 64, 96), wide())
         for q in range(4):
-            o = q ^ 1
-            copy("svvv"[q], r("wb", 128, 232, p0=32 * q, p1=32 * q + 32), r("wb", 0, 104, p0=32 * o, p1=32 * o + 32))
+            turn(r("yb", 32, 64, p0=32 * q, p1=32 * q + 32), wide(32 * (q ^ 1), 32 * (q ^ 1) + 32))
+        copy("s", r("wb", 0, 8), named())
+        copy("s", r("wb", 16, 24, p1=64), named(p0=64))
+        copy("s", r("wb", 16, 24, p0=64), named(p1=64))
+        for x in (1, 3):
+            for q in range(4):
+                copy("sv", r("wb", 8 * x, 8 * x + 8, p0=32 * q, p1=32 * q + 32), named(32 * (q ^ x), 32 * (q ^ x) + 32))
+        turn(r("wb", 96, 160, p1=64), r("yb", 16, 80, p0=64))
+        turn(r("wb", 96, 160, p0=64), r("yb", 16, 80, p1=64))
+        turn(r("wb", 32, 96), r("yb", 16, 80))
         ts(r(of), r("wb"), 512.0, 192.0, A.mult, A.add, off=cell("cu", 0))
 
+        bonus[0] = ZH
         for b in range(4):
-            copy("vs", r("zt", b, 512, 4), r("vp", 384 * b, 384 * b + 384), off=r(of, 0, 8))
+            copy(ZT[b], r("zt", b, 512, 4), r("vp", 384 * b, 384 * b + 384), off=r(of, 0, 8))
         quant("zq", "zsc", 0, 128, r("zt"))
         for b in range(4):
             mm(od[b], "wq", "wsc", 128 * b, "zq", "zsc", 0, 128)
@@ -522,9 +553,10 @@ def rank_program(g, core, T, topo):
                 scan(r("u1", a, a + step), r("dec", 0, step), r("d1", a, a + step), 0.0, A.add, A.min)
             return r("u1", 1024 * kind + 127, 1024 * kind + 1024, 128)
 
+        bonus[0] = LB
         copy("s", r("lb"), r("tab"), off=r(of, 0, 8))
         send(rank + 1 + t, [(r(ol), r(of, 0, 8))], "al%d" % t)
-        bonus[0] = ODD
+        bonus[0] = ODD1
         ts(r("f1"), first(0, r("lb")), 127.0, 128.0, A.add, A.min)
         bonus[0] = 0.0
         lin(r("fe"), first(1, r("lb")), 1.0, float(-GV), "sv")
@@ -548,14 +580,14 @@ def rank_program(g, core, T, topo):
             if not last:
                 (odd_part if a else even_part)(t + 1)
 
-    quant("lq", "ls", 0, 256, r("xl"))
-    mm(2, "vq", "vs", 0, "lq", "ls", 0, 128)
-    mm(3, "vq", "vs", 0, "lq", "ls", 128, 256)
+    for a in (0, 128):
+        quant("lq", "ls", a, a + 128, r("xl", 4 * a, 4 * a + 512))
+        mm(2 + a // 128, "vq", "vs", 0, "lq", "ls", a, a + 128)
     dma("y", T.oc[:], T.lq[:].bitcast(dt.uint8), [r("lq")], [], "outs")
     for k in range(4):
-        dma("sy"[k // 2], T.osc[4 * k:4 * k + 4, :], T.ls[32 * k:32 * k + 4, :], [r("ls")], [], "outs")
-    copy("v", r("yt", 0, 128), bk(2))
-    copy("s", r("yt", 128, 256), bk(3))
+        dma("y", T.osc[4 * k:4 * k + 4, :], T.ls[32 * k:32 * k + 4, :], [r("ls")], [], "outs")
+    copy("s", r("yt", 0, 128), bk(2))
+    copy("v", r("yt", 128, 256), bk(3))
     dma("s", T.y[:], T.yt[:], [r("yt")], [], "outs")
 
     if not PLAN:

from concourse.mybir import dt, AluOpType, ActivationFunctionType

C, K, R = 256, 128, 3
BIG = 1.0e29
RS = 385
SW = 137
GV, EW = 144, 288
STEP = 2.0 ** -13
CODES, U8 = "float8_e4m3fn_x4", "uint8"
F32, BF16, I32, U16 = "float32", "bfloat16", "int32", "uint16"
CYCLE, WAKE, LOAD, FLIGHT, HOP = 0.83e-3, 0.175, 1.7, 2.0, 1.2
FIX, FIRST, ODD, AHEAD = 0.05, 0.8, 0.0, 2.0
LATE, LEAD, XE, XO, APART = 6, 0.0, "vvvs", "svvs", True
LB, ODD1, ZH, ZT = 0.0, 0.0, 0.0, ["vs"] * 4
RULES = [(0, 1.0, 0.1, 0.1)]
URGE = {'wv': 2.0, 'nb6': 1.0, 'eqb': 1.0, 'nb7': -0.5, 'cb7': -0.5, 'cb3': 0.2, 'pu0': -0.5, 'jb0': -2.0, 'u12': -0.5, 'wi4': -0.5, 'f2': -0.2, 'sh2': 0.2, 'pf': -2.0, 'pt2': 1.0, 'et0': -2.0, 'd11': -1.0, 'sh1': 0.2, 'cb1': 0.5, 'cb2': 2.0}
WAIT = {'ht': 0.0, 'd12': 0.25, 'pr0': 0.25}
SIDE = {'zt': 0.0, 'd10': 0.0, 'ep0': 1.0, 'd11': 0.0, 'd12': 0.25, 'ep1': 1.0, 'ht': 0.05}
MARK, SUMS, PICK, HT, EP = 0.0, 0.0, 0.0, ["vs"] * 4, ["vs"] * 4
BY_SIGN = (0, 1, 2)
CUT, HALVES, QUICK = (2, 2, 2), 1, 0
ROWS = [["vs"] * 8, ["vs"] * 8, ["vs"] * 8]
TIES = ((1, 7), (7, 8))
JOINT = (3, 4, 5)

SCRATCH = {}
PLAN = []


def _sb(name, cols, dtype):
    SCRATCH[name] = ("sbuf", [128, cols], dtype)


for _n, _c, _d in [
    ("xn", 1024, BF16), ("xe", 512, BF16), ("xo", 512, BF16), ("xl", 1024, BF16), ("vt", 512, BF16),
    ("vq", 128, CODES), ("vs", 128, U8), ("wq", 512, CODES), ("wsc", 512, U8),
    ("lq", 256, CODES), ("ls", 256, U8), ("yt", 256, F32), ("opt", 32, F32),
    ("eb", 516, BF16), ("eq", 512, CODES), ("es", 512, U8),
    ("ij", 128, F32), ("ii", 8, F32), ("pw", 16, F32), ("pi", 8, I32), ("bi", 8, I32), ("bf", 8, F32),
    ("xr", 4, F32), ("tm", 8, F32), ("qc", 8, F32), ("tb", 96, F32), ("tc", 96, F32),
    ("mdiag", 128, F32), ("neg1", 256, BF16), ("one", SW - 1, BF16), ("rs2", SW * max(len(JOINT), 1), BF16), ("cfl", 18, F32), ("cu", 18, U16),
    ("tab", 384, BF16), ("dm", 128, F32), ("rst", 128, BF16), ("stp", 8, BF16),
    ("dec", 1024 // min(CUT), BF16), ("col", 24, BF16), ("ncol", 24, F32),
    ("so", 256, F32), ("pt", 8 * RS, F32), ("xg", 256, BF16), ("xh", 256, BF16), ("ma", 256, BF16), ("mb", 256, BF16),
    ("ya", 8, F32), ("ta", 8, F32), ("junk", 1024, F32), ("sums", 4, F32), ("wi", 8, I32), ("pu", 8, U16),
    ("gv", 128, F32), ("vv", 128, F32), ("pf", 16, BF16), ("pr", 128, BF16), ("vr", 64, F32),
    ("sg", 256, BF16), ("sc", SW - 1, F32), ("sh", 8 * SW, BF16), ("nb", 8 * SW, BF16), ("cb", 8 * SW, BF16), ("jb", 1024, BF16),
    ("eqb", 8, F32), ("zc", 8, F32), ("wv", 8, BF16), ("ab", 8, F32), ("et", 128, BF16), ("yy", 128, BF16), ("zz", 512, BF16),
    ("wb", 160, BF16), ("yb", 96, BF16), ("vp", 1536, BF16), ("zt", 512, BF16), ("zq", 128, CODES), ("zsc", 128, U8),
    ("ht", 512, BF16), ("lb", 128, BF16), ("lg", 128, BF16), ("d1", 3072, BF16), ("u1", 3072, BF16),
    ("fe", 8, F32), ("fm", 8, F32), ("f1", 8, U16), ("f2", 8, U16), ("ep", 4 * EW, BF16),
]:
    _sb(_n, _c, _d)
for _t in range(R):
    _sb("tq%d" % _t, 384, CODES)
    _sb("ts%d" % _t, 384, U8)
    _sb("hq%d" % _t, 256, CODES)
    _sb("hs%d" % _t, 256, U8)
    _sb("of%d" % _t, 16, U16)
    _sb("ol%d" % _t, 8, U16)
for _b in range(8):
    SCRATCH["bk%d" % _b] = ("psum", [128, 512], F32)

SEMAPHORES = ["cv", "cs", "ct", "cg", "lx", "lv", "lwc", "lws", "sent", "outs"] + \
    ["%s%d" % (_k, _t) for _k in ("at", "al", "ah") for _t in range(R)]

A = AluOpType
AF = ActivationFunctionType
WIDTH = {F32: 4, I32: 4, CODES: 4, BF16: 2, U16: 2, U8: 1}


def r(name, c0=0, c1=None, st=1, p0=0, p1=128):
    if c1 is None:
        c1 = SCRATCH[name][1][1]
    return (name, p0, p1, c0, c1, st)


def cols(x):
    return len(range(x[3], x[4], x[5]))


def is_bank(x):
    return SCRATCH[x[0]][0] == "psum"


def meet(a, b):
    if a[0] != b[0] or a[2] <= b[1] or b[2] <= a[1] or a[4] <= b[3] or b[4] <= a[3]:
        return False
    if a[5] == 1 and b[5] == 1:
        return True
    return not set(range(a[3], a[4], a[5])).isdisjoint(range(b[3], b[4], b[5]))


def kind(call):
    name, p0, p1, c0, c1, st = (call[2] or call[1])[0]
    part = {"d1": c0 // 1024, "u1": c0 // 1024, "ep": c0 % EW // GV, "pt": c0 % RS // 128, "so": c0, "wb": c0 // 64,
            "vp": (c0 % 384 + 127) // 128, "tq": c0 // 128, "hq": c0 // 128, "pr": c0, "et": c0, "sc": c0,
            "nb": c0 // SW, "cb": c0 // SW, "sh": c0 // SW, "jb": c0 // 128, "wi": c0, "pu": c0}.get(name[:2])
    return name if part is None else "%s%d" % (name[:2], part)


def arrange(calls):
    before, after, seen = [], [[] for c in calls], {}
    for i, (forms, reads, writes, delay, extra) in enumerate(calls):
        deps = {}
        for regs, wr in ((reads, False), (writes, True)):
            for x in regs:
                for (y, w, j) in seen.get(x[0], ()):
                    if is_bank(x):
                        alone = len(forms) == 1 and list(forms) == list(calls[j][0])
                        if w or wr or not alone:
                            deps[j] = max(deps.get(j, 0.0), 0.0 if alone else WAKE)
                    elif (w or wr) and meet(x, y):
                        deps[j] = (calls[j][3] if w else 0.0) + WAKE
        before.append(deps)
        for j in deps:
            after[j].append(i)
        for regs, wr in ((reads, False), (writes, True)):
            for x in regs:
                seen.setdefault(x[0], []).append((x, wr, i))
    way = [0.0] * len(calls)
    for i in range(len(calls) - 1, -1, -1):
        forms, reads, writes, delay, extra = calls[i]
        way[i] = min(c for c, f in forms.values()) + max([way[j] + before[j][i] for j in after[i]] + [delay])

    def place(own, weight, slack, spare):
        urgent = [own * min(x for x, f in c[0].values()) - w - weight * c[4] - URGE.get(kind(c), 0.0) for w, c in zip(way, calls)]
        spared = [SIDE.get(kind(c), spare) for c in calls]
        got, free = {}, {q: 0.0 for q in "vstgy"}
        left = [len(deps) for deps in before]
        ready = {i: 0.0 for i in range(len(calls)) if not left[i]}
        while ready:
            q = min(free, key=free.get)
            now = free[q]

            def fits(i):
                ends = {o: max(free[o], ready[i]) + c + spared[i] * (o == "v") for o, (c, f) in calls[i][0].items()}
                return q in ends and ends[q] <= min(ends.values())
            mine = sorted((i for i in ready if fits(i)), key=lambda i: (urgent[i], i))
            until, chosen = float("inf"), None
            for i in mine:
                if ready[i] <= now and now + calls[i][0][q][0] <= until:
                    chosen = i
                    break
                until = min(until, ready[i] + WAIT.get(kind(calls[i]), slack))
            if chosen is None:
                free[q] = min([ready[i] for i in mine if ready[i] > now] + [t for t in free.values() if t > now] + [now + 0.05])
                continue
            free[q] = now + calls[chosen][0][q][0]
            got[chosen] = (now, free[q], q)
            del ready[chosen]
            for j in after[chosen]:
                left[j] -= 1
                if not left[j]:
                    ready[j] = max(got[k][1] + gap for k, gap in before[j].items())
        return max(got[i][1] + calls[i][3] for i in got), got

    end, got = min((place(*rule) for rule in RULES), key=lambda x: x[0])
    return [(i, got[i][2]) for i in sorted(got, key=lambda i: (got[i][0], i))]


def rank_program(g, core, T, topo):
    rank = T.rank_of(core)
    if rank is None:
        return
    n = len(T.cores)
    queues = {"v": g.vector, "s": g.scalar, "t": g.tensor, "g": g, "y": g.sync}
    counter = {"v": "cv", "s": "cs", "t": "ct", "g": "cg"}
    total = {}
    known = {q: {} for q in queues}
    touched = {}
    calls = []
    bonus = [0.0]

    def ap(x):
        if x[5] == 1:
            return T[x[0]][x[1]:x[2], x[3]:x[4]]
        return T[x[0]][x[1]:x[2], x[3]:x[4]:x[5]]

    def val(x):
        return ap(x) if isinstance(x, tuple) else x

    def order(q, reads, writes):
        need = {}
        for regs, wr in ((reads, False), (writes, True)):
            for x in regs:
                for (y, w, oq, sem, cnt, clock) in touched.get(x[0], ()):
                    hit = oq != q if is_bank(x) else (w or wr) and meet(x, y)
                    if hit and need.get(sem, (0, None))[0] < cnt:
                        need[sem] = (cnt, clock)
        kn = known[q]
        for sem, (cnt, clock) in need.items():
            covered = any(o != sem and c2.get(sem, 0) >= cnt for o, (k2, c2) in need.items())
            if kn.get(sem, 0) < cnt and not covered:
                queues[q].wait_ge(T.sem[sem], cnt)
        for sem, (cnt, clock) in need.items():
            kn[sem] = max(kn.get(sem, 0), cnt)
            for s2, c2 in clock.items():
                kn[s2] = max(kn.get(s2, 0), c2)

    def note(q, reads, writes, sem, cnt):
        clock = dict(known[q]) if q in known else {}
        for regs, wr in ((reads, False), (writes, True)):
            for x in regs:
                touched.setdefault(x[0], []).append((x, wr, q, sem, cnt, clock))

    def add(forms, reads, writes):
        reads = [x for x in reads if isinstance(x, tuple)]

        def issue(q, call):
            def go():
                order(q, reads, writes)
                sem = counter[q]
                total[sem] = total.get(sem, 0) + 1
                call(queues[q]).then_inc(T.sem[sem], 1)
                note(q, reads, writes, sem, total[sem])
            return go
        calls.append(({q: (c, issue(q, f)) for q, (c, f) in forms.items()}, reads, writes, 0.0, bonus[0]))

    def dma(q, out, in_, reads, writes, sem, delay=LOAD):
        def go():
            order(q, reads, writes)
            total[sem] = total.get(sem, 0) + 16
            queues[q].dma_start(out, in_).then_inc(T.sem[sem], 16)
            note("dma", reads, writes, sem, total[sem])
        calls.append(({q: (0.06, go)}, reads, writes, delay, 0.0))

    def src(x, off):
        return ap(x) if off is None else ap(x).indirect(ap(off))

    def vcost(out, ins, off=None, rate=None):
        if off is not None:
            return FIX + 1.5 * 16 * cols(off) * CYCLE
        sides = [x for x in [out] + ins if isinstance(x, tuple)]
        if rate is None:
            rate = 0.5 if all(WIDTH[SCRATCH[x[0]][2]] == 2 for x in sides) else 1.0
        return FIX + rate * cols(out) * CYCLE

    def scost(out, off=None):
        return FIX + (1.0 if off is None else 1.5) * cols(out) * CYCLE

    def ts_form(out, in_, s1, s2, op0, op1=None, off=None):
        if op1 is None:
            return vcost(out, [in_], off), lambda e: e.tensor_scalar(ap(out), src(in_, off), val(s1), None, op0)
        return vcost(out, [in_], off), lambda e: e.tensor_scalar(ap(out), src(in_, off), val(s1), val(s2), op0, op1)

    def act_form(out, in_, func, bias, scale, acc=None, off=None):
        if func is AF.Copy:
            call = lambda e: e.activation(ap(out), src(in_, off), func) if scale == 1.0 else \
                e.activation(ap(out), src(in_, off), func, scale=scale)
        elif acc is None:
            call = lambda e: e.activation(ap(out), src(in_, off), func, bias=val(bias), scale=scale)
        else:
            call = lambda e: e.activation(ap(out), ap(in_), func, bias=val(bias), scale=scale, accum_out=ap(acc))
        return scost(out, off) + (0.02 if acc else 0.0), call

    def copy(qs, out, in_, off=None, scale=1.0, also=()):
        forms = {}
        if "v" in qs and scale == 1.0:
            forms["v"] = (vcost(out, [in_], off), lambda e: e.tensor_copy(ap(out), src(in_, off)))
        elif "v" in qs:
            forms["v"] = ts_form(out, in_, scale, None, A.mult, off=off)
        if "s" in qs:
            forms["s"] = act_form(out, in_, AF.Copy, 0.0, scale, off=off)
        add(forms, [in_, off] + list(also), [out])

    def ts(out, in_, s1, s2, op0, op1=None, off=None):
        add({"v": ts_form(out, in_, s1, s2, op0, op1, off)}, [in_, off, s1, s2], [out])

    def tt(out, a, b, op, off=None):
        cost = vcost(out, [a, b], off, 1.0 if is_bank(a) or is_bank(b) else 2.0)
        add({"v": (cost, lambda e: e.tensor_tensor(ap(out), src(a, off), ap(b), op))}, [a, b, off], [out])

    def scan(out, d0, d1, init, op0, op1):
        add({"v": (vcost(out, [d0, d1]), lambda e: e.tensor_tensor_scan(ap(out), ap(d0), ap(d1), val(init), op0, op1))},
            [d0, d1, init], [out])

    def turn(out, in_):
        add({"v": (vcost(out, [in_]), lambda e: e.transpose(ap(out), ap(in_)))}, [in_], [out])

    def act(out, in_, func, bias, scale, acc=None, off=None):
        add({"s": act_form(out, in_, func, bias, scale, acc, off)}, [in_, bias, off], [out] + ([acc] if acc else []))

    def lin(out, in_, scale, bias, qs="s"):
        forms = {"s": act_form(out, in_, AF.Identity, bias, scale), "v": ts_form(out, in_, scale, bias, A.mult, A.add)}
        add({q: forms[q] for q in qs}, [in_, bias], [out])

    def fill(out, c):
        forms = {"v": (vcost(out, []), lambda e: e.memset(ap(out), c))}
        if cols(out) <= 128:
            forms["s"] = act_form(out, r("ij", 0, cols(out)), AF.Identity, c, 0.0)
        add(forms, [r("ij")] if "s" in forms else [], [out])

    def iota(out, pattern, base, mult):
        if SCRATCH[out[0]][2] == I32:
            call = lambda e: e.iota(ap(out), pattern, base, mult)
        else:
            call = lambda e: e.iota(ap(out), pattern, base, mult, allow_small_or_imprecise_dtypes=True)
        add({"g": (0.13 + 2 * cols(out) * CYCLE, call)}, [], [out])

    def quant(cq, cs, a, b, tile):
        add({"v": (0.012 + 0.00022 * cols(tile), lambda e: e.quantize_mx(ap(r(cq, a, b)), ap(r(cs, a, b)), ap(tile)))},
            [tile], [r(cq, a, b), r(cs, a, b)])

    def mm(bank, lq, ls, la, rq, rs_, ra, rb):
        out = r("bk%d" % bank, 0, rb - ra)
        ins = [r(lq, la, la + 128), r(ls, la, la + 128), r(rq, ra, rb), r(rs_, ra, rb)]
        add({"t": ((rb - ra + 16) * CYCLE,
                   lambda e: e.matmul_mx(ap(out), ap(ins[0]), ap(ins[1]), ap(ins[2]), ap(ins[3]), True, True))}, ins, [out])

    shared = [e for e in range(16) if all(e in topo.engines(core, c) for c in T.cores if c != core)]

    def send(dst_rank, pairs, sem, apart=False):
        rid, pid, _ = topo.addr(T.cores[dst_rank % n])

        def go():
            total[sem] = 0
            for i, (out, in_) in enumerate(pairs):
                lanes = shared[i::len(pairs)] if apart and APART else shared
                order("g", [in_], [])
                a, b = ap(out), ap(in_)
                if SCRATCH[in_[0]][2] == CODES:
                    a, b = a.bitcast(dt.uint8), b.bitcast(dt.uint8)
                total["sent"] = total.get("sent", 0) + len(lanes)
                total[sem] += len(lanes)
                g.remote_dma(a, b, T.sem[sem], T.sem["sent"], pid, rid, sum(1 << e for e in lanes))
            note("far", [], [out for out, in_ in pairs], sem, total[sem])
        calls.append(({"g": (0.2 * len(pairs), go)}, [i for o, i in pairs], [o for o, i in pairs],
                      {"at": AHEAD, "ah": FLIGHT, "al": HOP}[sem[:2]] + FIRST * apart, 0.0))

    def bk(b, a=0, z=128):
        return r("bk%d" % b, a, z)

    def prow(k, a, z):
        return r("pt", k * RS + a, k * RS + z)

    def best(at, a=0, z=8):
        return r("pt", a * RS + at, z * RS, RS)

    def cell(name, j):
        return r(name, j, j + 1)

    dma("y", T.xn[:], T.x[:], [], [r("xn")], "lx")

    iota(r("ij"), [[1, 128]], 0, -1)
    fill(r("pw", 0, 8), 0.5)
    scan(r("pw", 8, 15), r("pw", 0, 7), r("pw", 0, 7), -128.0, A.mult, A.min)
    ts(r("pi", 0, 7), r("pw", 8, 15), cell("ij", 0), None, A.mult)
    fill(r("eb"), 0.0)
    ts(r("mdiag"), r("ij"), 0.0, -BIG, A.is_equal, A.mult)
    ts(r("eb", 4, 516, 4), r("ij"), 0.0, None, A.is_equal)
    for b in range(4):
        quant("eq", "es", 128 * b, 128 * b + 128, r("eb", 4 - b, 516 - b))
    for name, a, z, st, c in [
            ("ep", K, 4 * EW, GV, 0.0), ("neg1", 0, 256, 1, -1.0), ("one", 0, None, 1, 1.0),
            ("rs2", 0, None, 1, 1.0), ("rs2", 0, None, SW, 0.0),
            ("pt", 0, 8 * RS, RS, -BIG), ("ya", 0, 1, 1, -1.0), ("cfl", 1, 2, 1, 0.0),
            ("rst", 0, 128, 1, 1.0), ("rst", 0, 128, 16, 0.0), ("stp", 0, 7, 1, STEP), ("stp", 7, 8, 1, -STEP),
            ("et", 0, 128, 1, 0.0), ("pf", 8, 16, 1, 0.0), ("wv", 0, 1, 1, 0.0),
            ("zz", 128, 512, 1, 0.0)]:
        fill(r(name, a, z, st), c)
    ts(r("bi", 0, 7), r("pi", 0, 7), 6, 1, A.logical_shift_right, A.bitwise_and)
    ts(cell("bi", 7), cell("pi", 6), 15, None, A.bitwise_and)
    copy("v", r("bf"), r("bi"))
    iota(r("ii"), [[1, 8]], 0, 0)
    iota(r("tab", 0, 192), [[2, 192]], -384, 0)
    iota(r("tab", 192, 384), [[2, 192]], 0, 0)
    iota(r("dm"), [[0, 8], [1, 16]], 0, 0)
    ts(r("dm"), r("dm"), cell("bf", 7), None, A.is_equal)
    iota(r("qc"), [[16, 8]], 0, 0)
    ts(r("qc"), r("qc"), cell("bf", 7), None, A.add)
    for kind, (step, base) in enumerate(((4.0, -382.0), (4.0, -384.0), (2.0, 128.0))):
        lin(r("col", 8 * kind, 8 * kind + 8), r("qc"), step, base)
    lin(r("ncol"), r("col"), -256.0, 0.0)
    iota(r("dec"), [[0, cols(r("dec"))]], -1, 0)
    fill(r("dec", 0, None, 128), 1024.0)

    for k in range(3):
        act(cell("xr", k), cell("bf", k), AF.Abs, cell("bf", k + 4), -1.0)
    lin(cell("tm", 0), cell("bf", 5), 2.0, cell("bf", 4))
    lin(cell("tm", 1), cell("bf", 6), 4.0, cell("tm", 0))
    act(cell("xr", 3), cell("xr", 1), AF.Abs, cell("bf", 4), -1.0)
    lin(cell("tm", 2), cell("xr", 2), 2.0, cell("xr", 1))
    lin(cell("tm", 3), cell("xr", 2), 2.0, cell("xr", 3))
    lin(cell("tm", 4), cell("tm", 3), 32.0, 32.0)
    lin(cell("tm", 5), cell("tm", 2), -8.0, cell("tm", 4))
    lin(cell("tm", 6), cell("tm", 2), 8.0, cell("tm", 1))
    ts(cell("cfl", 0), cell("tm", 5), cell("xr", 0), cell("tm", 6), A.mult, A.add)
    iota(r("tb", 0, 32), [[0, 2], [RS, 2], [0, 8]], 384, 0)
    iota(r("tb", 32, 64), [[0, 4], [16, 8]], 15, 0)
    for o in range(2):
        iota(r("tb", 64 + o, 96, 2), [[0, 2], [1, 8]], o, 0)
    turn(r("tc"), r("tb"))
    lin(r("cfl", 2, 6), r("ii", 0, 4), 2.0 * RS, cell("tc", 0))
    lin(r("cfl", 6, 10), r("ii", 0, 4), 0.0, cell("tc", 32))
    lin(r("cfl", 10, 18), r("ii", 0, 8), 0.0, cell("tc", 64))
    copy("v", r("cu"), r("cfl"))

    ev, od = (0, 1, 6, 7), (2, 3, 4, 5)
    odd = r("so", 1, 256, 2)

    def planes(t, a, out, also=()):
        for b in range(4):
            mm(od[b], "eq", "es", 128 * b, "tq%d" % t, "ts%d" % t, a, a + 128)
            copy("s", r("vp", 384 * b + out[0], 384 * b + out[1], out[2]), bk(od[b]), also=also)

    def levels(at, data, low, parts=1):
        wide = 128 // parts
        for k, a in sorted(((k, a) for k in range(8) for a in range(0, 128, wide)), key=lambda s: (s[0] + s[1] // wide, s[1])):
            cut = lambda x: r(x[0], x[3] + a * x[5], x[3] + (a + wide - 1) * x[5] + 1, x[5])
            scan(prow(k, at + a + 1, at + a + wide + 1), cut(data), prow(k - 1, at + a, at + a + wide) if k else cut(low),
                 prow(k, at + a, at + a + 1), A.max, A.min if k else A.max)

    def odd_part(t):
        tq, tsc = "tq%d" % t, "ts%d" % t
        quant(tq, tsc, 0, 128, r("xo"))
        mm(od[3], tq, tsc, 0, tq, tsc, 0, 128)
        tt(odd, bk(od[3]), r("mdiag"), A.add)
        bonus[0] = 0.0
        levels(0, odd, odd)
        planes(t, 0, (1, 256, 2))

    def even_part(t):
        tq, tsc = "tq%d" % t, "ts%d" % t
        quant(tq, tsc, 128, 256, r("xe"))
        send(rank - 1 - t, [(r(tq, 256, 384), r(tq, 128, 256)), (r(tsc, 256, 384), r(tsc, 128, 256))], "at%d" % t, t == 0)

    bonus[0] = 5.0
    for j in range(4):
        copy(XE[j], r("xe", j, 512, 4), r("xn", j, 1024, 8))
    even_part(0)
    bonus[0] = 4.0
    for j in range(4):
        copy(XO[j], r("xo", j, 512, 4), r("xn", 4 + j, 1024, 8))
    odd_part(0)

    for t in range(R):
        tq, tsc, hq, hs = "tq%d" % t, "ts%d" % t, "hq%d" % t, "hs%d" % t
        of, ol = "of%d" % t, "ol%d" % t
        last = t == R - 1

        mm(ev[0], tq, tsc, 0, tq, tsc, 128, 256)
        mm(ev[1], tq, tsc, 0, tq, tsc, 128, 256)
        copy("s", r("so", 0, 256, 2), bk(ev[1]))
        levels(128, bk(ev[0]), odd, HALVES)
        edge = prow(7, 256, 257)
        bonus[0] = MARK
        act(r("ya", 1, 8), best(256, 0, 7), AF.Sign, edge, -1.0)
        ts(r("xg"), r("so"), edge, STEP, A.is_le, A.max)
        act(r("sg"), r("so"), AF.Sign, edge, -1.0)
        scan(r("ta"), r("ya"), r("stp"), 0.0, A.min, A.mult)
        scan(r("ma"), r("xg"), r("neg1"), cell("ta", 7), A.mult, A.max)
        ts(r("xh"), r("sg"), STEP, None, A.max)
        scan(r("mb"), r("xh"), r("ma"), 1.0, A.mult, A.max)
        bonus[0] = SUMS
        for j in range(4):
            act(r("junk", 256 * j, 256 * j + 256), r("mb"), AF.Relu, 4097.0, -STEP ** -(2 * j + 1), cell("sums", j))
        bonus[0] = PICK
        m = 4 - QUICK
        ts(r("wi", 0, m), r("sums", 0, m), -1.0, 4097.0 * 256, A.mult, A.add)
        ts(r("pu", 0, 2 * m, 2), r("sums", 0, m), -1.0 / 4096, 4097.0 / 16, A.mult, A.add)
        ts(r("wi", 4, 4 + m), r("wi", 0, m), 4095, None, A.bitwise_and)
        copy("v", r("pu", 1, 2 * m, 2), r("wi", 4, 4 + m))
        if QUICK:
            ts(cell("pu", 6), cell("sums", 3), -1.0 / 4096, 4097.0 / 16, A.mult, A.add)
            lin(cell("zc", 0), cell("sums", 3), -1.0, 4097.0 * 256)
            ts(cell("pu", 7), cell("pu", 6), -4096.0, cell("zc", 0), A.mult, A.add)
        tt(r("gv"), r("so"), r("dm"), A.mult, off=r("pu"))
        scan(r("vv"), r("rst"), r("gv"), 0.0, A.mult, A.add)
        ts(r("pf", 0, 8), r("pu"), 1.0 / 512, -0.375, A.mult, A.add)
        copy("s", r("pr"), r("pf"), off=r("cu", 10, 18))
        bonus[0] = 0.0
        planes(t, 128, (0, 256, 2))

        if t == 0:
            dma("y", T.wq[:].bitcast(dt.uint8), T.wc[:], [r(tq, 256, 384)], [r("wq")], "lwc")
            dma("y", T.wsc[:], T.ws[:], [r(tq, 256, 384)], [r("wsc")], "lws")
            dma("y", T.vt[:], T.v[:], [r("wq")], [r("vt")], "lv", 4 * LOAD)
        mm(ev[2], tq, tsc, 0, tq, tsc, 256, 384)
        mm(ev[3], tq, tsc, 0, tq, tsc, 256, 384)
        copy("s", r("sc", 0, 8), best(256))
        copy("s", r("sc", 8, 136), bk(ev[3]))
        levels(256, bk(ev[2]), r("so", 0, 128))
        for a, z in TIES:
            if z - a > 1:
                tt(r("eqb", a, z), best(384, a, z), best(384, a - 1, z - 1), A.is_equal)
                scan(r("wv", a, z), r("neg1", a, z), r("eqb", a, z), cell("wv", a - 1), A.add, A.mult)
            else:
                lin(cell("zc", a), cell("wv", a - 1), 1.0, -1.0, "sv")
                ts(cell("wv", a), best(384, a, z), best(384, a - 1, a), cell("zc", a), A.is_equal, A.mult)
        bonus[0] = 2.0
        lin(r("et", 0, 128, 16), r("wv"), 1.0, -0.5)
        for k in range(8):
            bonus[0] = LEAD * (7 - k)
            top = prow(k, 384, 385)
            row = lambda name, a=1, k=k: r(name, SW * k + a, SW * k + SW)
            if k in BY_SIGN:
                act(row("sh"), r("sc"), AF.Sign, top, -1.0)
                act(row("nb"), row("sh"), AF.Abs, 0.0, 1.0)
            else:
                ts(row("nb"), r("sc"), top, None, A.is_equal if k in JOINT else A.not_equal)
            if k not in JOINT:
                scan(row("cb"), r("one"), row("nb"), cell("wv", k), A.add, A.subtract)
            elif k == JOINT[-1]:
                a, z = SW * JOINT[0], SW * k + SW
                copy("s", r("nb", a, z, SW), r("wv", JOINT[0], k + 1))
                scan(r("cb", a, z), r("rs2"), r("nb", a, z), 0.0, A.mult, A.add)
            for j in ([k] if k not in JOINT else JOINT if k == JOINT[-1] else []):
                act(r("jb", 128 * j, 128 * j + 128), row("cb", 9, j), AF.Sign, 0.5, -1.0, cell("ab", j))
        bonus[0] = 0.0
        lin(r("pr", 15, 128, 16), r("ab"), 1.0 / 1024, 0.25)
        copy("s", r("vr"), r("pt"), off=r("cu", 2, 6))
        tt(r("et", 1, 128, 2), r("vv"), r("vr"), A.is_equal, off=r("cu", 6, 10))
        scan(r("yy"), r("rst"), r("et"), 0.0, A.mult, A.subtract)
        scan(r("zz", 0, 128), r("yy"), r("pr"), 0.0, A.max, A.min)
        named = lambda p0=0, p1=128: r("zz", 15, 128, 16, p0, p1)
        planes(t, 256, (256, 384, 1), [cell("ab", LATE)] if LATE < 8 else [])

        wide = lambda p0=0, p1=128: r("zz", 15, 512, 16, p0, p1)
        turn(r("yb", 0, 32), wide())
        turn(r("yb", 64, 96), wide())
        for q in range(4):
            turn(r("yb", 32, 64, p0=32 * q, p1=32 * q + 32), wide(32 * (q ^ 1), 32 * (q ^ 1) + 32))
        copy("s", r("wb", 0, 8), named())
        copy("s", r("wb", 16, 24, p1=64), named(p0=64))
        copy("s", r("wb", 16, 24, p0=64), named(p1=64))
        for x in (1, 3):
            for q in range(4):
                copy("sv", r("wb", 8 * x, 8 * x + 8, p0=32 * q, p1=32 * q + 32), named(32 * (q ^ x), 32 * (q ^ x) + 32))
        turn(r("wb", 96, 160, p1=64), r("yb", 16, 80, p0=64))
        turn(r("wb", 96, 160, p0=64), r("yb", 16, 80, p1=64))
        turn(r("wb", 32, 96), r("yb", 16, 80))
        ts(r(of), r("wb"), 512.0, 192.0, A.mult, A.add, off=cell("cu", 0))

        bonus[0] = ZH
        for b in range(4):
            copy(ZT[b], r("zt", b, 512, 4), r("vp", 384 * b, 384 * b + 384), off=r(of, 0, 8))
        quant("zq", "zsc", 0, 128, r("zt"))
        for b in range(4):
            mm(od[b], "wq", "wsc", 128 * b, "zq", "zsc", 0, 128)
            copy(HT[b], r("ht", b, 512, 4), bk(od[b]), scale=0.03125)
        quant(hq, hs, 0, 128, r("ht"))
        send(rank + 1 + t, [(r(hq, 128, 256), r(hq, 0, 128)), (r(hs, 128, 256), r(hs, 0, 128))], "ah%d" % t)

        def first(kind, lst):
            for c in range(8):
                row, j = r("d1", 1024 * kind + 128 * c, 1024 * kind + 128 * c + 128), 8 * kind + c
                forms = {"s": act_form(row, lst, AF.Abs, cell("ncol", j), 256.0),
                         "v": ts_form(row, lst, cell("col", j), 512.0, A.not_equal, A.mult)}
                add({q: forms[q] for q in ROWS[kind][c]}, [lst, cell("col", j), cell("ncol", j)], [row])
            step = 1024 // CUT[kind]
            for a in range(1024 * kind, 1024 * kind + 1024, step):
                scan(r("u1", a, a + step), r("dec", 0, step), r("d1", a, a + step), 0.0, A.add, A.min)
            return r("u1", 1024 * kind + 127, 1024 * kind + 1024, 128)

        bonus[0] = LB
        copy("s", r("lb"), r("tab"), off=r(of, 0, 8))
        send(rank + 1 + t, [(r(ol), r(of, 0, 8))], "al%d" % t)
        bonus[0] = ODD1
        ts(r("f1"), first(0, r("lb")), 127.0, 128.0, A.add, A.min)
        bonus[0] = 0.0
        lin(r("fe"), first(1, r("lb")), 1.0, float(-GV), "sv")
        copy("s", r("lg"), r("tab"), off=r(ol))
        tt(r("fm"), r("fe"), first(2, r("lg")), A.min)
        ts(r("f2"), r("fm"), GV + 127.0, GV + 128.0, A.add, A.min)
        if last:
            lin(r("opt"), r("yb", 0, 32), 512.0, 192.0)
            for a in range(4):
                dma("y", T.op[:, 32 * a:32 * a + 32], T.opt[32 * a:32 * a + 8, :], [r("opt")], [], "outs")
            quant("vq", "vs", 0, 128, r("vt"))

        for a, banks, lst, tile in ((1, od, "f1", "xo"), (0, ev, "f2", "xe")):
            bonus[0] = ODD * a
            for b in range(4):
                mm(banks[b], "eq", "es", 128 * b, hq, hs, 128 - 128 * a, 256 - 128 * a)
                copy("sv" if a else EP[b], r("ep", EW * b + GV - GV * a, EW * b + GV - GV * a + 128), bk(banks[b]))
            for b in range(4):
                tt(r("xl", 4 * a + b, 1024, 8) if last else r(tile, b, 512, 4), r("ep", EW * b, EW * b + (GV if a else EW)),
                   r("vp", 384 * b + a, 384 * b + 256, 2), A.add, off=r(lst, 0, 8))
            if not last:
                (odd_part if a else even_part)(t + 1)

    for a in (0, 128):
        quant("lq", "ls", a, a + 128, r("xl", 4 * a, 4 * a + 512))
        mm(2 + a // 128, "vq", "vs", 0, "lq", "ls", a, a + 128)
    dma("y", T.oc[:], T.lq[:].bitcast(dt.uint8), [r("lq")], [], "outs")
    for k in range(4):
        dma("y", T.osc[4 * k:4 * k + 4, :], T.ls[32 * k:32 * k + 4, :], [r("ls")], [], "outs")
    copy("s", r("yt", 0, 128), bk(2))
    copy("v", r("yt", 128, 256), bk(3))
    dma("s", T.y[:], T.yt[:], [r("yt")], [], "outs")

    if not PLAN:
        PLAN.extend(arrange(calls))
    for i, q in PLAN:
        calls[i][0][q][1]()
    for sem, cnt in total.items():
        if known["g"].get(sem, 0) < cnt:
            g.wait_ge(T.sem[sem], cnt)
